import numpy as np, ml_dtypes
CORES = [16,18,20,22]
N = 4
BF = ml_dtypes.bfloat16
W, P, L, SH, RO = 4096, 256, 16, 5, 4
def parts(rng):
    return (rng.integers(0, 256, (N, 8, 16, W)), rng.integers(0, W, (N, 8, 16, P)), rng.integers(0, W, (N, 8, 16, P)),
            rng.integers(500, 1300, (N, 8, 16)), rng.integers(30, 100, (N, 8, 16)))
def pack(x, r, m, t, e):
    return {"flood": np.ascontiguousarray(x.reshape(N, 128, W)).astype(np.float32).astype(BF), "riv": np.ascontiguousarray(r.reshape(N, 128, P)).astype(np.int32),
            "bord": np.ascontiguousarray(m.reshape(N, 128, P)).astype(np.int32), "th": t.reshape(N, 128, 1).astype(np.int32), "eps": e.reshape(N, 128, 1).astype(np.int32)}
def setup_inputs(rng):
    return pack(*parts(rng))
def setup_inputs_spread(rng):
    x = np.minimum((np.exp2(3 + 5.5 * rng.random((N, 8, 1, W))) * rng.random((N, 8, 16, W))).astype(np.int64), 255)
    r = (W * rng.random((N, 8, 16, P)) ** 3).astype(np.int64); m = W - 1 - (W * rng.random((N, 8, 16, P)) ** 3).astype(np.int64)
    t = np.minimum(np.exp2(7 + 5 * rng.random((N, 8, 16))).astype(np.int64), 4080); e = np.minimum(np.exp2(8 * rng.random((N, 8, 16))).astype(np.int64) - 1, 255)
    return pack(x, r, m, t, e)
def setup_inputs_ends(rng):
    x = 255 * rng.integers(0, 2, (N, 8, 16, W)); pure = 255 * rng.integers(0, 2, (N, 8, 1, W))
    kind = rng.random((N, 8)) < 0.4; kind[:, 7] = True
    x = np.where(kind[:, :, None, None], pure, x)
    k2 = (((W - 1) * (W - 1) >> SH) + 38 * (W - 1)) & (W - 1)
    x[:, 7, :, 0] = 0
    for c in (W - 1, W - 37, k2): x[:, 7, :, c] = 255
    r = (W - 1) * rng.integers(0, 2, (N, 8, 16, P)); m = (W - 1) * rng.integers(0, 2, (N, 8, 16, P))
    t = 4080 * rng.integers(0, 2, (N, 8, 16)); t[:, :, 2] = 0; t[:, :, 5] = 4080
    e = np.zeros((N, 8, 16), np.int64)
    for q in range(N):
        for g in range(8):
            n = int(rng.choice(np.array([0, 7, 8, 8, 9, 9, 16])))
            if g == 7: n = 8 + q % 2
            e[q, g, rng.permutation(16)[:n]] = 255
    for p in (1, 8, 15):
        r[:, 7, p] = np.where((np.arange(P) // L) % 2 == 0, W - 1, 0); m[:, 7, p] = W - 1; t[:, 7, p] = 4080
    for p in (0, 3, 14):
        r[:, 7, p] = W - 1; r[:, 7, p, P - 1] = 0; m[:, 7, p] = W - 1
    t[:, 7, 0] = 0; t[:, 7, 14] = 0
    r[:, 7, 10] = ((W - 1) * (np.arange(N) % 2))[:, None]; m[:, 7, 10] = W - 1; t[:, 7, 10] = 4080
    return pack(x, r, m, t, e)
def setup_inputs_corners(rng):
    x, r, m, t, e = parts(rng)
    r = np.argsort(rng.random((N, 8, 16, W)), axis=-1)[..., :P]; r = np.ascontiguousarray(r)
    kd = rng.integers(0, 7, (N, 8, 16)); kd[:, 0] = 6; kd[0::2, 3] = 0; kd[1::2, 3] = 6; kd[:, 7, 14] = 5; kd[:, 7, 15] = 2
    r[..., L] = np.where((kd == 1) | (kd == 3), r[..., 0], r[..., L])
    r[..., P - 1] = np.where((kd == 2) | (kd == 3), r[..., P - 1 - L], r[..., P - 1])
    m = np.where(rng.random((N, 8, 16, P)) < 0.3, r, m); e = np.zeros((N, 8, 16), np.int64)
    for q in range(N):
        for g in range(8):
            k = 8 if g in (0, 7) else int(rng.choice(np.array([7, 8, 8, 9]))); o = rng.permutation(16)
            x[q, g, o[:k]] = rng.integers(0, 256, (k, 1))
            n = max(0, 9 - k - int(rng.integers(0, 2))); e[q, g, o[k:k + n]] = 255
            v = x[q, g][:, r[q, g]]; s = np.min(np.add.reduce(np.abs(v[..., :P - L] - v[..., L:]), axis=0), axis=-1); c = kd[q, g]
            t[q, g] = np.where(c == 0, 0, np.where(c < 4, 1, np.where(c == 4, s, np.where(c == 5, np.minimum(s + 1, 4080), 4080))))
    return pack(x, r, m, t, e)
def setup_inputs_ties(rng):
    x = rng.integers(0, 4, (N, 8, 16, W)); r, m = rng.integers(0, W, (2, N, 8, 16, P))
    w = rng.integers(0, W, (N, 4, 1, 12)); w[..., 0] = 0; w[..., 11] = W - 1
    r[:, 1::2] = np.take_along_axis(np.broadcast_to(w, (N, 4, 16, 12)), rng.integers(0, 12, (N, 4, 16, P)), -1)
    m[:, ::2] = np.where(rng.random((N, 4, 16, P)) < 0.5, r[:, ::2], m[:, ::2])
    return pack(x, r, m, rng.integers(0, 18, (N, 8, 16)), rng.integers(0, 3, (N, 8, 16)))
def setup_inputs_far(rng):
    k = W // 16; n = W - 2 * k; pos = np.argsort(rng.random((N, 8, W)), axis=-1); o = np.argsort(pos, axis=-1)
    share = np.where(np.arange(8) % 2 == 0, 0.5, rng.choice(np.array([0.2, 0.8]), (N, 8)))
    hn = (share * n).astype(np.int64)[..., None]; high = (pos >= k) & (pos < 2 * k + hn)
    x = np.where((pos < 2 * k)[:, :, None], 0, rng.integers(0, 8, (N, 8, 16, W))); x = np.where(high[:, :, None], 255 - x, x)
    c = rng.integers(0, 2, (N, 8, 16, P)); c[:, :, ::2] = (np.arange(P) // L + rng.integers(0, 2, (N, 8, 8, 1))) % 2; c[:, :, 1::4, P - 1] = 0
    u = rng.random((N, 8, 16, P)); hn = hn[..., None]; odd = (np.arange(16) % 2 == 1)[:, None]
    mixed = np.where(c == 1, 2 * k + (u * hn).astype(np.int64), 2 * k + hn + (u * (n - hn)).astype(np.int64))
    i = np.where(odd, c * k + (u * k).astype(np.int64), mixed)
    r = np.take_along_axis(o, i.reshape(N, 8, -1), -1).reshape(N, 8, 16, P)
    i = (1 - c) * k + rng.integers(0, k, (N, 8, 16, P)); far = np.take_along_axis(o, i.reshape(N, 8, -1), -1).reshape(N, 8, 16, P)
    m = np.where(odd & (rng.random((N, 8, 16, P)) < 0.25), far, rng.integers(0, W, (N, 8, 16, P))); m[:, :, 1::4, P - 1] = far[:, :, 1::4, P - 1]
    t = rng.integers(3925, 3976, (N, 8, 16)); t[:, :, ::4] = 3929 + 4 * rng.integers(0, 12, (N, 8, 4)); t[:, :, 1::4] = 0; t[:, :, 3::4] = rng.integers(3900, 4080, (N, 8, 4))
    e = np.where(np.argsort(rng.random((N, 8, 16)), axis=-1) < 12, 254, rng.integers(247, 255, (N, 8, 16)))
    return pack(x, r, m, t, e)
def check_inputs(d):
    bad = []
    for k, lo, hi in (("flood", 0, 255), ("riv", 0, W - 1), ("bord", 0, W - 1), ("th", 0, 4080), ("eps", 0, 255)):
        v = np.asarray(d[k]).astype(np.float64)
        if not (np.all(v >= lo) and np.all(v <= hi)): bad.append("range of " + k)
        elif not np.all(v == np.floor(v)): bad.append("whole numbers in " + k)
    return bad
def columns(x, names):
    return np.take(x, names + W * np.arange(8)[:, None, None], axis=0)
def total(v):
    return np.add.reduce(v, axis=-1, dtype=np.int16)
def reference(flood, riv, bord, th, eps):
    R = riv.astype(np.int64).reshape(N, 8, 16, P); M = bord.astype(np.int64).reshape(N, 8, 16, P); A = np.zeros((N, 8, 16), np.int64)
    T = th.astype(np.int64).reshape(N, 8, 16); E = eps.astype(np.int16).reshape(N, 8, 1, 1, 16)
    X = [np.ascontiguousarray(a.astype(np.float32).astype(np.int16).reshape(8, 16, W).transpose(0, 2, 1)).reshape(8 * W, 16) for a in flood]
    place = np.arange(P)
    for t in range(RO):
        first = np.zeros((N, 8, 16), np.int64); loops = np.zeros((N, 8, 16, L), np.int64)
        for q in range(N):
            r, m = R[q], M[q]; h = r[..., :P - 1]; x = columns(X[q], r); nxt = x[:, :, 1:]; now = np.abs(x[:, :, :P - 1] - nxt)
            before = np.concatenate([r[..., :1], r[..., :P - 2]], axis=-1)
            cand = np.stack([((h * a >> SH) + 37 * h + a + 77 * t) & (W - 1) for a in (before, r[..., 1:], m[..., :P - 1], m[..., 1:])] + [m[..., :P - 1]])
            score = np.stack([total(np.abs(columns(X[q], c) - nxt)) for c in cand])
            best = np.take_along_axis(cand, np.argmin(score, axis=0)[None], 0)[0]
            near = total((np.abs(columns(X[q], best) - nxt) < now).astype(np.int16))
            R[q, :, :, :P - 1] = np.where(near >= 9, best, h)
            x = columns(X[q], R[q]); ok = total(np.abs(x[:, :, :P - L] - x[:, :, L:])) < (T[q] + 16 * A[q])[..., None]
            first[q] = np.where(np.any(ok, axis=-1), np.argmax(ok, axis=-1), P)
            loops[q] = np.take_along_axis(R[q], np.minimum(first[q] + 1, P - L)[..., None] + np.arange(L), -1)
        for q in range(N):
            src = (q - 1 - t % (N - 1)) % N
            lp = np.where((first[src] < P)[..., None], loops[src], loops[q])
            R[q] = np.take_along_axis(np.concatenate([R[q], lp], axis=-1), place + L * (place > first[q][..., None]), -1)
            A[q] = A[q] + (first[q] < P)
            near = total((np.abs(columns(X[q], R[q]) - columns(X[q], M[q])) <= E[q]).astype(np.int16))
            M[q] = np.where(near >= 9, R[q], M[q])
    return {"yr": R.reshape(N, 128, P).astype(np.float32), "ym": M.reshape(N, 128, P).astype(np.float32), "ya": A.reshape(N, 128, 1).astype(np.float32)}

@@ -1,0 +1,686 @@
+from concourse.mybir import AluOpType, AxisListType, ActivationFunctionType
+
+A_ = AluOpType
+F_ = ActivationFunctionType
+BND = [0, 128, 256]
+SC = 1024
+NSP = [1, 2]
+TBP = [0, 66, 130, 240, 256]
+TUNE = {'R2': (10, '.'), 'FR2': (420, 'S'), 'L00': (0, '.'), 'K0': (40, '.'), 'A0': (-35, '.'), 'C12': (120, '.'), 'R1': (-100, '.'), 'C02': (55, '.'), 'C10': (-140, '.'), 'Q11': (165, '.'), 'C11': (30, '.'), 'P01': (0, 'S'), 'FA2': (20, '.'), 'N0': (20, '.'), 'FA1': (-340, '.'), 'FA0': (205, '.'), 'M2': (0, 'S'), 'N1': (130, '.'), 'C00': (-85, 'V'), 'C13': (-30, 'V'), 'FR1': (195, 'V'), 'FR0': (-35, '.'), 'C14': (-105, '.'), 'C03': (30, '.'), 'Q00': (195, '.'), 'E01': (20, '.'), '': (55, '.'), 'C04': (-170, '.'), 'L11': (-40, '.'), 'M0': (-70, 'V'), 'R3': (-85, 'V'), 'P11': (-205, 'S'), 'P10': (-315, 'V'), 'L01': (35, '.'), 'M3': (-150, 'S'), 'R0': (45, 'V'), 'O': (-270, '.'), 'Q10': (-5, '.'), 'P00': (55, 'S'), 'FR3': (-110, 'V'), 'C01': (30, 'S'), 'E10': (30, '.'), 'M1': (40, '.'), 'D0': (-235, '.'), 'A1': (-5, '.'), 'S1': (-100, '.'), 'A3': (-55, '.'), 'S0': (-175, '.'), 'E00': (175, '.'), 'E11': (120, '.'), 'S2': (-5, '.'), 'I': (-95, '.'), 'L10': (-40, '.'), 'FA3': (-35, '.'), 'D1': (5, '.'), 'K1': (-95, '.')}
+WIN = 0.0
+NEARS = [(1, 1)]
+NA = 3
+PEC = 0.46
+RO = 4
+CY = 0.83
+GC = 1.5
+LAT = 70.0
+NCH = len(BND) - 1
+
+SCRATCH = {
+    "X": ("sbuf", [128, 4096], "bfloat16"), "RI": ("sbuf", [128, 256], "int32"), "BI": ("sbuf", [128, 256], "int32"),
+    "TI": ("sbuf", [128, 1], "int32"), "EI": ("sbuf", [128, 1], "int32"), "EPF": ("sbuf", [128, 1], "float32"),
+    "THR": ("sbuf", [128, 1], "float32"), "AC": ("sbuf", [128, 1], "float32"), "CNT": ("sbuf", [128, 1], "float32"),
+    "RN": ("sbuf", [128, 256], "float32"), "MN": ("sbuf", [128, 256], "float32"),
+    "YR": ("sbuf", [128, 272], "float32"), "YM": ("sbuf", [128, 272], "float32"),
+    "RU": ("sbuf", [128, 256], "uint16"), "MU": ("sbuf", [128, 256], "uint16"), "PU": ("sbuf", [128, 256], "uint16"),
+    "RP": ("sbuf", [128, 296], "float32"),
+    "GR": ("sbuf", [128, 4112], "bfloat16"), "GM": ("sbuf", [128, 4096], "bfloat16"), "GP": ("sbuf", [128, 4096], "bfloat16"),
+    "AB": ("sbuf", [128, 3840], "bfloat16"), "NW": ("sbuf", [128, 4096], "bfloat16"), "A3": ("sbuf", [128, 4096], "bfloat16"),
+    "I3": ("sbuf", [128, 4096], "bfloat16"), "NR": ("sbuf", [128, 4096], "bfloat16"),
+    "DM": ("sbuf", [128, 256], "float32"), "DDN": ("sbuf", [128, 256], "float32"), "RM": ("sbuf", [128, 256], "float32"),
+    "BIGC": ("sbuf", [128, 256], "float32"), "IOB": ("sbuf", [128, 128], "bfloat16"), "CMD": ("sbuf", [128, 256], "float32"),
+    "DIAG": ("sbuf", [128, 256], "float32"), "SEG": ("sbuf", [128, 256], "float32"), "IK": ("sbuf", [128, 16], "float32"),
+    "PI": ("sbuf", [128, 1], "int32"), "PF": ("sbuf", [128, 1], "float32"),
+    "ZT": ("sbuf", [128, 144], "bfloat16"), "IP": ("sbuf", [128, 128], "bfloat16"), "IN": ("sbuf", [128, 128], "bfloat16"),
+    "OFF": ("sbuf", [128, 16], "uint16"), "LG": ("sbuf", [128, 256], "float32"), "LS": ("sbuf", [128, 256], "float32"),
+    "LPI": ("sbuf", [128, 16], "int32"), "LD": ("sbuf", [128, 16], "float32"),
+    "KB0": ("psum", [128, 512], "float32"), "KB1": ("psum", [128, 512], "float32"), "CB": ("psum", [128, 512], "float32"),
+    "NB": ("psum", [128, 512], "float32"),
+    "SB0": ("psum", [128, 1024], "float32"), "SB1": ("psum", [128, 1024], "float32"),
+}
+for _k in range(NCH):
+    _n = BND[_k + 1] - BND[_k]
+    SCRATCH["CI%d" % _k] = ("sbuf", [128, 4 * _n], "int32")
+    SCRATCH["CU%d" % _k] = ("sbuf", [128, 4 * _n], "uint16")
+    SCRATCH["DS%d" % _k] = ("sbuf", [128, 64 * _n], "bfloat16")
+    SCRATCH["DA%d" % _k] = ("sbuf", [128, 80 * _n], "bfloat16")
+    SCRATCH["KM%d" % _k] = ("sbuf", [128, _n], "float32")
+    SCRATCH["KI%d" % _k] = ("sbuf", [128, _n], "int32")
+    SCRATCH["MI%d" % _k] = ("sbuf", [128, _n], "int32")
+    SCRATCH["FI%d" % _k] = ("sbuf", [128, _n], "float32")
+    SCRATCH["OU%d" % _k] = ("sbuf", [128, _n], "uint16")
+    SCRATCH["DD%d" % _k] = ("sbuf", [128, _n], "float32")
+    SCRATCH["CM%d" % _k] = ("sbuf", [128, 4 * _n], "bfloat16")
+for _k in range(RO):
+    SCRATCH["SEND%d" % _k] = ("sbuf", [128, 16], "float32")
+    SCRATCH["LAND%d" % _k] = ("sbuf", [128, 16], "float32")
+LOADS = ["RI", "BI", "X", "TI", "EI"]
+OUTS = ["yr", "ym", "ya"]
+SEMAPHORES = (["qV", "qS", "qP", "qG"] + ["ld" + n for n in LOADS] + ["st" + n for n in OUTS]
+              + ["arr%d" % t for t in range(RO)] + ["snt%d" % t for t in range(RO)])
+PSUM = [n for n in SCRATCH if SCRATCH[n][0] == "psum"]
+POOL = ["SB0", "SB1"]
+BW = 1024
+
+
+def sl(T, r):
+    return T[r[0]][:, r[1]:r[2]]
+
+
+def build_ops():
+    ops = []
+    seen = {}
+    cur = [""]
+
+    def O(engs, fn, R, W, **kw):
+        op = dict(kw, engs=engs, fn=fn, R=list(R), W=list(W), preds={}, i=len(ops), grp=cur[0])
+        for rd, lst in ((True, op["R"]), (False, op["W"])):
+            for (b, c0, c1) in lst:
+                if b == "POOL":
+                    continue
+                ws, rs = seen.setdefault(b, ([], []))
+                for (x0, x1, q) in ws:
+                    if x0 < c1 and c0 < x1:
+                        op["preds"][q["i"]] = 1
+                if not rd:
+                    for (x0, x1, q) in rs:
+                        if x0 < c1 and c0 < x1:
+                            op["preds"][q["i"]] = 1
+        for (b, c0, c1) in op["R"]:
+            if b != "POOL":
+                seen[b][1].append((c0, c1, op))
+        for (b, c0, c1) in op["W"]:
+            if b != "POOL":
+                ws, rs = seen[b]
+                ws[:] = [w for w in ws if not (c0 <= w[0] and w[1] <= c1)] + [(c0, c1, op)]
+                rs[:] = [w for w in rs if not (c0 <= w[0] and w[1] <= c1) or w[2] is op]
+        op["preds"].pop(op["i"], None)
+        ops.append(op)
+        return op
+
+    def vt(n, c):
+        return 55 + CY * max(64, n * c)
+
+    def tt(o, a, b, alu, cost=None):
+        n = o[2] - o[1]
+        if cost is None:
+            cost = 1 if (a[0] in PSUM or b[0] in PSUM) else 2
+        return O({"V": vt(n, cost)}, lambda e, g, T, op: g.vector.tensor_tensor(sl(T, o), sl(T, a), sl(T, b), alu), [a, b], [o])
+
+    def tsc(o, a, s1, s2, op0, op1=None, cost=1, sreads=()):
+        n = o[2] - o[1]
+
+        def fn(e, g, T, op):
+            v1 = sl(T, s1) if isinstance(s1, tuple) else s1
+            v2 = sl(T, s2) if isinstance(s2, tuple) else s2
+            if op1 is None:
+                return g.vector.tensor_scalar(sl(T, o), sl(T, a), v1, None, op0)
+            return g.vector.tensor_scalar(sl(T, o), sl(T, a), v1, v2, op0, op1)
+        rd = [a] + [s for s in (s1, s2) if isinstance(s, tuple)]
+        return O({"V": vt(n, cost)}, fn, rd, [o])
+
+    def copy(o, a, both=False):
+        n = o[2] - o[1]
+        engs = {"V": vt(n, 1)}
+        if both:
+            engs["S"] = 70 + CY * n
+
+        def fn(e, g, T, op):
+            if e == "V":
+                return g.vector.tensor_copy(sl(T, o), sl(T, a))
+            return g.scalar.activation(sl(T, o), sl(T, a), F_.Copy)
+        return O(engs, fn, [a], [o])
+
+    def affine(o, a, mul, add):
+        n = o[2] - o[1]
+
+        def fn(e, g, T, op):
+            if e == "V":
+                if mul == 1.0:
+                    return g.vector.tensor_scalar(sl(T, o), sl(T, a), add, None, A_.add)
+                return g.vector.tensor_scalar(sl(T, o), sl(T, a), mul, add, A_.mult, A_.add)
+            return g.scalar.activation(sl(T, o), sl(T, a), F_.Copy, bias=add, scale=mul)
+        return O({"V": vt(n, 1), "S": 70 + CY * n}, fn, [a], [o])
+
+    def memset(o, v):
+        return O({"V": vt(o[2] - o[1], 0.5)}, lambda e, g, T, op: g.vector.memset(sl(T, o), v), [], [o])
+
+    def gather(o, win, off, only=None):
+        n = o[2] - o[1]
+        engs = {"V": 50 + GC * CY * n, "S": 65 + GC * CY * n}
+        if only:
+            engs = {only: engs[only]}
+
+        def fn(e, g, T, op):
+            src = sl(T, win).indirect(sl(T, off))
+            if e == "V":
+                return g.vector.tensor_copy(sl(T, o), src)
+            return g.scalar.activation(sl(T, o), src, F_.Copy)
+        return O(engs, fn, [win, off], [o])
+
+    def gather_tt(o, win, off, b, alu):
+        n = o[2] - o[1]
+        return O({"V": 50 + GC * CY * n}, lambda e, g, T, op: g.vector.tensor_tensor(sl(T, o), sl(T, win).indirect(sl(T, off)), sl(T, b), alu),
+                 [win, off, b], [o])
+
+    def blocks(o, a, b):
+        tot = o[2] - o[1]
+        w = -(-tot // ((tot + BW - 1) // BW))
+        w = -(-w // 32) * 32
+        for c in range(0, tot, w):
+            m = min(w, tot - c)
+            yield [(x[0], x[1] + c, x[1] + c + m) for x in (o, a, b)] + [m]
+
+    def sub_op(a1, b1, m):
+        def sub(e, g, T, op):
+            r = None
+            for x in range(0, m, 512):
+                y = min(x + 512, m)
+                d = T[op["bank"]][:, x:y]
+                g.tensor.matmul(d, T.IP[:], T[a1[0]][:, a1[1] + x:a1[1] + y], True, False)
+                r = g.tensor.matmul(d, T.IN[:], T[b1[0]][:, b1[1] + x:b1[1] + y], False, True)
+            return r
+        return O({"P": 2 * PEC * max(64, m) + 30}, sub, [a1, b1, ("IP", 0, 128), ("IN", 0, 128)], [("POOL", 0, m)], alloc=True)
+
+    def signdiff(o, a, b):
+        absdiff(o, a, b, F_.Sign, -0.5)
+
+    def absdiff(o, a, b, func=F_.Abs, bias=0.0):
+        for o1, a1, b1, m in blocks(o, a, b):
+            q = sub_op(a1, b1, m)
+            r = O({"S": 70 + CY * m}, lambda e, g, T, op, o1=o1, m=m: g.scalar.activation(sl(T, o1), T[op["src"]["bank"]][:, 0:m], func, bias=bias),
+                  [("POOL", 0, m)], [o1], src=q)
+            r["preds"][q["i"]] = 1
+
+    def cand_abs(o, win, off, b, ds):
+        tot = o[2] - o[1]
+
+        def fn(e, g, T, op):
+            src = sl(T, win).indirect(sl(T, off))
+            if e == "V":
+                return g.vector.tensor_tensor(sl(T, ds), src, sl(T, b), A_.subtract)
+            return g.scalar.activation(sl(T, ds), src, F_.Copy)
+        G = O({"V": 50 + GC * CY * tot, "S": 65 + GC * CY * tot}, fn, [win, off, b], [ds])
+        G["subs"], G["abss"] = [], []
+        for o1, a1, b1, m in blocks(o, ds, b):
+            c = o1[1] - o[1]
+            q = sub_op(a1, b1, m)
+
+            def ab(e, g, T, op, o1=o1, m=m):
+                if op.get("whole"):
+                    return g.scalar.activation(sl(T, o), sl(T, ds), F_.Abs)
+                return g.scalar.activation(sl(T, o1), T[op["src"]["bank"]][:, 0:m], F_.Abs)
+            r = O({"S": 70 + CY * m}, ab, [ds, ("POOL", 0, m)], [o if c == 0 else o1], src=q, wdur=70 + CY * tot)
+            r["preds"][q["i"]] = 1
+            G["subs"].append(q["i"])
+            G["abss"].append(r["i"])
+        for x in G["abss"][1:]:
+            ops[x]["preds"].pop(G["abss"][0], None)
+
+    def stage_sum(o, a, tag=None):
+        n = o[2] - o[1]
+
+        def fn(e, g, T, op):
+            d = sl(T, o)
+            r = None
+            for x in tag or []:
+                g.tensor.matmul(d, T.IP[:], sl(T, x), x is tag[0], False)
+            for p in range(16):
+                r = g.tensor.matmul(d, T.ZT[:, 15 - p:143 - p], T[a[0]][:, a[1] + p:a[2]:16], tag is None and p == 0, p == 15)
+            return r
+        rd = [a, ("ZT", 0, 144)] + (tag + [("IP", 0, 128)] if tag is not None else [])
+        O({"P": (16 + len(tag or [])) * PEC * max(64, n) + 30}, fn, rd, [o])
+
+    def load(dst, src, w, ns):
+        O({"Y": ns}, lambda e, g, T, op: g.sync.dma_start(T[dst][:], T[src][:]), [], [(dst, 0, w)], sem="ld" + dst)
+    load("RI", "riv", 256, 2000)
+    load("X", "flood", 4096, 7000)
+    load("BI", "bord", 256, 2500)
+    load("TI", "th", 1, 2500)
+    load("EI", "eps", 1, 2500)
+
+    def gop(fn, ns, R, W):
+        O({"G": ns}, fn, R, W)
+
+    def sel(buf, n, pattern, base, cm, cmp):
+        gop(lambda e, g, T, op: g.affine_select(T[buf][:], T[buf][:], pattern, cmp, 0.0, base, cm), 170 + 2 * CY * n, [(buf, 0, n)], [(buf, 0, n)])
+    memset(("ZT", 0, 144), float(SC))
+    memset(("IP", 0, 128), 1.0)
+    sel("IP", 128, [[-1, 128]], 0, 1, A_.is_equal)
+    sel("ZT", 144, [[0, 9], [1, 16]], -15, 0, A_.is_equal)
+    sel("ZT", 144, [[-16, 9], [0, 16]], 0, 1, A_.is_ge)
+    sel("ZT", 144, [[16, 9], [0, 16]], 15, -1, A_.is_ge)
+    gop(lambda e, g, T, op: g.iota(T.PI[:], [[0, 1]], 0, 1), 140, [], [("PI", 0, 1)])
+    gop(lambda e, g, T, op: g.iota(T.IOB[:], [[1, 128]], 0, 0, allow_small_or_imprecise_dtypes=True), 350, [], [("IOB", 0, 128)])
+    gop(lambda e, g, T, op: g.iota(T.CMD[:], [[0, 16], [1, 16]], 0, 0, allow_small_or_imprecise_dtypes=True), 560, [], [("CMD", 0, 256)])
+    gop(lambda e, g, T, op: g.iota(T.IK[:], [[1, 16]], 256, 0, allow_small_or_imprecise_dtypes=True), 160, [], [("IK", 0, 16)])
+    tsc(("IN", 0, 128), ("IP", 0, 128), -1.0, None, A_.mult)
+    tsc(("PI", 0, 1), ("PI", 0, 1), 15, None, A_.bitwise_and)
+    copy(("PF", 0, 1), ("PI", 0, 1))
+    tsc(("DIAG", 0, 256), ("CMD", 0, 256), ("PF", 0, 1), None, A_.is_equal)
+    tsc(("SEG", 0, 256), ("CMD", 0, 256), 0.5, None, A_.is_gt)
+    memset(("BIGC", 0, 256), 1.0e7)
+    memset(("NW", 4080, 4096), 0.0)
+    memset(("GR", 4096, 4112), 0.0)
+    memset(("YR", 264, 272), 0.0)
+    memset(("YM", 256, 272), 0.0)
+    memset(("RP", 264, 296), -4096.0)
+    memset(("AC", 0, 1), 0.0)
+    for k in range(NCH):
+        n = BND[k + 1] - BND[k]
+        for m in range(1, 5):
+            memset(("CM%d" % k, (m - 1) * n, m * n), float(m * n))
+
+    XWIN = ("X", 0, 4096)
+    TB = TBP
+    NT = len(TB) - 1
+
+    def first_names(ta, tb):
+        tsc(("RU", ta, tb), ("RI", ta, tb), 0, None, A_.add)
+        copy(("RN", ta, tb), ("RI", ta, tb))
+
+    def names_side(t, ta, tb, kind):
+        if kind == "R":
+            gather(("GR", 16 * ta, 16 * tb), XWIN, ("RU", ta, tb))
+            affine(("NB", ta, tb), ("RN", ta, tb), 1.0, 32.0)
+            affine(("YR", 8 + ta, 8 + tb), ("RN", ta, tb), 1.0, -2912.0)
+            if ta == 0:
+                affine(("YR", 7, 8), ("RN", 0, 1), 1.0, -2912.0)
+            affine(("NB", 256 + ta, 256 + tb), ("RN", ta, tb), 128.0, 2912.0 + 77.0 * t)
+        else:
+            affine(("YM", ta, tb), ("MN", ta, tb), 1.0, -2912.0)
+            gather(("GM", 16 * ta, 16 * tb), XWIN, ("MU", ta, tb))
+
+    def accretion(ta, tb, last):
+        absdiff(("A3", 16 * ta, 16 * tb), ("GR", 16 * ta, 16 * tb), ("GM", 16 * ta, 16 * tb))
+        tsc(("I3", 16 * ta, 16 * tb), ("A3", 16 * ta, 16 * tb), ("EPF", 0, 1), None, A_.is_le, cost=0.5)
+        c = ("CB", ta, tb)
+        stage_sum(c, ("I3", 16 * ta, 16 * tb))
+        mn = ("MN", ta, tb)
+        tt(("DM", ta, tb), ("RN", ta, tb), mn, A_.subtract)
+        tsc(c, c, 8.5 * SC, None, A_.is_gt)
+        tt(c, c, ("DM", ta, tb), A_.mult)
+        tt(mn, c, mn, A_.add)
+        if not last:
+            copy(("MU", ta, tb), mn)
+
+    def cand_lists(k, half):
+        a, b = BND[k], BND[k + 1]
+        n = b - a
+        ci = "CI%d" % k
+        lo, hi = (0, 2 * n) if half == 0 else (2 * n, 4 * n)
+        other = [("YR", 7 + a, 7 + b), ("YR", 9 + a, 9 + b)] if half == 0 else [("YM", a, b), ("YM", a + 1, b + 1)]
+        for q in range(2):
+            tt((ci, lo + q * n, lo + q * n + n), ("NB", a, b), other[q], A_.mult)
+        tsc((ci, lo, hi), (ci, lo, hi), 5, None, A_.arith_shift_right)
+        for q in range(2):
+            r = (ci, lo + q * n, lo + q * n + n)
+            tt(r, ("NB", 256 + a, 256 + b), r, A_.add)
+        tsc((ci, lo, hi), (ci, lo, hi), 4095, None, A_.bitwise_and)
+        copy(("CU%d" % k, lo, hi), (ci, lo, hi))
+
+    def kreg(k, m):
+        n = BND[k + 1] - BND[k]
+        if m == 4:
+            return ("CB", 256 + BND[k], 256 + BND[k] + n)
+        return ("KB%d" % (k % 2), m * n, m * n + n)
+
+    def key(k, m):
+        n = BND[k + 1] - BND[k]
+        stage_sum(kreg(k, m), ("DA%d" % k, 16 * n * m, 16 * n * (m + 1)),
+                  [("IOB", 0, n)] + ([("CM%d" % k, (m - 1) * n, m * n)] if m else []))
+
+    def cand_heights(k, m):
+        a, b = BND[k], BND[k + 1]
+        n = b - a
+        nxt = ("GR", 16 * a + 16, 16 * b + 16)
+        da = ("DA%d" % k, 16 * n * m, 16 * n * (m + 1))
+        if m < 4:
+            ds = ("DS%d" % k, 16 * n * m, 16 * n * (m + 1))
+            cand_abs(da, XWIN, ("CU%d" % k, m * n, m * n + n), nxt, ds)
+        else:
+            absdiff(da, ("GM", 16 * a, 16 * b), nxt)
+        key(k, m)
+
+    def choose(k):
+        a, b = BND[k], BND[k + 1]
+        n = b - a
+        kb = "KB%d" % (k % 2)
+        cur[0] = "K%d" % k
+        km, ki = ("KM%d" % k, 0, n), ("KI%d" % k, 0, n)
+        order = [4, 0, 1, 2, 3]
+        copy(km, kreg(k, order[0]), both=True)
+        for m in order[1:]:
+            tt(ki if m == order[-1] else km, kreg(k, m), km, A_.min)
+        tsc(("MI%d" % k, 0, n), ki, SC - 1, None, A_.bitwise_and)
+        tsc(("OU%d" % k, 0, n), ("MI%d" % k, 0, n), 16.0, ("PF", 0, 1), A_.mult, A_.add)
+        ps = [a + n * q // NSP[k] for q in range(NSP[k] + 1)]
+        cur[0] = "E%d" % k
+        for x, y in zip(ps, ps[1:]):
+            nr, win, off = ("NR", 16 * x, 16 * y), ("DA%d" % k, 0, 80 * n), ("OU%d" % k, x - a, y - a)
+            cur[0] = "E%d%d" % (k, ps.index(x))
+            if (k, ps.index(x)) in NEARS:
+                gather(nr, win, off, "S")
+                signdiff(nr, ("NW", 16 * x, 16 * y), nr)
+            else:
+                gather_tt(nr, win, off, ("NW", 16 * x, 16 * y), A_.is_lt)
+            stage_sum(("CB", x, y), nr)
+        dd = ("DD%d" % k, 0, n)
+        cur[0] = "D%d" % k
+        for m in range(5):
+            r = kreg(k, m)
+            tt(r, r, ki, A_.is_equal)
+        tt((kb, 0, 4 * n), (kb, 0, 4 * n), ("CI%d" % k, 0, 4 * n), A_.mult)
+        r = kreg(k, 4)
+        tt(r, r, ("MN", a, b), A_.mult)
+        tt(dd, (kb, 0, n), ("RN", a, b), A_.subtract)
+        for m in range(1, 5):
+            tt(dd, kreg(k, m), dd, A_.add)
+        for x, y in zip(ps, ps[1:]):
+            cur[0] = "P%d%d" % (k, ps.index(x))
+            c = ("CB", x, y)
+            tsc(c, c, (1.0 if (k, ps.index(x)) in NEARS else 8.5) * SC, None, A_.is_gt)
+            tt(c, c, (dd[0], x - a, y - a), A_.mult)
+            rp = ("RP", 8 + x, 8 + y)
+            tt(rp, c, ("RN", x, y), A_.add)
+            copy(("PU", x, y), rp)
+            gather(("GP", 16 * x, 16 * y), XWIN, ("PU", x, y))
+
+    def necks(na, nb, last):
+        absdiff(("AB", 16 * na, 16 * nb), ("GP", 16 * na, 16 * nb), ("GP", 16 * na + 256, 16 * nb + 256))
+        stage_sum(("NB", na, nb), ("AB", 16 * na, 16 * nb))
+        tt(("DDN", na, nb), ("RP", 24 + na, 24 + nb), ("RP", 8 + na, 8 + nb), A_.subtract)
+        hi = 255 if last else nb
+        n = hi - na
+        ini = ("RM", na - 1, na) if na else 1.0e7
+        rd = [("NB", na, hi), ("BIGC", na, hi)] + ([ini] if na else [])
+        O({"V": vt(n, 1)}, lambda e, g, T, op: g.vector.tensor_tensor_scan(T.RM[:, na:hi], T.NB[:, na:hi], T.BIGC[:, na:hi],
+            sl(T, ini) if na else 1.0e7, A_.min, A_.min), rd, [("RM", na, hi)])
+        tsc(("NB", 257 + na, 257 + hi), ("RM", na, hi), ("THR", 0, 1), None, A_.is_lt)
+
+    def shift(ta, tb, last):
+        m = ("NB", ta, tb)
+        tt(m, ("NB", 256 + ta, 256 + tb), ("DDN", ta, tb), A_.mult)
+        tt(("RN", ta, tb), m, ("RP", 8 + ta, 8 + tb), A_.add)
+        copy(("RU", ta, tb), ("RN", ta, tb))
+
+    def loops(t):
+        O({"V": vt(256, 1)}, lambda e, g, T, op: g.vector.tensor_reduce(T.CNT[:], T.NB[:, 256:512], AxisListType.X, A_.add),
+          [("NB", 256, 512)], [("CNT", 0, 1)])
+        tsc(("OFF", 0, 16), ("IK", 0, 16), ("CNT", 0, 1), None, A_.subtract)
+        gather_tt(("LG", 0, 256), ("RP", 8, 296), ("OFF", 0, 16), ("DIAG", 0, 256), A_.mult)
+        O({"V": vt(256, 1)}, lambda e, g, T, op: g.vector.tensor_tensor_scan(T.LS[:], T.SEG[:], T.LG[:], 0.0, A_.mult, A_.add),
+          [("SEG", 0, 256), ("LG", 0, 256)], [("LS", 0, 256)])
+        s = "SEND%d" % t
+        O({"V": vt(16, 1)}, lambda e, g, T, op: g.vector.tensor_scalar(T[s][:], T.LS[:, 15:256:16], 4096.0, None, A_.add),
+          [("LS", 0, 256)], [(s, 0, 16)])
+        snd = O({"G": 1500}, None, [(s, 0, 16)], [], send=t)
+        tsc(("AC", 0, 1), ("NB", 511, 512), ("AC", 0, 1), None, A_.add)
+        tsc(("THR", 0, 1), ("NB", 511, 512), 16.0 * SC, ("THR", 0, 1), A_.mult, A_.add)
+        return snd
+
+    def loop_in(t, snd, last):
+        q = O({"V": vt(16, 2)}, lambda e, g, T, op: g.vector.tensor_tensor(T.LPI[:], T["LAND%d" % t][:], T.LS[:, 15:256:16], A_.max),
+              [("LS", 0, 256)], [("LPI", 0, 16)], ext="arr%d" % t)
+        q["preds"][snd["i"]] = 1
+        tsc(("LPI", 0, 16), ("LPI", 0, 16), 4095, None, A_.bitwise_and)
+        tt(("LD", 0, 16), ("LPI", 0, 16), ("RP", 248, 264), A_.subtract)
+        tt(("LD", 0, 16), ("NB", 496, 512), ("LD", 0, 16), A_.mult)
+        tt(("RN", 240, 256), ("LD", 0, 16), ("RP", 248, 264), A_.add)
+        copy(("RU", 240, 256), ("RN", 240, 256))
+
+    for i in range(NT):
+        first_names(TB[i], TB[i + 1])
+    copy(("MN", 0, 256), ("BI", 0, 256))
+    copy(("MU", 0, 256), ("BI", 0, 256))
+    copy(("EPF", 0, 1), ("EI", 0, 1))
+    tsc(("THR", 0, 1), ("TI", 0, 1), float(SC), None, A_.mult)
+    for t in range(RO):
+        for i in range(NT):
+            ta, tb = TB[i], TB[i + 1]
+            cur[0] = "R%d" % i
+            names_side(t, ta, tb, "R")
+            if i >= NA - 1 and i < NT - 1:
+                continue
+            if i == NT - 1:
+                ta = TB[NA - 1]
+            if t:
+                cur[0] = "A%d" % i
+                accretion(ta, tb, False)
+            cur[0] = "M%d" % i
+            names_side(t, ta, tb, "M")
+        for k in range(NCH):
+            a, b = BND[k], BND[k + 1]
+            cur[0] = "L%d0" % k
+            cand_lists(k, 0)
+            cur[0] = "L%d1" % k
+            cand_lists(k, 1)
+            hi = min(16 * b, 4080)
+            for m in (4, 0, 1, 2, 3):
+                cur[0] = "C%d%d" % (k, m)
+                cand_heights(k, m)
+            cur[0] = "N%d" % k
+            absdiff(("NW", 16 * a, hi), ("GR", 16 * a, hi), ("GR", 16 * a + 16, hi + 16))
+            choose(k)
+            for q in range(NSP[k]):
+                x, y = a + (b - a) * q // NSP[k], a + (b - a) * (q + 1) // NSP[k]
+                cur[0] = "Q%d%d" % (k, q)
+                if y == 256:
+                    memset(("NB", 240, 255), 1.0e7)
+                    memset(("NB", 256, 257), 0.0)
+                necks(x - 16 if x else 0, y - 16, y == 256)
+        cur[0] = "O"
+        snd = loops(t)
+        for i in range(NT - 1):
+            cur[0] = "S%d" % i
+            shift(TB[i], TB[i + 1], t == RO - 1)
+        cur[0] = "I"
+        loop_in(t, snd, t == RO - 1)
+    for i in range(NT):
+        ta, tb = TB[i], TB[i + 1]
+        cur[0] = "FR%d" % i
+        gather(("GR", 16 * ta, 16 * tb), XWIN, ("RU", ta, tb))
+        cur[0] = "FA%d" % i
+        accretion(ta, tb, True)
+
+    def store(dst, src, w):
+        O({"Y": 2000}, lambda e, g, T, op: g.sync.dma_start(T[dst][:], T[src][:, 0:w]), [(src, 0, w)], [], sem="st" + dst)
+    store("ya", "AC", 1)
+    store("yr", "RN", 256)
+    store("ym", "MN", 256)
+    return ops
+
+
+def schedule(ops):
+    n = len(ops)
+    succ = [[] for _ in range(n)]
+    left = [0] * n
+    for op in ops:
+        for p in op["preds"]:
+            succ[p].append(op["i"])
+            left[op["i"]] += 1
+    prio = [0.0] * n
+    free = {e: 0.0 for e in "VSPGY"}
+    fin = [0.0] * n
+    bank = {}
+    pool = {b: None for b in POOL}
+    ready = [i for i in range(n) if left[i] == 0]
+    order = []
+    choice = {}
+    for op in ops:
+        off, ch = TUNE.get(op["grp"], (0, "."))
+        prio[op["i"]] = -(op["i"] + off)
+        if len(op["engs"]) > 1 and ch in op["engs"] and max(op["engs"].values()) > 300:
+            choice[op["i"]] = ch
+
+    def done(i, f):
+        fin[i] = f
+        for q in succ[i]:
+            left[q] -= 1
+            if left[q] == 0:
+                if ops[q].get("null"):
+                    done(q, max([fin[p] for p in ops[q]["preds"]]))
+                else:
+                    ready.append(q)
+
+    for op in ops:
+        op["bk"] = sorted({r[0] for r in op["R"] + op["W"] if r[0] in PSUM})
+
+    while ready:
+        best = None
+        found = []
+        for i in ready:
+            op = ops[i]
+            t0 = 0.0
+            for p in op["preds"]:
+                x = fin[p] + LAT + (1500 if "send" in ops[p] else 0)
+                t0 = max(t0, x)
+            bk = None
+            if op.get("alloc"):
+                opts = [(fin[c] + LAT if c is not None else 0.0, b) for b, c in pool.items() if c != -1]
+                if not opts:
+                    continue
+                x, bk = min(opts)
+                t0 = max(t0, x)
+            cand = None
+            for e, d in op["engs"].items():
+                if choice.get(i, e) != e:
+                    continue
+                s = max(t0, free[e])
+                for b in op["bk"]:
+                    for f, (x, q) in bank.get(b, {}).items():
+                        if f != e:
+                            s = max(s, x + LAT)
+                if cand is None or s + d < cand[0]:
+                    cand = (s + d, s, e)
+            ef, s, e = cand
+            found.append((s, i, e, ef, bk))
+            if best is None or s < best[0]:
+                best = found[-1]
+        s0, e0 = best[0] + WIN, best[2]
+        for x in found:
+            if x[2] == e0 and x[0] <= s0 and prio[x[1]] > prio[best[1]]:
+                best = x
+        s, i, e, ef, bk = best
+        op = ops[i]
+        if "subs" in op and e == "V":
+            for x in op["subs"] + op["abss"][1:]:
+                ops[x]["null"] = True
+            z = ops[op["abss"][0]]
+            z["whole"] = True
+            z["engs"] = {"S": z["wdur"]}
+        ready.remove(i)
+        op["eng"] = e
+        op["deps"] = list(op["preds"])
+        if op.get("alloc"):
+            op["bank"] = bk
+            if pool[bk] is not None:
+                op["deps"].append(pool[bk])
+            pool[bk] = -1
+        if "src" in op and not op.get("whole"):
+            pool[op["src"]["bank"]] = i
+        for b in op["bk"]:
+            d = bank.setdefault(b, {})
+            for f, (x, q) in d.items():
+                if f != e:
+                    op["deps"].append(q)
+            d[e] = (ef, i)
+        op["start"] = s
+        free[e] = s + 60.0 if e == "Y" else ef
+        order.append(i)
+        done(i, ef)
+    return order, max(fin)
+
+
+def make_plan():
+    ops = build_ops()
+    order, span = schedule(ops)
+    know = {e: {} for e in "VSPGY"}
+    cnt = {"V": 0, "S": 0, "P": 0, "G": 0}
+    out = []
+    for i in order:
+        op = ops[i]
+        e = op["eng"]
+        need = {}
+        srcs = []
+        deps = list(op["deps"])
+        for d in deps:
+            q = ops[d]
+            if q.get("null"):
+                deps.extend(x for x in q["preds"] if x not in deps)
+                continue
+            if "send" in q:
+                if "ext" in op:
+                    need[op["ext"]] = "ARR"
+                continue
+            sem, v = q["tok"]
+            if know[e].get(sem, 0) < v:
+                srcs.append((v, sem, q))
+        srcs.sort(key=lambda x: -x[2]["pos"])
+        for v, sem, q in srcs:
+            if know[e].get(sem, 0) >= v:
+                continue
+            need[sem] = max(need.get(sem, 0), v)
+            know[e][sem] = v
+            for s2, v2 in q["clk"].items():
+                if know[e].get(s2, 0) < v2:
+                    know[e][s2] = v2
+        op["waits"] = need
+        op["clk"] = dict(know[e])
+        op["pos"] = len(out)
+        if "sem" in op:
+            op["tok"] = (op["sem"], 16)
+        elif "send" in op:
+            op["tok"] = None
+        else:
+            cnt[e] += 1
+            op["tok"] = ("q" + e, cnt[e])
+        out.append(op)
+    return out, cnt, span
+
+
+CACHE = {}
+
+
+def rank_program(g, core, T, topo):
+    rank = T.rank_of(core)
+    if rank is None:
+        return
+    if "plan" not in CACHE:
+        CACHE["plan"] = make_plan()
+    plan, cnt, span = CACHE["plan"]
+    N = len(T.cores)
+    hand = {"V": g.vector, "S": g.scalar, "P": g.tensor, "G": g, "Y": g.sync}
+
+    def link(src, dst):
+        return topo.engines(src, dst)[:4]
+
+    for op in plan:
+        e = op["eng"]
+        h = hand[e]
+        for sem, v in op["waits"].items():
+            if v == "ARR":
+                t = int(sem[3:])
+                v = len(link(T.cores[(rank - 1 - t % (N - 1)) % N], core))
+            h.wait_ge(T.sem[sem], v)
+        if "send" in op:
+            t = op["send"]
+            dst = T.cores[(rank + 1 + t % (N - 1)) % N]
+            rid, pid, _s = topo.addr(dst)
+            mask = 0
+            for x in link(core, dst):
+                mask |= 1 << x
+            g.remote_dma(T["LAND%d" % t][:], T["SEND%d" % t][:], T.sem["arr%d" % t], T.sem["snt%d" % t], pid, rid, mask)
+            continue
+        ins = op["fn"](e, g, T, op)
+        sem, v = op["tok"]
+        ins.then_inc(T.sem[sem], 16 if "sem" in op else 1)
+    for t in range(RO):
+        g.wait_ge(T.sem["snt%d" % t], len(link(core, T.cores[(rank + 1 + t % (N - 1)) % N])))
+    for e in "VSPG":
+        g.wait_ge(T.sem["q" + e], cnt[e])
+    for n in LOADS:
+        g.sync.wait_ge(T.sem["ld" + n], 16)
+    for n in OUTS:
+        g.sync.wait_ge(T.sem["st" + n], 16)

@@ -1,67 +1,84 @@
+import math
+import numpy as np
 from concourse.mybir import AluOpType, AxisListType, ActivationFunctionType
 
 A_ = AluOpType
 F_ = ActivationFunctionType
-BND = [0, 128, 256]
+BNDS = [[0, 102, 190, 256], [0, 84, 172, 256], [0, 66, 154, 256], [0, 100, 192, 256], [0, 82, 174, 256]]
+NCH = len(BNDS[0]) - 1
+ST = [max(b[k + 1] - b[k] for b in BNDS[:4]) for k in range(NCH)]
+SM = max(ST)
 SC = 1024
-NSP = [1, 2]
-TBP = [0, 66, 130, 240, 256]
-TUNE = {'R2': (10, '.'), 'FR2': (420, 'S'), 'L00': (0, '.'), 'K0': (40, '.'), 'A0': (-35, '.'), 'C12': (120, '.'), 'R1': (-100, '.'), 'C02': (55, '.'), 'C10': (-140, '.'), 'Q11': (165, '.'), 'C11': (30, '.'), 'P01': (0, 'S'), 'FA2': (20, '.'), 'N0': (20, '.'), 'FA1': (-340, '.'), 'FA0': (205, '.'), 'M2': (0, 'S'), 'N1': (130, '.'), 'C00': (-85, 'V'), 'C13': (-30, 'V'), 'FR1': (195, 'V'), 'FR0': (-35, '.'), 'C14': (-105, '.'), 'C03': (30, '.'), 'Q00': (195, '.'), 'E01': (20, '.'), '': (55, '.'), 'C04': (-170, '.'), 'L11': (-40, '.'), 'M0': (-70, 'V'), 'R3': (-85, 'V'), 'P11': (-205, 'S'), 'P10': (-315, 'V'), 'L01': (35, '.'), 'M3': (-150, 'S'), 'R0': (45, 'V'), 'O': (-270, '.'), 'Q10': (-5, '.'), 'P00': (55, 'S'), 'FR3': (-110, 'V'), 'C01': (30, 'S'), 'E10': (30, '.'), 'M1': (40, '.'), 'D0': (-235, '.'), 'A1': (-5, '.'), 'S1': (-100, '.'), 'A3': (-55, '.'), 'S0': (-175, '.'), 'E00': (175, '.'), 'E11': (120, '.'), 'S2': (-5, '.'), 'I': (-95, '.'), 'L10': (-40, '.'), 'FA3': (-35, '.'), 'D1': (5, '.'), 'K1': (-95, '.')}
-WIN = 0.0
-NEARS = [(1, 1)]
-NA = 3
-PEC = 0.46
+YO = 2048.0
+BIG = 12582912.0
+PRM = {
+    "NSP": [[1, 1, 1]] * 4,
+    "TBP": [[1, 1, 1]] * 5,
+    "NA": 0,
+    "ONS": ["C10"],
+    "ONV": ["R2L", "FR2L", "R00@0"],
+    "GW": 128,
+    "PEC": 0.48, "GC": 1.55, "LAT": 100.0, "FV": 55.0, "FS": 75.0, "XLD": 6000.0, "SND": 2000.0,
+    "WIN": 200.0, "FILL": 150.0, "HOLD": 1000.0, "BOOST": 1000.0,
+    "PASSES": 5, "TRIES": 6, "NOISE": 1000.0, "MOVES": 12000, "SEED": 0, "T0": 60.0, "T1": 5.0,
+}
 RO = 4
 CY = 0.83
-GC = 1.5
-LAT = 70.0
-NCH = len(BND) - 1
+ENGINES = 8
+CONST = {"KX": YO + 32.0, "KY": YO, "K1": 2464.0, "K2": 4928.0, "K3": 7392.0}
+DIAGS = {"IP": 1.0, "IA": YO + 32.0, "IB": 1152.0, "IW": YO + 1184.0, "IN": -1.0, "IF": 1.0, "NF": -1.0, "IY": YO}
 
 SCRATCH = {
     "X": ("sbuf", [128, 4096], "bfloat16"), "RI": ("sbuf", [128, 256], "int32"), "BI": ("sbuf", [128, 256], "int32"),
     "TI": ("sbuf", [128, 1], "int32"), "EI": ("sbuf", [128, 1], "int32"), "EPF": ("sbuf", [128, 1], "float32"),
+    "ES": ("sbuf", [128, 1], "float32"), "TH0": ("sbuf", [128, 1], "float32"),
     "THR": ("sbuf", [128, 1], "float32"), "AC": ("sbuf", [128, 1], "float32"), "CNT": ("sbuf", [128, 1], "float32"),
-    "RN": ("sbuf", [128, 256], "float32"), "MN": ("sbuf", [128, 256], "float32"),
-    "YR": ("sbuf", [128, 272], "float32"), "YM": ("sbuf", [128, 272], "float32"),
+    "OR": ("sbuf", [128, 256], "float32"), "OM": ("sbuf", [128, 256], "float32"), "MR": ("sbuf", [128, 256], "float32"),
+    "YR": ("sbuf", [128, 272], "float16"), "YM": ("sbuf", [128, 272], "float16"), "YP": ("sbuf", [128, 280], "float32"),
     "RU": ("sbuf", [128, 256], "uint16"), "MU": ("sbuf", [128, 256], "uint16"), "PU": ("sbuf", [128, 256], "uint16"),
-    "RP": ("sbuf", [128, 296], "float32"),
     "GR": ("sbuf", [128, 4112], "bfloat16"), "GM": ("sbuf", [128, 4096], "bfloat16"), "GP": ("sbuf", [128, 4096], "bfloat16"),
     "AB": ("sbuf", [128, 3840], "bfloat16"), "NW": ("sbuf", [128, 4096], "bfloat16"), "A3": ("sbuf", [128, 4096], "bfloat16"),
     "I3": ("sbuf", [128, 4096], "bfloat16"), "NR": ("sbuf", [128, 4096], "bfloat16"),
-    "DM": ("sbuf", [128, 256], "float32"), "DDN": ("sbuf", [128, 256], "float32"), "RM": ("sbuf", [128, 256], "float32"),
-    "BIGC": ("sbuf", [128, 256], "float32"), "IOB": ("sbuf", [128, 128], "bfloat16"), "CMD": ("sbuf", [128, 256], "float32"),
-    "DIAG": ("sbuf", [128, 256], "float32"), "SEG": ("sbuf", [128, 256], "float32"), "IK": ("sbuf", [128, 16], "float32"),
-    "PI": ("sbuf", [128, 1], "int32"), "PF": ("sbuf", [128, 1], "float32"),
-    "ZT": ("sbuf", [128, 144], "bfloat16"), "IP": ("sbuf", [128, 128], "bfloat16"), "IN": ("sbuf", [128, 128], "bfloat16"),
+    "MK": ("sbuf", [128, 256], "bfloat16"), "MA": ("sbuf", [128, 256], "bfloat16"), "M0": ("sbuf", [128, 256], "bfloat16"),
+    "MS": ("sbuf", [128, 256], "bfloat16"), "ZE": ("sbuf", [128, 256], "bfloat16"), "JK": ("sbuf", [128, 256], "bfloat16"),
+    "TG": ("sbuf", [128, 5 * SM], "float16"), "TF": ("sbuf", [128, 5 * SM], "float32"), "CMD": ("sbuf", [128, 256], "float32"),
+    "DIAG": ("sbuf", [128, 256], "float32"), "SEG": ("sbuf", [128, 256], "bfloat16"), "IK": ("sbuf", [128, 16], "float32"),
+    "PI": ("sbuf", [128, 1], "int32"), "PF": ("sbuf", [128, 1], "float32"), "ZT": ("sbuf", [128, 144], "bfloat16"),
+    "EP": ("sbuf", [128, 128], "float16"), "EN": ("sbuf", [128, 128], "float16"),
     "OFF": ("sbuf", [128, 16], "uint16"), "LG": ("sbuf", [128, 256], "float32"), "LS": ("sbuf", [128, 256], "float32"),
-    "LPI": ("sbuf", [128, 16], "int32"), "LD": ("sbuf", [128, 16], "float32"),
-    "KB0": ("psum", [128, 512], "float32"), "KB1": ("psum", [128, 512], "float32"), "CB": ("psum", [128, 512], "float32"),
+    "LPI": ("sbuf", [128, 16], "int32"), "OWN": ("sbuf", [128, 16], "float32"),
+    "KB0": ("psum", [128, 512], "float32"), "KB1": ("psum", [128, 512], "float32"), "KB2": ("psum", [128, 512], "float32"),
     "NB": ("psum", [128, 512], "float32"),
     "SB0": ("psum", [128, 1024], "float32"), "SB1": ("psum", [128, 1024], "float32"),
 }
+for _k in CONST:
+    SCRATCH[_k] = ("sbuf", [128, SM + 2], "bfloat16")
+for _k in DIAGS:
+    SCRATCH[_k] = ("sbuf", [128, 128], "float32" if _k[1] == "F" else "bfloat16")
 for _k in range(NCH):
-    _n = BND[_k + 1] - BND[_k]
-    SCRATCH["CI%d" % _k] = ("sbuf", [128, 4 * _n], "int32")
-    SCRATCH["CU%d" % _k] = ("sbuf", [128, 4 * _n], "uint16")
-    SCRATCH["DS%d" % _k] = ("sbuf", [128, 64 * _n], "bfloat16")
-    SCRATCH["DA%d" % _k] = ("sbuf", [128, 80 * _n], "bfloat16")
-    SCRATCH["KM%d" % _k] = ("sbuf", [128, _n], "float32")
-    SCRATCH["KI%d" % _k] = ("sbuf", [128, _n], "int32")
-    SCRATCH["MI%d" % _k] = ("sbuf", [128, _n], "int32")
-    SCRATCH["FI%d" % _k] = ("sbuf", [128, _n], "float32")
-    SCRATCH["OU%d" % _k] = ("sbuf", [128, _n], "uint16")
-    SCRATCH["DD%d" % _k] = ("sbuf", [128, _n], "float32")
-    SCRATCH["CM%d" % _k] = ("sbuf", [128, 4 * _n], "bfloat16")
+    for _b, _w, _d in (("CI", 4, "int32"), ("CU", 4, "uint16"), ("DS", 64, "bfloat16"), ("DA", 80, "bfloat16"), ("KM", 1, "float32"),
+                       ("KI", 1, "int32"), ("MI", 1, "int32"), ("OU", 1, "uint16"), ("E5", 1, "bfloat16"), ("EC", 4, "float32"),
+                       ("EM", 1, "float16")):
+        SCRATCH["%s%d" % (_b, _k)] = ("sbuf", [128, _w * ST[_k]], _d)
+    SCRATCH["PB%d" % _k] = ("sbuf", [128, ST[_k] + 2], "int32")
 for _k in range(RO):
     SCRATCH["SEND%d" % _k] = ("sbuf", [128, 16], "float32")
     SCRATCH["LAND%d" % _k] = ("sbuf", [128, 16], "float32")
 LOADS = ["RI", "BI", "X", "TI", "EI"]
-OUTS = ["yr", "ym", "ya"]
-SEMAPHORES = (["qV", "qS", "qP", "qG"] + ["ld" + n for n in LOADS] + ["st" + n for n in OUTS]
+STORES = 8
+SEMAPHORES = (["qV", "qS", "qP", "qG"] + ["ld" + n for n in LOADS] + ["st%d" % n for n in range(STORES)]
               + ["arr%d" % t for t in range(RO)] + ["snt%d" % t for t in range(RO)])
 PSUM = [n for n in SCRATCH if SCRATCH[n][0] == "psum"]
+WIDE = [n for n in SCRATCH if SCRATCH[n][2] in ("float32", "int32")]
 POOL = ["SB0", "SB1"]
+BANKS = [b for b in PSUM if b not in POOL]
 BW = 1024
+EN = "VSPGY"
+
+
+def cut(a, b, k):
+    ps = [a + (b - a) * q // k // 2 * 2 for q in range(k)] + [b]
+    return list(zip(ps, ps[1:]))
 
 
 def sl(T, r):
@@ -72,6 +89,13 @@ def build_ops():
     ops = []
     seen = {}
     cur = [""]
+    rnd = [0]
+    stores = [0]
+    NSP, TBP, NA, PEC, GC = PRM["NSP"], PRM["TBP"], PRM["NA"], PRM["PEC"], PRM["GC"]
+    FV, FS = PRM["FV"], PRM["FS"]
+
+    def on(name):
+        return cur[0] in PRM[name] or "%s@%d" % (cur[0], rnd[0]) in PRM[name]
 
     def O(engs, fn, R, W, **kw):
         op = dict(kw, engs=engs, fn=fn, R=list(R), W=list(W), preds={}, i=len(ops), grp=cur[0])
@@ -100,16 +124,19 @@ def build_ops():
         return op
 
     def vt(n, c):
-        return 55 + CY * max(64, n * c)
+        return FV + CY * max(64, n * c)
 
-    def tt(o, a, b, alu, cost=None):
+    def st(n):
+        return FS + CY * n
+
+    def tt(o, a, b, alu):
         n = o[2] - o[1]
-        if cost is None:
-            cost = 1 if (a[0] in PSUM or b[0] in PSUM) else 2
+        cost = 1 if (a[0] in PSUM or b[0] in PSUM) else 2
         return O({"V": vt(n, cost)}, lambda e, g, T, op: g.vector.tensor_tensor(sl(T, o), sl(T, a), sl(T, b), alu), [a, b], [o])
 
-    def tsc(o, a, s1, s2, op0, op1=None, cost=1, sreads=()):
+    def tsc(o, a, s1, s2, op0, op1=None):
         n = o[2] - o[1]
+        cost = 1 if (o[0] in WIDE or a[0] in WIDE) else 0.5
 
         def fn(e, g, T, op):
             v1 = sl(T, s1) if isinstance(s1, tuple) else s1
@@ -120,103 +147,90 @@ def build_ops():
         rd = [a] + [s for s in (s1, s2) if isinstance(s, tuple)]
         return O({"V": vt(n, cost)}, fn, rd, [o])
 
-    def copy(o, a, both=False):
-        n = o[2] - o[1]
-        engs = {"V": vt(n, 1)}
-        if both:
-            engs["S"] = 70 + CY * n
+    def copy(o, a):
+        return O({"V": vt(o[2] - o[1], 1)}, lambda e, g, T, op: g.vector.tensor_copy(sl(T, o), sl(T, a)), [a], [o])
 
-        def fn(e, g, T, op):
-            if e == "V":
-                return g.vector.tensor_copy(sl(T, o), sl(T, a))
-            return g.scalar.activation(sl(T, o), sl(T, a), F_.Copy)
-        return O(engs, fn, [a], [o])
-
-    def affine(o, a, mul, add):
+    def plus(o, a, add, step=1):
         n = o[2] - o[1]
 
         def fn(e, g, T, op):
+            src = T[a[0]][:, a[1]:a[2]:step]
             if e == "V":
-                if mul == 1.0:
-                    return g.vector.tensor_scalar(sl(T, o), sl(T, a), add, None, A_.add)
-                return g.vector.tensor_scalar(sl(T, o), sl(T, a), mul, add, A_.mult, A_.add)
-            return g.scalar.activation(sl(T, o), sl(T, a), F_.Copy, bias=add, scale=mul)
-        return O({"V": vt(n, 1), "S": 70 + CY * n}, fn, [a], [o])
+                return g.vector.tensor_scalar(sl(T, o), src, add, None, A_.add)
+            return g.scalar.activation(sl(T, o), src, F_.Copy, bias=add)
+        narrow = SCRATCH[o[0]][2] != "float32" or SCRATCH[a[0]][2] != "float32"
+        return O({"V": vt(n, 1)} if narrow else {"V": vt(n, 1), "S": st(n)}, fn, [a], [o])
+
+    def over(o, a, limit, scale=1.0, only=None):
+        n = o[2] - o[1]
+
+        def fn(e, g, T, op):
+            if e == "V":
+                return g.vector.tensor_scalar(sl(T, o), sl(T, a), limit, None, A_.is_gt)
+            return g.scalar.activation(sl(T, o), sl(T, a), F_.Sigmoid, bias=-limit * scale, scale=scale)
+        return O(only or {"V": vt(n, 1), "S": st(n)}, fn, [a], [o])
 
     def memset(o, v):
         return O({"V": vt(o[2] - o[1], 0.5)}, lambda e, g, T, op: g.vector.memset(sl(T, o), v), [], [o])
 
-    def gather(o, win, off, only=None):
-        n = o[2] - o[1]
-        engs = {"V": 50 + GC * CY * n, "S": 65 + GC * CY * n}
-        if only:
-            engs = {only: engs[only]}
+    def parts(off, *big):
+        k = off[2] - off[1]
+        for x, y in cut(0, k, -(-k // PRM["GW"])):
+            yield [(off[0], off[1] + x, off[1] + y)] + [(r[0], r[1] + 16 * x, r[1] + 16 * y) for r in big]
 
-        def fn(e, g, T, op):
-            src = sl(T, win).indirect(sl(T, off))
-            if e == "V":
-                return g.vector.tensor_copy(sl(T, o), src)
-            return g.scalar.activation(sl(T, o), src, F_.Copy)
-        return O(engs, fn, [win, off], [o])
+    def gather(o, win, off):
+        for off1, o1 in parts(off, o):
+            def fn(e, g, T, op, off1=off1, o1=o1):
+                src = sl(T, win).indirect(sl(T, off1))
+                if e == "V":
+                    return g.vector.tensor_copy(sl(T, o1), src)
+                return g.scalar.activation(sl(T, o1), src, F_.Copy)
+            n = o1[2] - o1[1]
+            O({"V": 50 + GC * CY * n, "S": 65 + GC * CY * n}, fn, [win, off1], [o1], first="V" if on("ONV") else "S")
 
     def gather_tt(o, win, off, b, alu):
-        n = o[2] - o[1]
-        return O({"V": 50 + GC * CY * n}, lambda e, g, T, op: g.vector.tensor_tensor(sl(T, o), sl(T, win).indirect(sl(T, off)), sl(T, b), alu),
-                 [win, off, b], [o])
+        for off1, o1, b1 in parts(off, o, b):
+            O({"V": 50 + GC * CY * (o1[2] - o1[1])}, lambda e, g, T, op, off1=off1, o1=o1, b1=b1: g.vector.tensor_tensor(
+                sl(T, o1), sl(T, win).indirect(sl(T, off1)), sl(T, b1), alu), [win, off1, b1], [o1])
 
-    def blocks(o, a, b):
+    def lin(sums):
+        def fn(e, g, T, op):
+            r = None
+            for o, terms in sums:
+                for j, (w, x) in enumerate(terms):
+                    r = g.tensor.matmul(sl(T, o), T[w][:], sl(T, x), j == 0, j == len(terms) - 1)
+            return r
+        ns = 30 + sum(PEC * max(64, o[2] - o[1]) * (4 if w in WIDE else 1) for o, terms in sums for w, x in terms)
+        rd = [x for o, terms in sums for w, x in terms] + [(w, 0, 128) for o, terms in sums for w, x in terms]
+        return O({"P": ns}, fn, rd, [o for o, terms in sums])
+
+    def diff(o, a, b, wp, wn, engs, read):
         tot = o[2] - o[1]
         w = -(-tot // ((tot + BW - 1) // BW))
         w = -(-w // 32) * 32
         for c in range(0, tot, w):
             m = min(w, tot - c)
-            yield [(x[0], x[1] + c, x[1] + c + m) for x in (o, a, b)] + [m]
+            o1, a1, b1 = [(x[0], x[1] + c, x[1] + c + m) for x in (o, a, b)]
 
-    def sub_op(a1, b1, m):
-        def sub(e, g, T, op):
-            r = None
-            for x in range(0, m, 512):
-                y = min(x + 512, m)
-                d = T[op["bank"]][:, x:y]
-                g.tensor.matmul(d, T.IP[:], T[a1[0]][:, a1[1] + x:a1[1] + y], True, False)
-                r = g.tensor.matmul(d, T.IN[:], T[b1[0]][:, b1[1] + x:b1[1] + y], False, True)
-            return r
-        return O({"P": 2 * PEC * max(64, m) + 30}, sub, [a1, b1, ("IP", 0, 128), ("IN", 0, 128)], [("POOL", 0, m)], alloc=True)
-
-    def signdiff(o, a, b):
-        absdiff(o, a, b, F_.Sign, -0.5)
-
-    def absdiff(o, a, b, func=F_.Abs, bias=0.0):
-        for o1, a1, b1, m in blocks(o, a, b):
-            q = sub_op(a1, b1, m)
-            r = O({"S": 70 + CY * m}, lambda e, g, T, op, o1=o1, m=m: g.scalar.activation(sl(T, o1), T[op["src"]["bank"]][:, 0:m], func, bias=bias),
+            def sub(e, g, T, op, a1=a1, b1=b1, m=m):
+                r = None
+                for x in range(0, m, 512):
+                    y = min(x + 512, m)
+                    d = T[op["bank"]][:, x:y]
+                    g.tensor.matmul(d, T[wp][:], T[a1[0]][:, a1[1] + x:a1[1] + y], True, False)
+                    r = g.tensor.matmul(d, T[wn][:], T[b1[0]][:, b1[1] + x:b1[1] + y], False, True)
+                return r
+            q = O({"P": 2 * PEC * max(64, m) + 30}, sub, [a1, b1, (wp, 0, 128), (wn, 0, 128)], [("POOL", 0, m)], alloc=True)
+            r = O(engs(m), lambda e, g, T, op, o1=o1, m=m: read(g, sl(T, o1), T[op["src"]["bank"]][:, 0:m]),
                   [("POOL", 0, m)], [o1], src=q)
             r["preds"][q["i"]] = 1
 
-    def cand_abs(o, win, off, b, ds):
-        tot = o[2] - o[1]
+    def absdiff(o, a, b, func=F_.Abs, bias=0.0):
+        diff(o, a, b, "IP", "IN", lambda m: {"S": st(m)}, lambda g, x, y: g.scalar.activation(x, y, func, bias=bias))
 
-        def fn(e, g, T, op):
-            src = sl(T, win).indirect(sl(T, off))
-            if e == "V":
-                return g.vector.tensor_tensor(sl(T, ds), src, sl(T, b), A_.subtract)
-            return g.scalar.activation(sl(T, ds), src, F_.Copy)
-        G = O({"V": 50 + GC * CY * tot, "S": 65 + GC * CY * tot}, fn, [win, off, b], [ds])
-        G["subs"], G["abss"] = [], []
-        for o1, a1, b1, m in blocks(o, ds, b):
-            c = o1[1] - o[1]
-            q = sub_op(a1, b1, m)
-
-            def ab(e, g, T, op, o1=o1, m=m):
-                if op.get("whole"):
-                    return g.scalar.activation(sl(T, o), sl(T, ds), F_.Abs)
-                return g.scalar.activation(sl(T, o1), T[op["src"]["bank"]][:, 0:m], F_.Abs)
-            r = O({"S": 70 + CY * m}, ab, [ds, ("POOL", 0, m)], [o if c == 0 else o1], src=q, wdur=70 + CY * tot)
-            r["preds"][q["i"]] = 1
-            G["subs"].append(q["i"])
-            G["abss"].append(r["i"])
-        for x in G["abss"][1:]:
-            ops[x]["preds"].pop(G["abss"][0], None)
+    def within(o, a, b):
+        diff(o, a, b, "EP", "EN", lambda m: {"V": vt(m, 1)},
+             lambda g, x, y: g.vector.tensor_scalar(x, y, BIG, BIG, A_.add, A_.is_equal))
 
     def stage_sum(o, a, tag=None):
         n = o[2] - o[1]
@@ -224,379 +238,534 @@ def build_ops():
         def fn(e, g, T, op):
             d = sl(T, o)
             r = None
-            for x in tag or []:
-                g.tensor.matmul(d, T.IP[:], sl(T, x), x is tag[0], False)
+            if tag:
+                g.tensor.matmul(d, T.IP[:], sl(T, tag), True, False)
             for p in range(16):
-                r = g.tensor.matmul(d, T.ZT[:, 15 - p:143 - p], T[a[0]][:, a[1] + p:a[2]:16], tag is None and p == 0, p == 15)
+                r = g.tensor.matmul(d, T.ZT[:, 15 - p:143 - p], T[a[0]][:, a[1] + p:a[2]:16], not tag and p == 0, p == 15)
             return r
-        rd = [a, ("ZT", 0, 144)] + (tag + [("IP", 0, 128)] if tag is not None else [])
-        O({"P": (16 + len(tag or [])) * PEC * max(64, n) + 30}, fn, rd, [o])
+        O({"P": (17 if tag else 16) * PEC * max(64, n) + 30}, fn, [a, ("ZT", 0, 144)] + ([tag, ("IP", 0, 128)] if tag else []), [o])
 
     def load(dst, src, w, ns):
         O({"Y": ns}, lambda e, g, T, op: g.sync.dma_start(T[dst][:], T[src][:]), [], [(dst, 0, w)], sem="ld" + dst)
-    load("RI", "riv", 256, 2000)
-    load("X", "flood", 4096, 7000)
-    load("BI", "bord", 256, 2500)
-    load("TI", "th", 1, 2500)
-    load("EI", "eps", 1, 2500)
 
-    def gop(fn, ns, R, W):
-        O({"G": ns}, fn, R, W)
+    def store(dst, r):
+        whole = r[2] - r[1] == SCRATCH[r[0]][1][1]
+        O({"Y": 1300.0 + 2 * (r[2] - r[1])}, lambda e, g, T, op: g.sync.dma_start(T[dst][:] if whole else T[dst][:, r[1]:r[2]], sl(T, r)),
+          [r], [], sem="st%d" % stores[0])
+        stores[0] += 1
+    load("RI", "riv", 256, 1500)
+    load("X", "flood", 4096, PRM["XLD"])
+    load("BI", "bord", 256, 2000)
+    load("TI", "th", 1, 2000)
+    load("EI", "eps", 1, 2000)
 
     def sel(buf, n, pattern, base, cm, cmp):
-        gop(lambda e, g, T, op: g.affine_select(T[buf][:], T[buf][:], pattern, cmp, 0.0, base, cm), 170 + 2 * CY * n, [(buf, 0, n)], [(buf, 0, n)])
+        O({"G": 170 + 2 * CY * n}, lambda e, g, T, op: g.affine_select(T[buf][:], T[buf][:], pattern, cmp, 0.0, base, cm),
+          [(buf, 0, n)], [(buf, 0, n)])
+
+    def iota(r, pattern, base, cm):
+        kw = {} if r[0] == "PI" else {"allow_small_or_imprecise_dtypes": True}
+        O({"G": 130 + 2 * CY * (r[2] - r[1])}, lambda e, g, T, op: g.iota(sl(T, r), pattern, base, cm, **kw), [], [r])
+    cur[0] = "0"
+    iota(("CMD", 0, 256), [[0, 16], [1, 16]], 0, 0)
+    over(("SEG", 0, 256), ("CMD", 0, 256), 0.5, 1024.0, {"S": st(256) + 1300})
+    cur[0] = ""
+    for b in DIAGS:
+        memset((b, 0, 128), DIAGS[b])
+        sel(b, 128, [[-1, 128]], 0, 1, A_.is_equal)
+    for b in CONST:
+        memset((b, 0, SM + 2), CONST[b])
     memset(("ZT", 0, 144), float(SC))
-    memset(("IP", 0, 128), 1.0)
-    sel("IP", 128, [[-1, 128]], 0, 1, A_.is_equal)
     sel("ZT", 144, [[0, 9], [1, 16]], -15, 0, A_.is_equal)
     sel("ZT", 144, [[-16, 9], [0, 16]], 0, 1, A_.is_ge)
     sel("ZT", 144, [[16, 9], [0, 16]], 15, -1, A_.is_ge)
-    gop(lambda e, g, T, op: g.iota(T.PI[:], [[0, 1]], 0, 1), 140, [], [("PI", 0, 1)])
-    gop(lambda e, g, T, op: g.iota(T.IOB[:], [[1, 128]], 0, 0, allow_small_or_imprecise_dtypes=True), 350, [], [("IOB", 0, 128)])
-    gop(lambda e, g, T, op: g.iota(T.CMD[:], [[0, 16], [1, 16]], 0, 0, allow_small_or_imprecise_dtypes=True), 560, [], [("CMD", 0, 256)])
-    gop(lambda e, g, T, op: g.iota(T.IK[:], [[1, 16]], 256, 0, allow_small_or_imprecise_dtypes=True), 160, [], [("IK", 0, 16)])
-    tsc(("IN", 0, 128), ("IP", 0, 128), -1.0, None, A_.mult)
+    iota(("PI", 0, 1), [[0, 1]], 0, 1)
+    iota(("TF", 0, 5 * SM), [[1, 5 * SM]], 0, 0)
+    copy(("TG", 0, 5 * SM), ("TF", 0, 5 * SM))
+    iota(("IK", 0, 16), [[1, 16]], 256, 0)
+    for k in range(NCH):
+        for m in range(5):
+            r = ("DA%d" % k, 16 * (ST[k] * m + BNDS[0][k + 1] - BNDS[0][k]), 16 * ST[k] * (m + 1))
+            if r[1] < r[2]:
+                iota(r, [[0, r[2] - r[1]]], 0, 0)
     tsc(("PI", 0, 1), ("PI", 0, 1), 15, None, A_.bitwise_and)
     copy(("PF", 0, 1), ("PI", 0, 1))
     tsc(("DIAG", 0, 256), ("CMD", 0, 256), ("PF", 0, 1), None, A_.is_equal)
-    tsc(("SEG", 0, 256), ("CMD", 0, 256), 0.5, None, A_.is_gt)
-    memset(("BIGC", 0, 256), 1.0e7)
-    memset(("NW", 4080, 4096), 0.0)
-    memset(("GR", 4096, 4112), 0.0)
-    memset(("YR", 264, 272), 0.0)
-    memset(("YM", 256, 272), 0.0)
-    memset(("RP", 264, 296), -4096.0)
-    memset(("AC", 0, 1), 0.0)
-    for k in range(NCH):
-        n = BND[k + 1] - BND[k]
-        for m in range(1, 5):
-            memset(("CM%d" % k, (m - 1) * n, m * n), float(m * n))
+    for r in (("ZE", 0, 256), ("M0", 240, 256), ("MS", 0, 1), ("NW", 4080, 4096), ("GR", 4096, 4112)):
+        memset(r, 0.0)
+    copy(("YR", 264, 272), ("ZE", 0, 8))
+    copy(("YM", 256, 264), ("ZE", 0, 8))
 
     XWIN = ("X", 0, 4096)
-    TB = TBP
-    NT = len(TB) - 1
 
-    def first_names(ta, tb):
-        tsc(("RU", ta, tb), ("RI", ta, tb), 0, None, A_.add)
-        copy(("RN", ta, tb), ("RI", ta, tb))
+    def yr(a, b):
+        return ("YR", 8 + a, 8 + b)
 
-    def names_side(t, ta, tb, kind):
-        if kind == "R":
-            gather(("GR", 16 * ta, 16 * tb), XWIN, ("RU", ta, tb))
-            affine(("NB", ta, tb), ("RN", ta, tb), 1.0, 32.0)
-            affine(("YR", 8 + ta, 8 + tb), ("RN", ta, tb), 1.0, -2912.0)
-            if ta == 0:
-                affine(("YR", 7, 8), ("RN", 0, 1), 1.0, -2912.0)
-            affine(("NB", 256 + ta, 256 + tb), ("RN", ta, tb), 128.0, 2912.0 + 77.0 * t)
-        else:
-            affine(("YM", ta, tb), ("MN", ta, tb), 1.0, -2912.0)
-            gather(("GM", 16 * ta, 16 * tb), XWIN, ("MU", ta, tb))
+    def yp(a, b):
+        return ("YP", 8 + a, 8 + b)
+
+    def choice(o, mask, d, base, names=None):
+        tt(d, d, mask, A_.mult)
+        tt(o, d, base, A_.add)
+        if names:
+            tsc(names, o, YO, None, A_.add)
 
     def accretion(ta, tb, last):
-        absdiff(("A3", 16 * ta, 16 * tb), ("GR", 16 * ta, 16 * tb), ("GM", 16 * ta, 16 * tb))
-        tsc(("I3", 16 * ta, 16 * tb), ("A3", 16 * ta, 16 * tb), ("EPF", 0, 1), None, A_.is_le, cost=0.5)
-        c = ("CB", ta, tb)
-        stage_sum(c, ("I3", 16 * ta, 16 * tb))
-        mn = ("MN", ta, tb)
-        tt(("DM", ta, tb), ("RN", ta, tb), mn, A_.subtract)
-        tsc(c, c, 8.5 * SC, None, A_.is_gt)
-        tt(c, c, ("DM", ta, tb), A_.mult)
-        tt(mn, c, mn, A_.add)
-        if not last:
-            copy(("MU", ta, tb), mn)
+        gr, gm, a3, i3 = [(b, 16 * ta, 16 * tb) for b in ("GR", "GM", "A3", "I3")]
+        if on("ONS"):
+            absdiff(a3, gr, gm)
+            tsc(i3, a3, ("EPF", 0, 1), None, A_.is_le)
+        else:
+            within(i3, gr, gm)
+        stage_sum(("NB", ta, tb), i3)
+        dm, ma = ("NB", 256 + ta, 256 + tb), ("MA", ta, tb)
+        lin([(dm, [("IP", yr(ta, tb)), ("IN", ("YM", ta, tb))])])
+        over(ma, ("NB", ta, tb), 8.5 * SC)
+        if last:
+            choice(("OM", ta, tb), ma, dm, ("MR", ta, tb))
+            store("ym", ("OM", ta, tb))
+        else:
+            choice(("YM", ta, tb), ma, dm, ("YM", ta, tb), ("MU", ta, tb))
 
-    def cand_lists(k, half):
-        a, b = BND[k], BND[k + 1]
+    def lists(k, t, a, b):
         n = b - a
-        ci = "CI%d" % k
-        lo, hi = (0, 2 * n) if half == 0 else (2 * n, 4 * n)
-        other = [("YR", 7 + a, 7 + b), ("YR", 9 + a, 9 + b)] if half == 0 else [("YM", a, b), ("YM", a + 1, b + 1)]
-        for q in range(2):
-            tt((ci, lo + q * n, lo + q * n + n), ("NB", a, b), other[q], A_.mult)
-        tsc((ci, lo, hi), (ci, lo, hi), 5, None, A_.arith_shift_right)
-        for q in range(2):
-            r = (ci, lo + q * n, lo + q * n + n)
-            tt(r, ("NB", 256 + a, 256 + b), r, A_.add)
-        tsc((ci, lo, hi), (ci, lo, hi), 4095, None, A_.bitwise_and)
-        copy(("CU%d" % k, lo, hi), (ci, lo, hi))
+        ci, kb, pb = "CI%d" % k, "KB%d" % k, "PB%d" % k
+        c = [("IP", ("K%d" % t, 0, n))] if t else []
+        cur[0] = "L%d0" % k
+        lin([((kb, 4 * n, 5 * n + 1), [("IP", yr(a - 1, b)), ("IP", ("KX", 0, n + 1))]),
+             ((kb, n, 2 * n), [("IA", yr(a - 1, b - 1)), ("IB", yr(a, b))] + c),
+             ((kb, 2 * n, 3 * n), [("IW", yr(a, b))] + c), ((kb, 3 * n, 4 * n), [("IW", yr(a, b))] + c)])
+        for half in range(2):
+            cur[0] = "L%d%d" % (k, half)
+            lo, hi = 2 * n * half, 2 * n * half + 2 * n
+            if half == 0:
+                tt((pb, 0, n + 1), (kb, 4 * n, 5 * n + 1), yr(a, b + 1), A_.mult)
+                for q in range(2):
+                    tt((ci, q * n, q * n + n), (kb, n + q * n, 2 * n + q * n), (pb, q, q + n), A_.add)
+            else:
+                for q in range(2):
+                    tt((ci, lo + q * n, lo + q * n + n), (kb, 4 * n + 1, 5 * n + 1), ("YM", a + q, b + q), A_.mult)
+                tt((ci, lo, hi), (kb, lo, hi), (ci, lo, hi), A_.add)
+            tsc((ci, lo, hi), (ci, lo, hi), 5, 4095, A_.arith_shift_right, A_.bitwise_and)
+            copy(("CU%d" % k, lo, hi), (ci, lo, hi))
 
-    def kreg(k, m):
-        n = BND[k + 1] - BND[k]
-        if m == 4:
-            return ("CB", 256 + BND[k], 256 + BND[k] + n)
-        return ("KB%d" % (k % 2), m * n, m * n + n)
-
-    def key(k, m):
-        n = BND[k + 1] - BND[k]
-        stage_sum(kreg(k, m), ("DA%d" % k, 16 * n * m, 16 * n * (m + 1)),
-                  [("IOB", 0, n)] + ([("CM%d" % k, (m - 1) * n, m * n)] if m else []))
-
-    def cand_heights(k, m):
-        a, b = BND[k], BND[k + 1]
+    def keys(k, a, b):
         n = b - a
         nxt = ("GR", 16 * a + 16, 16 * b + 16)
-        da = ("DA%d" % k, 16 * n * m, 16 * n * (m + 1))
-        if m < 4:
-            ds = ("DS%d" % k, 16 * n * m, 16 * n * (m + 1))
-            cand_abs(da, XWIN, ("CU%d" % k, m * n, m * n + n), nxt, ds)
-        else:
-            absdiff(da, ("GM", 16 * a, 16 * b), nxt)
-        key(k, m)
+        for m in (4, 0, 1, 2, 3):
+            cur[0] = "C%d%d" % (k, m)
+            da = ("DA%d" % k, 16 * ST[k] * m, 16 * (ST[k] * m + n))
+            ds, off = ("DS%d" % k, 16 * n * m, 16 * n * (m + 1)), ("CU%d" % k, m * n, m * n + n)
+            if m == 4:
+                absdiff(da, ("GM", 16 * a, 16 * b), nxt)
+            elif on("ONS"):
+                gather(ds, XWIN, off)
+                absdiff(da, ds, nxt)
+            else:
+                gather_tt(ds, XWIN, off, nxt, A_.subtract)
+                for _, o1, d1 in parts(off, da, ds):
+                    O({"S": st(o1[2] - o1[1])}, lambda e, g, T, op, o1=o1, d1=d1: g.scalar.activation(sl(T, o1), sl(T, d1), F_.Abs),
+                      [d1], [o1])
+            stage_sum(("KB%d" % k, m * n, m * n + n), da, ("TG", m * ST[k], m * ST[k] + n))
 
-    def choose(k):
-        a, b = BND[k], BND[k + 1]
+    def choose(k, a, b):
         n = b - a
-        kb = "KB%d" % (k % 2)
+        kb, ec = "KB%d" % k, "EC%d" % k
+        key = [(kb, m * n, m * n + n) for m in range(5)]
         cur[0] = "K%d" % k
         km, ki = ("KM%d" % k, 0, n), ("KI%d" % k, 0, n)
-        order = [4, 0, 1, 2, 3]
-        copy(km, kreg(k, order[0]), both=True)
-        for m in order[1:]:
-            tt(ki if m == order[-1] else km, kreg(k, m), km, A_.min)
+        plus(km, key[0], 0.0)
+        for m in (1, 4, 2, 3):
+            tt(ki if m == 3 else km, key[m], km, A_.min)
         tsc(("MI%d" % k, 0, n), ki, SC - 1, None, A_.bitwise_and)
         tsc(("OU%d" % k, 0, n), ("MI%d" % k, 0, n), 16.0, ("PF", 0, 1), A_.mult, A_.add)
-        ps = [a + n * q // NSP[k] for q in range(NSP[k] + 1)]
-        cur[0] = "E%d" % k
-        for x, y in zip(ps, ps[1:]):
-            nr, win, off = ("NR", 16 * x, 16 * y), ("DA%d" % k, 0, 80 * n), ("OU%d" % k, x - a, y - a)
-            cur[0] = "E%d%d" % (k, ps.index(x))
-            if (k, ps.index(x)) in NEARS:
-                gather(nr, win, off, "S")
-                signdiff(nr, ("NW", 16 * x, 16 * y), nr)
+        ps = cut(a, b, NSP[rnd[0]][k])
+        for q, (x, y) in enumerate(ps):
+            nr, win, off = ("NR", 16 * x, 16 * y), ("DA%d" % k, 0, 80 * ST[k]), ("OU%d" % k, x - a, y - a)
+            cur[0] = "E%d%d" % (k, q)
+            if on("ONS"):
+                gather(nr, win, off)
+                absdiff(nr, ("NW", 16 * x, 16 * y), nr, F_.Sign, -0.5)
             else:
                 gather_tt(nr, win, off, ("NW", 16 * x, 16 * y), A_.is_lt)
-            stage_sum(("CB", x, y), nr)
-        dd = ("DD%d" % k, 0, n)
+            stage_sum(("NB", x, y), nr)
+            over(("MK", x, y), ("NB", x, y), (1.0 if on("ONS") else 8.5) * SC)
         cur[0] = "D%d" % k
-        for m in range(5):
-            r = kreg(k, m)
-            tt(r, r, ki, A_.is_equal)
-        tt((kb, 0, 4 * n), (kb, 0, 4 * n), ("CI%d" % k, 0, 4 * n), A_.mult)
-        r = kreg(k, 4)
-        tt(r, r, ("MN", a, b), A_.mult)
-        tt(dd, (kb, 0, n), ("RN", a, b), A_.subtract)
-        for m in range(1, 5):
-            tt(dd, kreg(k, m), dd, A_.add)
-        for x, y in zip(ps, ps[1:]):
-            cur[0] = "P%d%d" % (k, ps.index(x))
-            c = ("CB", x, y)
-            tsc(c, c, (1.0 if (k, ps.index(x)) in NEARS else 8.5) * SC, None, A_.is_gt)
-            tt(c, c, (dd[0], x - a, y - a), A_.mult)
-            rp = ("RP", 8 + x, 8 + y)
-            tt(rp, c, ("RN", x, y), A_.add)
-            copy(("PU", x, y), rp)
+        for m in range(4):
+            tt(key[m], key[m], ki, A_.is_equal)
+        tt((ec, 0, 4 * n), (kb, 0, 4 * n), ("CI%d" % k, 0, 4 * n), A_.mult)
+        e5, em = ("E5%d" % k, 0, n), ("EM%d" % k, 0, n)
+        tt(e5, key[4], ki, A_.is_equal)
+        lin([(key[4], [("IP", ("YM", a, b))])])
+        tt(em, key[4], e5, A_.mult)
+        lin([(key[0], [("IN", yr(a, b)), ("IN", ("KY", 0, n)), ("IY", e5), ("IP", em)]
+              + [("IF", (ec, m * n, m * n + n)) for m in range(4)])])
+        for q, (x, y) in enumerate(ps):
+            cur[0] = "P%d%d" % (k, q)
+            choice(yp(x, y), ("MK", x, y), (kb, x - a, y - a), yr(x, y), ("PU", x, y))
             gather(("GP", 16 * x, 16 * y), XWIN, ("PU", x, y))
 
     def necks(na, nb, last):
-        absdiff(("AB", 16 * na, 16 * nb), ("GP", 16 * na, 16 * nb), ("GP", 16 * na + 256, 16 * nb + 256))
-        stage_sum(("NB", na, nb), ("AB", 16 * na, 16 * nb))
-        tt(("DDN", na, nb), ("RP", 24 + na, 24 + nb), ("RP", 8 + na, 8 + nb), A_.subtract)
-        hi = 255 if last else nb
-        n = hi - na
-        ini = ("RM", na - 1, na) if na else 1.0e7
-        rd = [("NB", na, hi), ("BIGC", na, hi)] + ([ini] if na else [])
-        O({"V": vt(n, 1)}, lambda e, g, T, op: g.vector.tensor_tensor_scan(T.RM[:, na:hi], T.NB[:, na:hi], T.BIGC[:, na:hi],
-            sl(T, ini) if na else 1.0e7, A_.min, A_.min), rd, [("RM", na, hi)])
-        tsc(("NB", 257 + na, 257 + hi), ("RM", na, hi), ("THR", 0, 1), None, A_.is_lt)
+        ab = ("AB", 16 * na, 16 * nb)
+        absdiff(ab, ("GP", 16 * na, 16 * nb), ("GP", 16 * na + 256, 16 * nb + 256))
+        stage_sum(("NB", na, nb), ab)
 
-    def shift(ta, tb, last):
-        m = ("NB", ta, tb)
-        tt(m, ("NB", 256 + ta, 256 + tb), ("DDN", ta, tb), A_.mult)
-        tt(("RN", ta, tb), m, ("RP", 8 + ta, 8 + tb), A_.add)
-        copy(("RU", ta, tb), ("RN", ta, tb))
+        def under(e, g, T, op):
+            if e == "V":
+                return g.vector.tensor_scalar(T.M0[:, na:nb], T.NB[:, na:nb], T.THR[:], None, A_.is_lt)
+            return g.scalar.activation(T.M0[:, na:nb], T.NB[:, na:nb], F_.Sign, bias=T.THR[:], scale=-1.0)
+        O({"V": vt(nb - na, 1), "S": st(nb - na)}, under, [("NB", na, nb), ("THR", 0, 1)], [("M0", na, nb)])
+        hi = 255 if last else nb
+        O({"V": vt(hi - na, 0.5)}, lambda e, g, T, op: g.vector.tensor_tensor_scan(
+            T.MS[:, na + 1:hi + 1], T.M0[:, na:hi], T.ZE[:, na:hi], T.MS[:, na:na + 1], A_.max, A_.max),
+          [("M0", na, hi), ("ZE", na, hi), ("MS", na, na + 1)], [("MS", na + 1, hi + 1)])
+
+    def shift(ta, tb):
+        d = ("NB", 256 + ta, 256 + tb)
+        lin([(d, [("IF", yp(ta + 16, tb + 16)), ("NF", yp(ta, tb))])])
+        choice(yr(ta, tb), ("MS", ta, tb), d, yp(ta, tb), ("RU", ta, tb))
 
     def loops(t):
-        O({"V": vt(256, 1)}, lambda e, g, T, op: g.vector.tensor_reduce(T.CNT[:], T.NB[:, 256:512], AxisListType.X, A_.add),
-          [("NB", 256, 512)], [("CNT", 0, 1)])
+        h = ("MS", 255, 256)
+        plus(yp(256, 272), yp(240, 256), 8192.0)
+
+        def count(e, g, T, op):
+            if e == "V":
+                return g.vector.tensor_reduce(T.CNT[:], T.MS[:], AxisListType.X, A_.add)
+            return g.scalar.activation(T.JK[:], T.MS[:], F_.Copy, accum_out=T.CNT[:])
+        O({"V": vt(256, 1), "S": st(256) + 20}, count, [("MS", 0, 256)], [("CNT", 0, 1), ("JK", 0, 256)])
         tsc(("OFF", 0, 16), ("IK", 0, 16), ("CNT", 0, 1), None, A_.subtract)
-        gather_tt(("LG", 0, 256), ("RP", 8, 296), ("OFF", 0, 16), ("DIAG", 0, 256), A_.mult)
+        gather_tt(("LG", 0, 256), yp(0, 272), ("OFF", 0, 16), ("DIAG", 0, 256), A_.mult)
         O({"V": vt(256, 1)}, lambda e, g, T, op: g.vector.tensor_tensor_scan(T.LS[:], T.SEG[:], T.LG[:], 0.0, A_.mult, A_.add),
           [("SEG", 0, 256), ("LG", 0, 256)], [("LS", 0, 256)])
         s = "SEND%d" % t
-        O({"V": vt(16, 1)}, lambda e, g, T, op: g.vector.tensor_scalar(T[s][:], T.LS[:, 15:256:16], 4096.0, None, A_.add),
-          [("LS", 0, 256)], [(s, 0, 16)])
-        snd = O({"G": 1500}, None, [(s, 0, 16)], [], send=t)
-        tsc(("AC", 0, 1), ("NB", 511, 512), ("AC", 0, 1), None, A_.add)
-        tsc(("THR", 0, 1), ("NB", 511, 512), 16.0 * SC, ("THR", 0, 1), A_.mult, A_.add)
+        O({"V": vt(16, 1)}, lambda e, g, T, op: g.vector.tensor_scalar(T[s][:], T.LS[:, 15:256:16], YO + 4096.0, sl(T, h), A_.add, A_.mult),
+          [("LS", 0, 256), h], [(s, 0, 16)])
+        snd = O({"G": PRM["SND"]}, None, [(s, 0, 16)], [], send=t, lag=PRM["SND"])
+        plus(("OWN", 0, 16), ("LS", 15, 256), YO, 16)
+        tsc(("THR", 0, 1), h, 16.0 * SC, ("THR", 0, 1), A_.mult, A_.add)
         return snd
 
-    def loop_in(t, snd, last):
-        q = O({"V": vt(16, 2)}, lambda e, g, T, op: g.vector.tensor_tensor(T.LPI[:], T["LAND%d" % t][:], T.LS[:, 15:256:16], A_.max),
-              [("LS", 0, 256)], [("LPI", 0, 16)], ext="arr%d" % t)
+    def loop_in(t, snd):
+        q = O({"V": vt(16, 2)}, lambda e, g, T, op: g.vector.tensor_tensor(T.LPI[:], T["LAND%d" % t][:], T.OWN[:], A_.max),
+              [("OWN", 0, 16)], [("LPI", 0, 16)], ext="arr%d" % t)
         q["preds"][snd["i"]] = 1
         tsc(("LPI", 0, 16), ("LPI", 0, 16), 4095, None, A_.bitwise_and)
-        tt(("LD", 0, 16), ("LPI", 0, 16), ("RP", 248, 264), A_.subtract)
-        tt(("LD", 0, 16), ("NB", 496, 512), ("LD", 0, 16), A_.mult)
-        tt(("RN", 240, 256), ("LD", 0, 16), ("RP", 248, 264), A_.add)
-        copy(("RU", 240, 256), ("RN", 240, 256))
+        copy(("RU", 240, 256), ("LPI", 0, 16))
+        tsc(yr(240, 256), ("LPI", 0, 16), -YO, None, A_.add)
 
-    for i in range(NT):
-        first_names(TB[i], TB[i + 1])
-    copy(("MN", 0, 256), ("BI", 0, 256))
+    copy(("RU", 0, 256), ("RI", 0, 256))
+    tsc(yr(0, 256), ("RI", 0, 256), -YO, None, A_.add)
     copy(("MU", 0, 256), ("BI", 0, 256))
+    tsc(("YM", 0, 256), ("BI", 0, 256), -YO, None, A_.add)
+    tsc(("TH0", 0, 1), ("TI", 0, 1), float(SC), None, A_.mult)
+    copy(("THR", 0, 1), ("TH0", 0, 1))
     copy(("EPF", 0, 1), ("EI", 0, 1))
-    tsc(("THR", 0, 1), ("TI", 0, 1), float(SC), None, A_.mult)
-    for t in range(RO):
-        for i in range(NT):
-            ta, tb = TB[i], TB[i + 1]
-            cur[0] = "R%d" % i
-            names_side(t, ta, tb, "R")
-            if i >= NA - 1 and i < NT - 1:
-                continue
-            if i == NT - 1:
-                ta = TB[NA - 1]
-            if t:
-                cur[0] = "A%d" % i
-                accretion(ta, tb, False)
-            cur[0] = "M%d" % i
-            names_side(t, ta, tb, "M")
-        for k in range(NCH):
-            a, b = BND[k], BND[k + 1]
-            cur[0] = "L%d0" % k
-            cand_lists(k, 0)
-            cur[0] = "L%d1" % k
-            cand_lists(k, 1)
-            hi = min(16 * b, 4080)
-            for m in (4, 0, 1, 2, 3):
-                cur[0] = "C%d%d" % (k, m)
-                cand_heights(k, m)
-            cur[0] = "N%d" % k
-            absdiff(("NW", 16 * a, hi), ("GR", 16 * a, hi), ("GR", 16 * a + 16, hi + 16))
-            choose(k)
-            for q in range(NSP[k]):
-                x, y = a + (b - a) * q // NSP[k], a + (b - a) * (q + 1) // NSP[k]
-                cur[0] = "Q%d%d" % (k, q)
-                if y == 256:
-                    memset(("NB", 240, 255), 1.0e7)
-                    memset(("NB", 256, 257), 0.0)
-                necks(x - 16 if x else 0, y - 16, y == 256)
-        cur[0] = "O"
-        snd = loops(t)
-        for i in range(NT - 1):
-            cur[0] = "S%d" % i
-            shift(TB[i], TB[i + 1], t == RO - 1)
-        cur[0] = "I"
-        loop_in(t, snd, t == RO - 1)
-    for i in range(NT):
-        ta, tb = TB[i], TB[i + 1]
-        cur[0] = "FR%d" % i
-        gather(("GR", 16 * ta, 16 * tb), XWIN, ("RU", ta, tb))
-        cur[0] = "FA%d" % i
-        accretion(ta, tb, True)
+    tsc(("ES", 0, 1), ("EI", 0, 1), 2.0, 1.0, A_.mult, A_.add)
+    O({"V": 250}, lambda e, g, T, op: g.vector.reciprocal(T.ES[:], T.ES[:]), [("ES", 0, 1)], [("ES", 0, 1)])
+    tsc(("EP", 0, 128), ("IP", 0, 128), ("ES", 0, 1), None, A_.mult)
+    tsc(("EN", 0, 128), ("IN", 0, 128), ("ES", 0, 1), None, A_.mult)
 
-    def store(dst, src, w):
-        O({"Y": 2000}, lambda e, g, T, op: g.sync.dma_start(T[dst][:], T[src][:, 0:w]), [(src, 0, w)], [], sem="st" + dst)
-    store("ya", "AC", 1)
-    store("yr", "RN", 256)
-    store("ym", "MN", 256)
+    def pieces(t):
+        b = [0] + [x + 2 for x in BNDS[t][1:-1]] + [240]
+        return [("%d%d" % (k, q), x, y) for k in range(NCH) for q, (x, y) in enumerate(cut(b[k], b[k + 1], TBP[t][k]))] + [
+            ("%dL" % (NCH - 1), 240, 256)]
+
+    for t in range(RO + 1):
+        last = t == RO
+        rnd[0] = t
+        pre = "F" if last else ""
+        if last:
+            cur[0] = "F"
+            plus(("MR", 0, 256), ("YM", 0, 256), YO)
+            tsc(("AC", 0, 1), ("THR", 0, 1), ("TH0", 0, 1), 1.0 / (16 * SC), A_.subtract, A_.mult)
+            store("ya", ("AC", 0, 1))
+            for x, y in ((0, 240), (240, 256)):
+                plus(("OR", x, y), yr(x, y), YO)
+                store("yr", ("OR", x, y))
+        for k in range(NCH):
+            ps = pieces(t)
+            for j, (i, ta, tb) in enumerate(ps):
+                if i[0] != str(k):
+                    continue
+                cur[0] = pre + "R" + i
+                gather(("GR", 16 * ta, 16 * tb), XWIN, ("RU", ta, tb))
+                if j == 0 and not last:
+                    plus(yr(-1, 0), yr(0, 1), 0.0)
+                if not (NA or last):
+                    if tb == 240:
+                        continue
+                    if tb == 256:
+                        ta = ps[j - 1][1]
+                if t:
+                    cur[0] = pre + "A" + i
+                    accretion(ta, tb, last)
+                if not last:
+                    cur[0] = "M" + i
+                    gather(("GM", 16 * ta, 16 * tb), XWIN, ("MU", ta, tb))
+            if last:
+                continue
+            a, b = BNDS[t][k:k + 2]
+            lists(k, t, a, b)
+            keys(k, a, b)
+            cur[0] = "N%d" % k
+            hi = min(16 * b, 4080)
+            absdiff(("NW", 16 * a, hi), ("GR", 16 * a, hi), ("GR", 16 * a + 16, hi + 16))
+            choose(k, a, b)
+            for q, (x, y) in enumerate(cut(a, b, NSP[t][k])):
+                cur[0] = "Q%d%d" % (k, q)
+                necks(x - 16 if x else 0, y - 16, y == 256)
+            if b == 256:
+                cur[0] = "O"
+                snd = loops(t)
+            for i, ta, tb in pieces(t + 1)[:-1]:
+                if a < tb + 16 <= b:
+                    cur[0] = "S" + i
+                    shift(ta, tb)
+        if not last:
+            cur[0] = "I"
+            loop_in(t, snd)
+    for op in ops:
+        op["bk"] = sorted({BANKS.index(r[0]) for r in op["R"] + op["W"] if r[0] in BANKS})
     return ops
+
+
+def place(ops, before, after, mate, key):
+    LAT, WIN, FILL, HOLD, BOOST = PRM["LAT"], PRM["WIN"], PRM["FILL"], PRM["HOLD"], PRM["BOOST"]
+    n = len(ops)
+    engs = [{op["first"]: op["engs"][op["first"]]} if "first" in op else op["engs"] for op in ops]
+    start, fin, eng, bank = [0.0] * n, [0.0] * n, [None] * n, {}
+    left = [len(x) for x in before]
+    head = {b: a for a, b in mate.items()}
+    key = list(key)
+    free = {e: 0.0 for e in EN}
+    used = [{} for b in BANKS]
+    pool = {b: 0.0 for b in POOL}
+    ready = {i: 0.0 for i in range(n) if left[i] == 0}
+    while ready:
+        found = []
+        opts = [(x, b) for b, x in pool.items() if x is not None]
+        px = min(opts) if opts else None
+        for i, t in ready.items():
+            if i in mate:
+                if px is None:
+                    continue
+                j = mate[i]
+                e = min(engs[j])
+                x = free[e] - HOLD - min(engs[i].values()) + (2000.0 if left[j] > 1 else 0.0)
+                for q in ready:
+                    if key[q] < key[j] - BOOST and e in engs[q] and q not in mate:
+                        x += engs[q][e]
+                t = max(t, px[0], x)
+            c = None
+            for e, d in engs[i].items():
+                s = max(free[e], t)
+                for b in ops[i]["bk"]:
+                    for f, x in used[b].items():
+                        if f != e and x > s:
+                            s = x
+                if c is None or s + d < c[3]:
+                    c = (s, e, i, s + d)
+            found.append(c)
+        s0, e0 = min(found)[:2]
+        mine = [x for x in found if x[1] == e0 and x[0] <= s0 + (WIN if e0 in "VSP" else 0.0)]
+        best = min(mine, key=lambda x: key[x[2]])
+        short = [x for x in mine if x[3] <= best[0] + FILL and x[0] < best[0]]
+        if short:
+            best = min(short, key=lambda x: key[x[2]])
+        s, e, i, f = best
+        del ready[i]
+        start[i], fin[i], eng[i] = s, f, e
+        free[e] = s if e == "Y" else f
+        if i in mate:
+            bank[i] = bank[mate[i]] = px[1]
+            pool[px[1]] = None
+            key[mate[i]] -= BOOST
+        if i in head:
+            pool[bank[i]] = f + LAT
+        for b in ops[i]["bk"]:
+            used[b][e] = f + LAT
+        for q in after[i]:
+            left[q] -= 1
+            if left[q] == 0:
+                ready[q] = max(fin[p] + lag for p, lag in before[q])
+    return start, fin, eng
+
+
+STEP = 48
+
+
+def run(perm, eng, dur, D, old=None, a=0):
+    pre, bks, role, src, LAT = D
+    n = len(perm)
+    if old is None:
+        fin, why, slot, marks, c = [0.0] * n, [-1] * n, [0] * n, [], 0
+        st, so = [0.0] * 19, [-1] * 19
+    else:
+        c = a // STEP
+        fin, why, slot, marks = old[0][:], old[1][:], old[2][:], old[3][:c]
+        st, so = old[3][c][0][:], old[3][c][1][:]
+    for c in range(c * STEP, n, STEP):
+        marks.append((st[:], so[:]))
+        for i in perm[c:c + STEP]:
+            e = eng[i]
+            t = st[e]
+            w = so[e]
+            for p, lag in pre[i]:
+                x = fin[p] + lag
+                if x > t:
+                    t = x
+                    w = p
+            r = role[i]
+            if r == 1:
+                a, b = st[17], st[18]
+                if a < 0 and b < 0:
+                    return None
+                s = 18 if a < 0 or 0 <= b < a else 17
+                if st[s] > t:
+                    t = st[s]
+                    w = so[s]
+                st[s] = -1.0
+                slot[i] = s
+            bk = bks[i]
+            for b in bk:
+                for f in (b, b + 1, b + 2):
+                    if st[f] > t and f != b + e:
+                        t = st[f]
+                        w = so[f]
+            f = t + dur[i]
+            fin[i] = f
+            why[i] = w
+            if e != 4:
+                st[e] = f
+                so[e] = i
+            else:
+                st[e] = t
+            if r == 2:
+                s = slot[i] = slot[src[i]]
+                st[s] = f + LAT
+                so[s] = i
+            for b in bk:
+                st[b + e] = f + LAT
+                so[b + e] = i
+    return fin, why, slot, marks
+
+
+def anneal(ops, D, perm, eng, rng):
+    n = len(ops)
+    moves = PRM["MOVES"]
+    pset = [set(op["preds"]) for op in ops]
+    dur = [ops[i]["engs"][EN[eng[i]]] for i in range(n)]
+    cur = run(perm, eng, dur, D)
+    val = max(cur[0])
+    best = (val, list(perm), list(eng))
+    arcs = None
+    kept = 0
+    for it, (r0, r1, r2, r3) in enumerate(rng.rand(moves, 4).tolist()):
+        temp = PRM["T0"] * (PRM["T1"] / PRM["T0"]) ** (it / moves)
+        if arcs is None:
+            fin, why = cur[0], cur[1]
+            v = fin.index(val)
+            arcs, two = [], []
+            while why[v] >= 0:
+                if len(ops[v]["engs"]) > 1:
+                    two.append(v)
+                if why[v] not in pset[v]:
+                    arcs.append((why[v], v))
+                v = why[v]
+            pos = [0] * n
+            for j, x in enumerate(perm):
+                pos[x] = j
+        if r0 < 0.1 and two:
+            v = two[int(r1 * len(two))]
+            undo = (v, eng[v], dur[v])
+            eng[v] = 1 - eng[v]
+            dur[v] = ops[v]["engs"][EN[eng[v]]]
+            new, a = perm, pos[v]
+        else:
+            undo = None
+            u, v = arcs[int(r1 * len(arcs))]
+            a, b = pos[u], pos[v]
+            seg = perm[a:b + 1]
+            if r2 < 0.5:
+                mov, need = {v}, set(pset[v])
+                for y in reversed(seg[:-1]):
+                    if y in need:
+                        mov.add(y)
+                        need |= pset[y]
+                if u in mov:
+                    continue
+                new = perm[:a] + [y for y in seg if y in mov] + [y for y in seg if y not in mov] + perm[b + 1:]
+            else:
+                mov = {u}
+                for y in seg[1:]:
+                    if pset[y] & mov:
+                        mov.add(y)
+                if v in mov:
+                    continue
+                new = perm[:a] + [y for y in seg if y not in mov] + [y for y in seg if y in mov] + perm[b + 1:]
+        r = run(new, eng, dur, D, cur, a)
+        nv = max(r[0]) if r else None
+        if r and (nv <= val or r3 < math.exp((val - nv) / temp)):
+            perm, cur, val, arcs = new, r, nv, None
+            kept += 1
+            if kept % 8 == 0:
+                p2 = sorted(perm, key=lambda i: r[0][i] - dur[i])
+                z = run(p2, eng, dur, D)
+                if z and max(z[0]) <= val:
+                    perm, cur, val = p2, z, max(z[0])
+            if val < best[0]:
+                best = (val, list(perm), list(eng))
+        elif undo:
+            eng[undo[0]], dur[undo[0]] = undo[1], undo[2]
+    return best
 
 
 def schedule(ops):
     n = len(ops)
-    succ = [[] for _ in range(n)]
-    left = [0] * n
+    fw, bw = [[] for _ in range(n)], [[] for _ in range(n)]
     for op in ops:
         for p in op["preds"]:
-            succ[p].append(op["i"])
-            left[op["i"]] += 1
-    prio = [0.0] * n
-    free = {e: 0.0 for e in "VSPGY"}
-    fin = [0.0] * n
-    bank = {}
-    pool = {b: None for b in POOL}
-    ready = [i for i in range(n) if left[i] == 0]
-    order = []
-    choice = {}
-    for op in ops:
-        off, ch = TUNE.get(op["grp"], (0, "."))
-        prio[op["i"]] = -(op["i"] + off)
-        if len(op["engs"]) > 1 and ch in op["engs"] and max(op["engs"].values()) > 300:
-            choice[op["i"]] = ch
-
-    def done(i, f):
-        fin[i] = f
-        for q in succ[i]:
-            left[q] -= 1
-            if left[q] == 0:
-                if ops[q].get("null"):
-                    done(q, max([fin[p] for p in ops[q]["preds"]]))
-                else:
-                    ready.append(q)
-
-    for op in ops:
-        op["bk"] = sorted({r[0] for r in op["R"] + op["W"] if r[0] in PSUM})
-
-    while ready:
-        best = None
-        found = []
-        for i in ready:
-            op = ops[i]
-            t0 = 0.0
-            for p in op["preds"]:
-                x = fin[p] + LAT + (1500 if "send" in ops[p] else 0)
-                t0 = max(t0, x)
-            bk = None
-            if op.get("alloc"):
-                opts = [(fin[c] + LAT if c is not None else 0.0, b) for b, c in pool.items() if c != -1]
-                if not opts:
-                    continue
-                x, bk = min(opts)
-                t0 = max(t0, x)
-            cand = None
-            for e, d in op["engs"].items():
-                if choice.get(i, e) != e:
-                    continue
-                s = max(t0, free[e])
-                for b in op["bk"]:
-                    for f, (x, q) in bank.get(b, {}).items():
-                        if f != e:
-                            s = max(s, x + LAT)
-                if cand is None or s + d < cand[0]:
-                    cand = (s + d, s, e)
-            ef, s, e = cand
-            found.append((s, i, e, ef, bk))
-            if best is None or s < best[0]:
-                best = found[-1]
-        s0, e0 = best[0] + WIN, best[2]
-        for x in found:
-            if x[2] == e0 and x[0] <= s0 and prio[x[1]] > prio[best[1]]:
-                best = x
-        s, i, e, ef, bk = best
+            lag = PRM["LAT"] + ops[p].get("lag", 0.0)
+            fw[op["i"]].append((p, lag))
+            bw[p].append((op["i"], lag))
+    pair = {op["src"]["i"]: op["i"] for op in ops if "src" in op}
+    back = {b: a for a, b in pair.items()}
+    fa, ba = [[q for q, lag in x] for x in bw], [[q for q, lag in x] for x in fw]
+    rng = np.random.RandomState(PRM["SEED"])
+    best = None
+    key = [float(i) for i in range(n)]
+    for turn in range(PRM["TRIES"] + 1):
+        for _ in range(2 if turn else PRM["PASSES"]):
+            r = place(ops, fw, fa, pair, [-1.0e9 if op["grp"] == "0" else x for op, x in zip(ops, key)])
+            if best is None or max(r[1]) < max(best[1]):
+                best = r
+            key = [-x for x in place(ops, bw, ba, back, [-x for x in r[1]])[1]]
+        key = [s + PRM["NOISE"] * x for s, x in zip(best[0], rng.rand(n).tolist())]
+    D = (fw, [[5 + 3 * b for b in op["bk"]] for op in ops], [1 if op.get("alloc") else 2 if "src" in op else 0 for op in ops],
+         [op["src"]["i"] if "src" in op else -1 for op in ops], PRM["LAT"])
+    span, order, eng = anneal(ops, D, sorted(range(n), key=lambda i: (best[0][i], i)), [EN.index(e) for e in best[2]], rng)
+    fin, why, slot, marks = run(order, eng, [ops[i]["engs"][EN[eng[i]]] for i in range(n)], D)
+    last = {}
+    for i in order:
         op = ops[i]
-        if "subs" in op and e == "V":
-            for x in op["subs"] + op["abss"][1:]:
-                ops[x]["null"] = True
-            z = ops[op["abss"][0]]
-            z["whole"] = True
-            z["engs"] = {"S": z["wdur"]}
-        ready.remove(i)
-        op["eng"] = e
-        op["deps"] = list(op["preds"])
+        op["eng"], op["fin"], op["deps"] = EN[eng[i]], fin[i], list(op["preds"])
         if op.get("alloc"):
-            op["bank"] = bk
-            if pool[bk] is not None:
-                op["deps"].append(pool[bk])
-            pool[bk] = -1
-        if "src" in op and not op.get("whole"):
-            pool[op["src"]["bank"]] = i
+            op["bank"] = POOL[slot[i] - 17]
+            op["deps"] += last.get(op["bank"], [])
+        if "src" in op:
+            last[op["src"]["bank"]] = [i]
         for b in op["bk"]:
-            d = bank.setdefault(b, {})
-            for f, (x, q) in d.items():
-                if f != e:
-                    op["deps"].append(q)
-            d[e] = (ef, i)
-        op["start"] = s
-        free[e] = s + 60.0 if e == "Y" else ef
-        order.append(i)
-        done(i, ef)
-    return order, max(fin)
+            d = last.setdefault(b, {})
+            op["deps"] += [q for f, q in d.items() if f != eng[i]]
+            d[eng[i]] = i
+    return order, span
 
 
 def make_plan():
     ops = build_ops()
     order, span = schedule(ops)
-    know = {e: {} for e in "VSPGY"}
+    know = {e: {} for e in EN}
     cnt = {"V": 0, "S": 0, "P": 0, "G": 0}
     out = []
     for i in order:
@@ -604,15 +773,10 @@ def make_plan():
         e = op["eng"]
         need = {}
         srcs = []
-        deps = list(op["deps"])
-        for d in deps:
+        for d in op["deps"]:
             q = ops[d]
-            if q.get("null"):
-                deps.extend(x for x in q["preds"] if x not in deps)
-                continue
             if "send" in q:
-                if "ext" in op:
-                    need[op["ext"]] = "ARR"
+                need[op["ext"]] = "ARR"
                 continue
             sem, v = q["tok"]
             if know[e].get(sem, 0) < v:
@@ -654,7 +818,7 @@ def rank_program(g, core, T, topo):
     hand = {"V": g.vector, "S": g.scalar, "P": g.tensor, "G": g, "Y": g.sync}
 
     def link(src, dst):
-        return topo.engines(src, dst)[:4]
+        return topo.engines(src, dst)[:ENGINES]
 
     for op in plan:
         e = op["eng"]
@@ -680,7 +844,6 @@ def rank_program(g, core, T, topo):
         g.wait_ge(T.sem["snt%d" % t], len(link(core, T.cores[(rank + 1 + t % (N - 1)) % N])))
     for e in "VSPG":
         g.wait_ge(T.sem["q" + e], cnt[e])
-    for n in LOADS:
-        g.sync.wait_ge(T.sem["ld" + n], 16)
-    for n in OUTS:
-        g.sync.wait_ge(T.sem["st" + n], 16)
+    for op in plan:
+        if "sem" in op:
+            g.sync.wait_ge(T.sem[op["sem"]], 16)

@@ -4,49 +4,53 @@ from concourse.mybir import AluOpType, AxisListType, ActivationFunctionType
 
 A_ = AluOpType
 F_ = ActivationFunctionType
-BNDS = [[0, 102, 190, 256], [0, 84, 172, 256], [0, 66, 154, 256], [0, 100, 192, 256], [0, 82, 174, 256]]
-NCH = len(BNDS[0]) - 1
-ST = [max(b[k + 1] - b[k] for b in BNDS[:4]) for k in range(NCH)]
-SM = max(ST)
+BNDS = [[0, 102, 172, 256], [0, 102, 204, 256], [0, 84, 186, 256], [0, 66, 168, 256], [0, 48, 150, 256]]
+NCH = 3
+RO = 4
+SM = 102
 SC = 1024
 YO = 2048.0
 BIG = 12582912.0
-PRM = {
-    "NSP": [[1, 1, 1]] * 4,
-    "TBP": [[1, 1, 1]] * 5,
-    "NA": 0,
-    "ONS": ["C10"],
-    "ONV": ["R2L", "FR2L", "R00@0"],
-    "GW": 128,
-    "PEC": 0.48, "GC": 1.55, "LAT": 100.0, "FV": 55.0, "FS": 75.0, "XLD": 6000.0, "SND": 2000.0,
-    "WIN": 200.0, "FILL": 150.0, "HOLD": 1000.0, "BOOST": 1000.0,
-    "PASSES": 5, "TRIES": 6, "NOISE": 1000.0, "MOVES": 12000, "SEED": 0, "T0": 60.0, "T1": 5.0,
-}
-RO = 4
-CY = 0.83
 ENGINES = 8
+CY = 0.83
+PRM = {
+    "ONS": ["C10", "C20@3"],
+    "ONV": ["FR2L", "R00@0"],
+    "END": 24,
+    "WIN": [100, 150, 200, 250], "FILL": [100, 150, 200], "HOLD": [700, 1000, 1500], "BOOST": [700, 1000, 2000],
+    "TRIES": 50, "NOISE": [500, 1000, 2000, 3000], "SEED": 15, "WIDTH": 70,
+    "ONE": (3, 10, 900, 100.0, 12.0), "ALL": (6, 0, 520, 120.0, 15.0),
+}
+HOW = ("WIN", "FILL", "HOLD", "BOOST")
+COSTS = [{"GC": 1.55, "PEC": 0.48, "LAT": 100.0, "FV": 55.0, "FS": 75.0, "SND": 2000.0, "XLD": 6000.0, "W": 0.35},
+         {"GC": 1.2, "PEC": 0.5, "LAT": 110.0, "FV": 55.0, "FS": 90.0, "SND": 2300.0, "XLD": 6000.0, "W": 0.12},
+         {"GC": 1.8, "PEC": 0.58, "LAT": 70.0, "FV": 55.0, "FS": 70.0, "SND": 1400.0, "XLD": 4200.0, "W": 0.16},
+         {"GC": 2.0, "PEC": 0.45, "LAT": 70.0, "FV": 55.0, "FS": 70.0, "SND": 1500.0, "XLD": 4500.0, "W": 0.2},
+         {"GC": 1.35, "PEC": 0.44, "LAT": 55.0, "FV": 52.0, "FS": 67.0, "SND": 1300.0, "XLD": 4500.0, "W": 0.22}]
 CONST = {"KX": YO + 32.0, "KY": YO, "K1": 2464.0, "K2": 4928.0, "K3": 7392.0}
-DIAGS = {"IP": 1.0, "IA": YO + 32.0, "IB": 1152.0, "IW": YO + 1184.0, "IN": -1.0, "IF": 1.0, "NF": -1.0, "IY": YO}
+DIAGS = {"IP": 1.0, "IA": YO + 32.0, "IB": 1152.0, "IW": YO + 1184.0, "IN": -1.0, "IF": 1.0}
 
 SCRATCH = {
     "X": ("sbuf", [128, 4096], "bfloat16"), "RI": ("sbuf", [128, 256], "int32"), "BI": ("sbuf", [128, 256], "int32"),
-    "TI": ("sbuf", [128, 1], "int32"), "EI": ("sbuf", [128, 1], "int32"), "EPF": ("sbuf", [128, 1], "float32"),
-    "ES": ("sbuf", [128, 1], "float32"), "TH0": ("sbuf", [128, 1], "float32"),
-    "THR": ("sbuf", [128, 1], "float32"), "AC": ("sbuf", [128, 1], "float32"), "CNT": ("sbuf", [128, 1], "float32"),
+    "TI": ("sbuf", [128, 1], "int32"), "EI": ("sbuf", [128, 1], "int32"),
+    "ES": ("sbuf", [128, 1], "float32"), "THR": ("sbuf", [128, RO + 1], "float32"),
+    "AC": ("sbuf", [128, 1], "float32"), "CNT": ("sbuf", [128, 1], "float32"),
     "OR": ("sbuf", [128, 256], "float32"), "OM": ("sbuf", [128, 256], "float32"), "MR": ("sbuf", [128, 256], "float32"),
-    "YR": ("sbuf", [128, 272], "float16"), "YM": ("sbuf", [128, 272], "float16"), "YP": ("sbuf", [128, 280], "float32"),
+    "YR": ("sbuf", [128, 520], "float16"), "YM": ("sbuf", [128, 520], "float16"),
+    "YP": ("sbuf", [128, 768], "float16"), "LW0": ("sbuf", [128, 272], "float32"), "LW1": ("sbuf", [128, 272], "float32"),
     "RU": ("sbuf", [128, 256], "uint16"), "MU": ("sbuf", [128, 256], "uint16"), "PU": ("sbuf", [128, 256], "uint16"),
     "GR": ("sbuf", [128, 4112], "bfloat16"), "GM": ("sbuf", [128, 4096], "bfloat16"), "GP": ("sbuf", [128, 4096], "bfloat16"),
-    "AB": ("sbuf", [128, 3840], "bfloat16"), "NW": ("sbuf", [128, 4096], "bfloat16"), "A3": ("sbuf", [128, 4096], "bfloat16"),
+    "AB": ("sbuf", [128, 3840], "bfloat16"), "NW": ("sbuf", [128, 4096], "bfloat16"),
     "I3": ("sbuf", [128, 4096], "bfloat16"), "NR": ("sbuf", [128, 4096], "bfloat16"),
-    "MK": ("sbuf", [128, 256], "bfloat16"), "MA": ("sbuf", [128, 256], "bfloat16"), "M0": ("sbuf", [128, 256], "bfloat16"),
-    "MS": ("sbuf", [128, 256], "bfloat16"), "ZE": ("sbuf", [128, 256], "bfloat16"), "JK": ("sbuf", [128, 256], "bfloat16"),
+    "MK": ("sbuf", [128, 768], "bfloat16"), "MA": ("sbuf", [128, 512], "bfloat16"), "M0": ("sbuf", [128, 256], "bfloat16"),
+    "MS0": ("sbuf", [128, 512], "bfloat16"), "MS1": ("sbuf", [128, 512], "bfloat16"),
+    "ZE": ("sbuf", [128, 256], "bfloat16"), "JK": ("sbuf", [128, 256], "bfloat16"),
     "TG": ("sbuf", [128, 5 * SM], "float16"), "TF": ("sbuf", [128, 5 * SM], "float32"), "CMD": ("sbuf", [128, 256], "float32"),
     "DIAG": ("sbuf", [128, 256], "float32"), "SEG": ("sbuf", [128, 256], "bfloat16"), "IK": ("sbuf", [128, 16], "float32"),
     "PI": ("sbuf", [128, 1], "int32"), "PF": ("sbuf", [128, 1], "float32"), "ZT": ("sbuf", [128, 144], "bfloat16"),
-    "EP": ("sbuf", [128, 128], "float16"), "EN": ("sbuf", [128, 128], "float16"),
+    "ZF": ("sbuf", [128, 128], "float32"), "EP": ("sbuf", [128, 128], "float16"), "EN": ("sbuf", [128, 128], "float16"),
     "OFF": ("sbuf", [128, 16], "uint16"), "LG": ("sbuf", [128, 256], "float32"), "LS": ("sbuf", [128, 256], "float32"),
-    "LPI": ("sbuf", [128, 16], "int32"), "OWN": ("sbuf", [128, 16], "float32"),
+    "LPI": ("sbuf", [128, 16], "int32"),
     "KB0": ("psum", [128, 512], "float32"), "KB1": ("psum", [128, 512], "float32"), "KB2": ("psum", [128, 512], "float32"),
     "NB": ("psum", [128, 512], "float32"),
     "SB0": ("psum", [128, 1024], "float32"), "SB1": ("psum", [128, 1024], "float32"),
@@ -57,16 +61,13 @@ for _k in DIAGS:
     SCRATCH[_k] = ("sbuf", [128, 128], "float32" if _k[1] == "F" else "bfloat16")
 for _k in range(NCH):
     for _b, _w, _d in (("CI", 4, "int32"), ("CU", 4, "uint16"), ("DS", 64, "bfloat16"), ("DA", 80, "bfloat16"), ("KM", 1, "float32"),
-                       ("KI", 1, "int32"), ("MI", 1, "int32"), ("OU", 1, "uint16"), ("E5", 1, "bfloat16"), ("EC", 4, "float32"),
-                       ("EM", 1, "float16")):
-        SCRATCH["%s%d" % (_b, _k)] = ("sbuf", [128, _w * ST[_k]], _d)
-    SCRATCH["PB%d" % _k] = ("sbuf", [128, ST[_k] + 2], "int32")
+                       ("KI", 1, "int32"), ("MI", 1, "int32"), ("OU", 1, "uint16"), ("EC", 4, "float32")):
+        SCRATCH["%s%d" % (_b, _k)] = ("sbuf", [128, _w * SM], _d)
+    SCRATCH["PB%d" % _k] = ("sbuf", [128, SM + 2], "int32")
 for _k in range(RO):
     SCRATCH["SEND%d" % _k] = ("sbuf", [128, 16], "float32")
     SCRATCH["LAND%d" % _k] = ("sbuf", [128, 16], "float32")
-LOADS = ["RI", "BI", "X", "TI", "EI"]
-STORES = 8
-SEMAPHORES = (["qV", "qS", "qP", "qG"] + ["ld" + n for n in LOADS] + ["st%d" % n for n in range(STORES)]
+SEMAPHORES = (["qV", "qS", "qP", "qG"] + ["ld" + n for n in ("RI", "BI", "X", "TI", "EI")] + ["st%d" % n for n in range(7)]
               + ["arr%d" % t for t in range(RO)] + ["snt%d" % t for t in range(RO)])
 PSUM = [n for n in SCRATCH if SCRATCH[n][0] == "psum"]
 WIDE = [n for n in SCRATCH if SCRATCH[n][2] in ("float32", "int32")]
@@ -76,29 +77,52 @@ BW = 1024
 EN = "VSPGY"
 
 
-def cut(a, b, k):
-    ps = [a + (b - a) * q // k // 2 * 2 for q in range(k)] + [b]
-    return list(zip(ps, ps[1:]))
+def after_choice(t, a, b):
+    return [(a, b - PRM["END"]), (b - PRM["END"], b)] if t == RO - 1 and b == 256 else [(a, b)]
+
+
+def pieces(t):
+    b = [0] + [x + 2 for x in BNDS[t][1:-1]] + [240]
+    return [("%d0" % k, b[k], b[k + 1]) for k in range(NCH)] + [("%dL" % (NCH - 1), 240, 256)]
 
 
 def sl(T, r):
-    return T[r[0]][:, r[1]:r[2]]
+    return T[r[0]][:, r[1]:r[2]:r[3]] if len(r) > 3 else T[r[0]][:, r[1]:r[2]]
 
 
-def build_ops():
+def ln(r):
+    return len(range(*r[1:]))
+
+
+def odd(b, x, y, c=0):
+    return (b, c + 2 * x + 1, c + 2 * y, 2)
+
+
+def even(b, x, y, c=0):
+    return (b, c + 2 * x, c + 2 * y - 1, 2)
+
+
+def third(b, x, y, j):
+    return (b, 3 * x + j, 3 * y - 2 + j, 3)
+
+
+def every(r):
+    return (r[0], r[1] - r[3] + 1, r[2])
+
+
+def build_ops(cost):
     ops = []
     seen = {}
     cur = [""]
     rnd = [0]
     stores = [0]
-    NSP, TBP, NA, PEC, GC = PRM["NSP"], PRM["TBP"], PRM["NA"], PRM["PEC"], PRM["GC"]
-    FV, FS = PRM["FV"], PRM["FS"]
+    PEC, GC, FV, FS, SND = [cost[x] for x in ("PEC", "GC", "FV", "FS", "SND")]
 
     def on(name):
         return cur[0] in PRM[name] or "%s@%d" % (cur[0], rnd[0]) in PRM[name]
 
     def O(engs, fn, R, W, **kw):
-        op = dict(kw, engs=engs, fn=fn, R=list(R), W=list(W), preds={}, i=len(ops), grp=cur[0])
+        op = dict(kw, engs=engs, fn=fn, R=[r[:3] for r in R], W=[r[:3] for r in W], preds={}, i=len(ops), grp=cur[0])
         for rd, lst in ((True, op["R"]), (False, op["W"])):
             for (b, c0, c1) in lst:
                 if b == "POOL":
@@ -130,12 +154,10 @@ def build_ops():
         return FS + CY * n
 
     def tt(o, a, b, alu):
-        n = o[2] - o[1]
         cost = 1 if (a[0] in PSUM or b[0] in PSUM) else 2
-        return O({"V": vt(n, cost)}, lambda e, g, T, op: g.vector.tensor_tensor(sl(T, o), sl(T, a), sl(T, b), alu), [a, b], [o])
+        return O({"V": vt(ln(o), cost)}, lambda e, g, T, op: g.vector.tensor_tensor(sl(T, o), sl(T, a), sl(T, b), alu), [a, b], [o])
 
     def tsc(o, a, s1, s2, op0, op1=None):
-        n = o[2] - o[1]
         cost = 1 if (o[0] in WIDE or a[0] in WIDE) else 0.5
 
         def fn(e, g, T, op):
@@ -144,54 +166,39 @@ def build_ops():
             if op1 is None:
                 return g.vector.tensor_scalar(sl(T, o), sl(T, a), v1, None, op0)
             return g.vector.tensor_scalar(sl(T, o), sl(T, a), v1, v2, op0, op1)
-        rd = [a] + [s for s in (s1, s2) if isinstance(s, tuple)]
-        return O({"V": vt(n, cost)}, fn, rd, [o])
+        return O({"V": vt(ln(o), cost)}, fn, [a] + [s for s in (s1, s2) if isinstance(s, tuple)], [o])
 
     def copy(o, a):
-        return O({"V": vt(o[2] - o[1], 1)}, lambda e, g, T, op: g.vector.tensor_copy(sl(T, o), sl(T, a)), [a], [o])
+        return O({"V": vt(ln(o), 1)}, lambda e, g, T, op: g.vector.tensor_copy(sl(T, o), sl(T, a)), [a], [o])
 
-    def plus(o, a, add, step=1):
-        n = o[2] - o[1]
-
+    def plus(o, a, add):
         def fn(e, g, T, op):
-            src = T[a[0]][:, a[1]:a[2]:step]
             if e == "V":
-                return g.vector.tensor_scalar(sl(T, o), src, add, None, A_.add)
-            return g.scalar.activation(sl(T, o), src, F_.Copy, bias=add)
-        narrow = SCRATCH[o[0]][2] != "float32" or SCRATCH[a[0]][2] != "float32"
-        return O({"V": vt(n, 1)} if narrow else {"V": vt(n, 1), "S": st(n)}, fn, [a], [o])
+                return g.vector.tensor_scalar(sl(T, o), sl(T, a), add, None, A_.add)
+            return g.scalar.activation(sl(T, o), sl(T, a), F_.Copy, bias=add)
+        return O({"V": vt(ln(o), 1), "S": st(ln(o))}, fn, [a], [o])
 
     def over(o, a, limit, scale=1.0, only=None):
-        n = o[2] - o[1]
-
         def fn(e, g, T, op):
             if e == "V":
                 return g.vector.tensor_scalar(sl(T, o), sl(T, a), limit, None, A_.is_gt)
             return g.scalar.activation(sl(T, o), sl(T, a), F_.Sigmoid, bias=-limit * scale, scale=scale)
-        return O(only or {"V": vt(n, 1), "S": st(n)}, fn, [a], [o])
+        return O(only or {"V": vt(ln(o), 1), "S": st(ln(o))}, fn, [a], [o])
 
     def memset(o, v):
-        return O({"V": vt(o[2] - o[1], 0.5)}, lambda e, g, T, op: g.vector.memset(sl(T, o), v), [], [o])
-
-    def parts(off, *big):
-        k = off[2] - off[1]
-        for x, y in cut(0, k, -(-k // PRM["GW"])):
-            yield [(off[0], off[1] + x, off[1] + y)] + [(r[0], r[1] + 16 * x, r[1] + 16 * y) for r in big]
+        return O({"V": vt(ln(o), 0.5)}, lambda e, g, T, op: g.vector.memset(sl(T, o), v), [], [o])
 
     def gather(o, win, off):
-        for off1, o1 in parts(off, o):
-            def fn(e, g, T, op, off1=off1, o1=o1):
-                src = sl(T, win).indirect(sl(T, off1))
-                if e == "V":
-                    return g.vector.tensor_copy(sl(T, o1), src)
-                return g.scalar.activation(sl(T, o1), src, F_.Copy)
-            n = o1[2] - o1[1]
-            O({"V": 50 + GC * CY * n, "S": 65 + GC * CY * n}, fn, [win, off1], [o1], first="V" if on("ONV") else "S")
+        def fn(e, g, T, op):
+            src = sl(T, win).indirect(sl(T, off))
+            if e == "V":
+                return g.vector.tensor_copy(sl(T, o), src)
+            return g.scalar.activation(sl(T, o), src, F_.Copy)
+        O({"V": 50 + GC * CY * ln(o), "S": 65 + GC * CY * ln(o)}, fn, [win, off], [o], first="V" if on("ONV") else "S")
 
     def gather_tt(o, win, off, b, alu):
-        for off1, o1, b1 in parts(off, o, b):
-            O({"V": 50 + GC * CY * (o1[2] - o1[1])}, lambda e, g, T, op, off1=off1, o1=o1, b1=b1: g.vector.tensor_tensor(
-                sl(T, o1), sl(T, win).indirect(sl(T, off1)), sl(T, b1), alu), [win, off1, b1], [o1])
+        O({"V": 50 + GC * CY * ln(o)}, lambda e, g, T, op: g.vector.tensor_tensor(
+            sl(T, o), sl(T, win).indirect(sl(T, off)), sl(T, b), alu), [win, off, b], [o])
 
     def lin(sums):
         def fn(e, g, T, op):
@@ -200,7 +207,7 @@ def build_ops():
                 for j, (w, x) in enumerate(terms):
                     r = g.tensor.matmul(sl(T, o), T[w][:], sl(T, x), j == 0, j == len(terms) - 1)
             return r
-        ns = 30 + sum(PEC * max(64, o[2] - o[1]) * (4 if w in WIDE else 1) for o, terms in sums for w, x in terms)
+        ns = 30 + sum(PEC * max(64, ln(o)) * (4 if w in WIDE else 1) for o, terms in sums for w, x in terms)
         rd = [x for o, terms in sums for w, x in terms] + [(w, 0, 128) for o, terms in sums for w, x in terms]
         return O({"P": ns}, fn, rd, [o for o, terms in sums])
 
@@ -225,16 +232,14 @@ def build_ops():
                   [("POOL", 0, m)], [o1], src=q)
             r["preds"][q["i"]] = 1
 
-    def absdiff(o, a, b, func=F_.Abs, bias=0.0):
-        diff(o, a, b, "IP", "IN", lambda m: {"S": st(m)}, lambda g, x, y: g.scalar.activation(x, y, func, bias=bias))
+    def absdiff(o, a, b):
+        diff(o, a, b, "IP", "IN", lambda m: {"S": st(m)}, lambda g, x, y: g.scalar.activation(x, y, F_.Abs))
 
     def within(o, a, b):
         diff(o, a, b, "EP", "EN", lambda m: {"V": vt(m, 1)},
              lambda g, x, y: g.vector.tensor_scalar(x, y, BIG, BIG, A_.add, A_.is_equal))
 
     def stage_sum(o, a, tag=None):
-        n = o[2] - o[1]
-
         def fn(e, g, T, op):
             d = sl(T, o)
             r = None
@@ -243,119 +248,126 @@ def build_ops():
             for p in range(16):
                 r = g.tensor.matmul(d, T.ZT[:, 15 - p:143 - p], T[a[0]][:, a[1] + p:a[2]:16], not tag and p == 0, p == 15)
             return r
-        O({"P": (17 if tag else 16) * PEC * max(64, n) + 30}, fn, [a, ("ZT", 0, 144)] + ([tag, ("IP", 0, 128)] if tag else []), [o])
+        O({"P": (17 if tag else 16) * PEC * max(64, ln(o)) + 30}, fn, [a, ("ZT", 0, 144)] + ([tag, ("IP", 0, 128)] if tag else []), [o])
+
+    def pick(o, mask, d, names):
+        O({"V": vt(ln(every(o)), 1)}, lambda e, g, T, op: g.vector.tensor_tensor_scan(
+            sl(T, every(o)), sl(T, every(mask)), sl(T, every(d)), 0.0, A_.mult, A_.add), [every(mask), every(d)], [every(o)])
+        tsc(names, o, YO, None, A_.add)
 
     def load(dst, src, w, ns):
         O({"Y": ns}, lambda e, g, T, op: g.sync.dma_start(T[dst][:], T[src][:]), [], [(dst, 0, w)], sem="ld" + dst)
 
     def store(dst, r):
-        whole = r[2] - r[1] == SCRATCH[r[0]][1][1]
-        O({"Y": 1300.0 + 2 * (r[2] - r[1])}, lambda e, g, T, op: g.sync.dma_start(T[dst][:] if whole else T[dst][:, r[1]:r[2]], sl(T, r)),
+        whole = ln(r) == SCRATCH[r[0]][1][1]
+        O({"Y": 1300.0 + 2 * ln(r)}, lambda e, g, T, op: g.sync.dma_start(T[dst][:] if whole else T[dst][:, r[1]:r[2]], sl(T, r)),
           [r], [], sem="st%d" % stores[0])
         stores[0] += 1
     load("RI", "riv", 256, 1500)
-    load("X", "flood", 4096, PRM["XLD"])
+    load("X", "flood", 4096, cost.get("XLD", 6000.0))
     load("BI", "bord", 256, 2000)
     load("TI", "th", 1, 2000)
     load("EI", "eps", 1, 2000)
 
-    def sel(buf, n, pattern, base, cm, cmp):
-        O({"G": 170 + 2 * CY * n}, lambda e, g, T, op: g.affine_select(T[buf][:], T[buf][:], pattern, cmp, 0.0, base, cm),
-          [(buf, 0, n)], [(buf, 0, n)])
+    def sel(o, a, pattern, cmp, fill, base, cm):
+        O({"G": 170 + 2 * CY * ln(o)}, lambda e, g, T, op: g.affine_select(sl(T, o), sl(T, a), pattern, cmp, fill, base, cm), [a], [o])
 
     def iota(r, pattern, base, cm):
         kw = {} if r[0] == "PI" else {"allow_small_or_imprecise_dtypes": True}
-        O({"G": 130 + 2 * CY * (r[2] - r[1])}, lambda e, g, T, op: g.iota(sl(T, r), pattern, base, cm, **kw), [], [r])
+        O({"G": 130 + 2 * CY * ln(r)}, lambda e, g, T, op: g.iota(sl(T, r), pattern, base, cm, **kw), [], [r])
     cur[0] = "0"
     iota(("CMD", 0, 256), [[0, 16], [1, 16]], 0, 0)
     over(("SEG", 0, 256), ("CMD", 0, 256), 0.5, 1024.0, {"S": st(256) + 1300})
     cur[0] = ""
+    memset(("ZE", 0, 256), 0.0)
+    memset(("ZF", 0, 128), 0.0)
     for b in DIAGS:
-        memset((b, 0, 128), DIAGS[b])
-        sel(b, 128, [[-1, 128]], 0, 1, A_.is_equal)
+        sel((b, 0, 128), ("ZF" if b in WIDE else "ZE", 0, 128), [[-1, 128]], A_.not_equal, DIAGS[b], 0, 1)
     for b in CONST:
-        memset((b, 0, SM + 2), CONST[b])
-    memset(("ZT", 0, 144), float(SC))
-    sel("ZT", 144, [[0, 9], [1, 16]], -15, 0, A_.is_equal)
-    sel("ZT", 144, [[-16, 9], [0, 16]], 0, 1, A_.is_ge)
-    sel("ZT", 144, [[16, 9], [0, 16]], 15, -1, A_.is_ge)
+        iota((b, 0, SM + 2), [[0, SM + 2]], int(CONST[b]), 0)
+    zt = ("ZT", 0, 144)
+    iota(zt, [[0, 144]], SC, 0)
+    sel(zt, zt, [[0, 9], [1, 16]], A_.is_equal, 0.0, -15, 0)
+    sel(zt, zt, [[-16, 9], [0, 16]], A_.is_ge, 0.0, 0, 1)
+    sel(zt, zt, [[16, 9], [0, 16]], A_.is_ge, 0.0, 15, -1)
     iota(("PI", 0, 1), [[0, 1]], 0, 1)
     iota(("TF", 0, 5 * SM), [[1, 5 * SM]], 0, 0)
     copy(("TG", 0, 5 * SM), ("TF", 0, 5 * SM))
     iota(("IK", 0, 16), [[1, 16]], 256, 0)
-    for k in range(NCH):
-        for m in range(5):
-            r = ("DA%d" % k, 16 * (ST[k] * m + BNDS[0][k + 1] - BNDS[0][k]), 16 * ST[k] * (m + 1))
-            if r[1] < r[2]:
-                iota(r, [[0, r[2] - r[1]]], 0, 0)
     tsc(("PI", 0, 1), ("PI", 0, 1), 15, None, A_.bitwise_and)
     copy(("PF", 0, 1), ("PI", 0, 1))
     tsc(("DIAG", 0, 256), ("CMD", 0, 256), ("PF", 0, 1), None, A_.is_equal)
-    for r in (("ZE", 0, 256), ("M0", 240, 256), ("MS", 0, 1), ("NW", 4080, 4096), ("GR", 4096, 4112)):
-        memset(r, 0.0)
-    copy(("YR", 264, 272), ("ZE", 0, 8))
-    copy(("YM", 256, 264), ("ZE", 0, 8))
+    for r in (("GR", 4096, 4112), ("NW", 4080, 4096), ("MK", 0, 768), ("M0", 240, 256), ("MS0", 0, 512), ("MA", 0, 512),
+              ("MS1", 0, 512)):
+        iota(r, [[0, ln(r)]], 0, 0)
+    copy(("YR", 512, 520), ("ZE", 0, 8))
+    copy(("YM", 512, 520), ("ZE", 0, 8))
 
     XWIN = ("X", 0, 4096)
 
     def yr(a, b):
-        return ("YR", 8 + a, 8 + b)
+        return odd("YR", a, b)
+
+    def ym(a, b):
+        return odd("YM", a, b)
 
     def yp(a, b):
-        return ("YP", 8 + a, 8 + b)
+        return third("YP", a, b, 2)
 
-    def choice(o, mask, d, base, names=None):
-        tt(d, d, mask, A_.mult)
-        tt(o, d, base, A_.add)
-        if names:
-            tsc(names, o, YO, None, A_.add)
+    def lw(a, b):
+        return ("LW%d" % (rnd[0] % 2), a, b)
+
+    def ms(a, b):
+        return odd("MS%d" % (rnd[0] % 2), a, b)
 
     def accretion(ta, tb, last):
-        gr, gm, a3, i3 = [(b, 16 * ta, 16 * tb) for b in ("GR", "GM", "A3", "I3")]
-        if on("ONS"):
-            absdiff(a3, gr, gm)
-            tsc(i3, a3, ("EPF", 0, 1), None, A_.is_le)
-        else:
-            within(i3, gr, gm)
+        gr, gm, i3 = [(b, 16 * ta, 16 * tb) for b in ("GR", "GM", "I3")]
+        within(i3, gr, gm)
         stage_sum(("NB", ta, tb), i3)
-        dm, ma = ("NB", 256 + ta, 256 + tb), ("MA", ta, tb)
-        lin([(dm, [("IP", yr(ta, tb)), ("IN", ("YM", ta, tb))])])
+        ma, terms = odd("MA", ta, tb), [("IP", yr(ta, tb)), ("IN", ym(ta, tb))]
         over(ma, ("NB", ta, tb), 8.5 * SC)
         if last:
-            choice(("OM", ta, tb), ma, dm, ("MR", ta, tb))
+            dm = ("NB", 256 + ta, 256 + tb)
+            lin([(dm, terms)])
+            tt(dm, dm, ma, A_.mult)
+            tt(("OM", ta, tb), dm, ("MR", ta, tb), A_.add)
             store("ym", ("OM", ta, tb))
         else:
-            choice(("YM", ta, tb), ma, dm, ("YM", ta, tb), ("MU", ta, tb))
+            lin([(even("NB", 0, tb - ta, 256), terms), (odd("NB", 0, tb - ta, 256), [("IP", ym(ta, tb))])])
+            pick(ym(ta, tb), ma, odd("NB", 0, tb - ta, 256), ("MU", ta, tb))
 
     def lists(k, t, a, b):
         n = b - a
         ci, kb, pb = "CI%d" % k, "KB%d" % k, "PB%d" % k
         c = [("IP", ("K%d" % t, 0, n))] if t else []
         cur[0] = "L%d0" % k
-        lin([((kb, 4 * n, 5 * n + 1), [("IP", yr(a - 1, b)), ("IP", ("KX", 0, n + 1))]),
-             ((kb, n, 2 * n), [("IA", yr(a - 1, b - 1)), ("IB", yr(a, b))] + c),
-             ((kb, 2 * n, 3 * n), [("IW", yr(a, b))] + c), ((kb, 3 * n, 4 * n), [("IW", yr(a, b))] + c)])
+        z = 0 if a else 1
+        lin([((kb, 4 * n + z, 5 * n + 1), [("IP", yr(a - 1 + z, b)), ("IP", ("KX", 0, n + 1 - z))]),
+             ((kb, n + z, 2 * n), [("IA", yr(a - 1 + z, b - 1)), ("IB", yr(a + z, b))] + [(w, (x[0], 0, n - z)) for w, x in c]),
+             ((kb, 2 * n, 3 * n), [("IW", yr(a, b))] + c), ((kb, 3 * n, 4 * n), [("IW", yr(a, b))] + c)]
+            + ([((kb, 4 * n, 4 * n + 1), [("IP", yr(0, 1)), ("IP", ("KX", 0, 1))]),
+                ((kb, n, n + 1), [("IW", yr(0, 1))] + [(w, (x[0], 0, 1)) for w, x in c])] if z else []))
         for half in range(2):
             cur[0] = "L%d%d" % (k, half)
-            lo, hi = 2 * n * half, 2 * n * half + 2 * n
+            r = (ci, 2 * n * half, 2 * n * half + 2 * n)
             if half == 0:
                 tt((pb, 0, n + 1), (kb, 4 * n, 5 * n + 1), yr(a, b + 1), A_.mult)
                 for q in range(2):
                     tt((ci, q * n, q * n + n), (kb, n + q * n, 2 * n + q * n), (pb, q, q + n), A_.add)
             else:
                 for q in range(2):
-                    tt((ci, lo + q * n, lo + q * n + n), (kb, 4 * n + 1, 5 * n + 1), ("YM", a + q, b + q), A_.mult)
-                tt((ci, lo, hi), (kb, lo, hi), (ci, lo, hi), A_.add)
-            tsc((ci, lo, hi), (ci, lo, hi), 5, 4095, A_.arith_shift_right, A_.bitwise_and)
-            copy(("CU%d" % k, lo, hi), (ci, lo, hi))
+                    tt((ci, 2 * n + q * n, 3 * n + q * n), (kb, 4 * n + 1, 5 * n + 1), ym(a + q, b + q), A_.mult)
+                tt(r, (kb, 2 * n, 4 * n), r, A_.add)
+            tsc(r, r, 5, 4095, A_.arith_shift_right, A_.bitwise_and)
+            copy(("CU%d" % k,) + r[1:], r)
 
     def keys(k, a, b):
         n = b - a
         nxt = ("GR", 16 * a + 16, 16 * b + 16)
         for m in (4, 0, 1, 2, 3):
             cur[0] = "C%d%d" % (k, m)
-            da = ("DA%d" % k, 16 * ST[k] * m, 16 * (ST[k] * m + n))
-            ds, off = ("DS%d" % k, 16 * n * m, 16 * n * (m + 1)), ("CU%d" % k, m * n, m * n + n)
+            da, ds = [("%s%d" % (x, k), 16 * n * m, 16 * n * (m + 1)) for x in ("DA", "DS")]
+            off = ("CU%d" % k, m * n, m * n + n)
             if m == 4:
                 absdiff(da, ("GM", 16 * a, 16 * b), nxt)
             elif on("ONS"):
@@ -363,10 +375,8 @@ def build_ops():
                 absdiff(da, ds, nxt)
             else:
                 gather_tt(ds, XWIN, off, nxt, A_.subtract)
-                for _, o1, d1 in parts(off, da, ds):
-                    O({"S": st(o1[2] - o1[1])}, lambda e, g, T, op, o1=o1, d1=d1: g.scalar.activation(sl(T, o1), sl(T, d1), F_.Abs),
-                      [d1], [o1])
-            stage_sum(("KB%d" % k, m * n, m * n + n), da, ("TG", m * ST[k], m * ST[k] + n))
+                O({"S": st(16 * n)}, lambda e, g, T, op, da=da, ds=ds: g.scalar.activation(sl(T, da), sl(T, ds), F_.Abs), [ds], [da])
+            stage_sum(("KB%d" % k, m * n, m * n + n), da, ("TG", m * n, m * n + n))
 
     def choose(k, a, b):
         n = b - a
@@ -379,76 +389,74 @@ def build_ops():
             tt(ki if m == 3 else km, key[m], km, A_.min)
         tsc(("MI%d" % k, 0, n), ki, SC - 1, None, A_.bitwise_and)
         tsc(("OU%d" % k, 0, n), ("MI%d" % k, 0, n), 16.0, ("PF", 0, 1), A_.mult, A_.add)
-        ps = cut(a, b, NSP[rnd[0]][k])
-        for q, (x, y) in enumerate(ps):
-            nr, win, off = ("NR", 16 * x, 16 * y), ("DA%d" % k, 0, 80 * ST[k]), ("OU%d" % k, x - a, y - a)
-            cur[0] = "E%d%d" % (k, q)
-            if on("ONS"):
-                gather(nr, win, off)
-                absdiff(nr, ("NW", 16 * x, 16 * y), nr, F_.Sign, -0.5)
-            else:
-                gather_tt(nr, win, off, ("NW", 16 * x, 16 * y), A_.is_lt)
-            stage_sum(("NB", x, y), nr)
-            over(("MK", x, y), ("NB", x, y), (1.0 if on("ONS") else 8.5) * SC)
         cur[0] = "D%d" % k
+        tt(third("MK", a, b, 1), key[4], ki, A_.is_equal)
         for m in range(4):
             tt(key[m], key[m], ki, A_.is_equal)
         tt((ec, 0, 4 * n), (kb, 0, 4 * n), ("CI%d" % k, 0, 4 * n), A_.mult)
-        e5, em = ("E5%d" % k, 0, n), ("EM%d" % k, 0, n)
-        tt(e5, key[4], ki, A_.is_equal)
-        lin([(key[4], [("IP", ("YM", a, b))])])
-        tt(em, key[4], e5, A_.mult)
-        lin([(key[0], [("IN", yr(a, b)), ("IN", ("KY", 0, n)), ("IY", e5), ("IP", em)]
-              + [("IF", (ec, m * n, m * n + n)) for m in range(4)])])
+        lin([(third(kb, 0, n, 0), [("IP", ym(a, b)), ("IP", ("KY", 0, n))]), (third(kb, 0, n, 2), [("IP", yr(a, b))]),
+             (third(kb, 0, n, 1), [("IN", yr(a, b)), ("IN", ("KY", 0, n))] + [("IF", (ec, m * n, m * n + n)) for m in range(4)])])
+        ps = after_choice(rnd[0], a, b)
+        for q, (x, y) in enumerate(ps):
+            cur[0] = "E%d%d" % (k, q)
+            nr = ("NR", 16 * x, 16 * y)
+            gather_tt(nr, ("DA%d" % k, 0, 80 * n), ("OU%d" % k, x - a, y - a), ("NW", 16 * x, 16 * y), A_.is_lt)
+            stage_sum(("NB", x, y), nr)
+            over(third("MK", x, y, 2), ("NB", x, y), 8.5 * SC)
         for q, (x, y) in enumerate(ps):
             cur[0] = "P%d%d" % (k, q)
-            choice(yp(x, y), ("MK", x, y), (kb, x - a, y - a), yr(x, y), ("PU", x, y))
+            pick(yp(x, y), third("MK", x, y, 2), third(kb, x - a, y - a, 2), ("PU", x, y))
             gather(("GP", 16 * x, 16 * y), XWIN, ("PU", x, y))
+            lin([((kb, 320 + x - a, 320 + y - a), [("IP", yp(x, y))])])
+            plus(lw(x, y), (kb, 320 + x - a, 320 + y - a), YO)
 
     def necks(na, nb, last):
-        ab = ("AB", 16 * na, 16 * nb)
+        ab, thr = ("AB", 16 * na, 16 * nb), ("THR", rnd[0], rnd[0] + 1)
         absdiff(ab, ("GP", 16 * na, 16 * nb), ("GP", 16 * na + 256, 16 * nb + 256))
         stage_sum(("NB", na, nb), ab)
 
         def under(e, g, T, op):
             if e == "V":
-                return g.vector.tensor_scalar(T.M0[:, na:nb], T.NB[:, na:nb], T.THR[:], None, A_.is_lt)
-            return g.scalar.activation(T.M0[:, na:nb], T.NB[:, na:nb], F_.Sign, bias=T.THR[:], scale=-1.0)
-        O({"V": vt(nb - na, 1), "S": st(nb - na)}, under, [("NB", na, nb), ("THR", 0, 1)], [("M0", na, nb)])
+                return g.vector.tensor_scalar(T.M0[:, na:nb], T.NB[:, na:nb], sl(T, thr), None, A_.is_lt)
+            return g.scalar.activation(T.M0[:, na:nb], T.NB[:, na:nb], F_.Sign, bias=sl(T, thr), scale=-1.0)
+        O({"V": vt(nb - na, 1), "S": st(nb - na)}, under, [("NB", na, nb), thr], [("M0", na, nb)])
         hi = 255 if last else nb
+        old, new = ms(na, na + 1), ms(na + 1, hi + 1)
         O({"V": vt(hi - na, 0.5)}, lambda e, g, T, op: g.vector.tensor_tensor_scan(
-            T.MS[:, na + 1:hi + 1], T.M0[:, na:hi], T.ZE[:, na:hi], T.MS[:, na:na + 1], A_.max, A_.max),
-          [("M0", na, hi), ("ZE", na, hi), ("MS", na, na + 1)], [("MS", na + 1, hi + 1)])
+            sl(T, new), T.M0[:, na:hi], T.ZE[:, na:hi], sl(T, old), A_.max, A_.max), [("M0", na, hi), ("ZE", na, hi), old], [new])
 
-    def shift(ta, tb):
-        d = ("NB", 256 + ta, 256 + tb)
-        lin([(d, [("IF", yp(ta + 16, tb + 16)), ("NF", yp(ta, tb))])])
-        choice(yr(ta, tb), ("MS", ta, tb), d, yp(ta, tb), ("RU", ta, tb))
+    def shift(k, c, ta, tb):
+        kb, n = "KB%d" % k, tb - ta
+        lin([(even(kb, 0, n, c), [("IP", yp(ta + 16, tb + 16)), ("IN", yp(ta, tb))]), (odd(kb, 0, n, c), [("IP", yp(ta, tb))])])
+        pick(yr(ta, tb), ms(ta, tb), odd(kb, 0, n, c), ("RU", ta, tb))
 
     def loops(t):
-        h = ("MS", 255, 256)
-        plus(yp(256, 272), yp(240, 256), 8192.0)
+        h, mall = ms(255, 256), ms(0, 256)
+        plus(lw(256, 272), lw(240, 256), 8192.0)
 
         def count(e, g, T, op):
             if e == "V":
-                return g.vector.tensor_reduce(T.CNT[:], T.MS[:], AxisListType.X, A_.add)
-            return g.scalar.activation(T.JK[:], T.MS[:], F_.Copy, accum_out=T.CNT[:])
-        O({"V": vt(256, 1), "S": st(256) + 20}, count, [("MS", 0, 256)], [("CNT", 0, 1), ("JK", 0, 256)])
+                return g.vector.tensor_reduce(T.CNT[:], sl(T, mall), AxisListType.X, A_.add)
+            return g.scalar.activation(T.JK[:], sl(T, mall), F_.Copy, accum_out=T.CNT[:])
+        O({"V": vt(256, 1), "S": st(256) + 20}, count, [mall], [("CNT", 0, 1), ("JK", 0, 256)])
         tsc(("OFF", 0, 16), ("IK", 0, 16), ("CNT", 0, 1), None, A_.subtract)
-        gather_tt(("LG", 0, 256), yp(0, 272), ("OFF", 0, 16), ("DIAG", 0, 256), A_.mult)
+        gather_tt(("LG", 0, 256), lw(0, 272), ("OFF", 0, 16), ("DIAG", 0, 256), A_.mult)
         O({"V": vt(256, 1)}, lambda e, g, T, op: g.vector.tensor_tensor_scan(T.LS[:], T.SEG[:], T.LG[:], 0.0, A_.mult, A_.add),
           [("SEG", 0, 256), ("LG", 0, 256)], [("LS", 0, 256)])
-        s = "SEND%d" % t
-        O({"V": vt(16, 1)}, lambda e, g, T, op: g.vector.tensor_scalar(T[s][:], T.LS[:, 15:256:16], YO + 4096.0, sl(T, h), A_.add, A_.mult),
-          [("LS", 0, 256), h], [(s, 0, 16)])
-        snd = O({"G": PRM["SND"]}, None, [(s, 0, 16)], [], send=t, lag=PRM["SND"])
-        plus(("OWN", 0, 16), ("LS", 15, 256), YO, 16)
-        tsc(("THR", 0, 1), h, 16.0 * SC, ("THR", 0, 1), A_.mult, A_.add)
+        s, own = ("SEND%d" % t, 0, 16), ("LS", 15, 256, 16)
+        tsc(s, own, 4096.0, h, A_.add, A_.mult)
+        snd = O({"G": SND}, None, [s], [], send=t, lag=SND)
+
+        def more(e, g, T, op):
+            if e == "V":
+                return g.vector.tensor_scalar(T.THR[:, t + 1:t + 2], sl(T, h), 16.0 * SC, T.THR[:, t:t + 1], A_.mult, A_.add)
+            return g.scalar.activation(T.THR[:, t + 1:t + 2], sl(T, h), F_.Identity, bias=T.THR[:, t:t + 1], scale=16.0 * SC)
+        O({"V": vt(1, 1), "S": st(1)}, more, [h, ("THR", t, t + 1)], [("THR", t + 1, t + 2)])
         return snd
 
     def loop_in(t, snd):
-        q = O({"V": vt(16, 2)}, lambda e, g, T, op: g.vector.tensor_tensor(T.LPI[:], T["LAND%d" % t][:], T.OWN[:], A_.max),
-              [("OWN", 0, 16)], [("LPI", 0, 16)], ext="arr%d" % t)
+        q = O({"V": vt(16, 2)}, lambda e, g, T, op: g.vector.tensor_tensor(T.LPI[:], T["LAND%d" % t][:], T.LS[:, 15:256:16], A_.max),
+              [("LS", 0, 256)], [("LPI", 0, 16)], ext="arr%d" % t)
         q["preds"][snd["i"]] = 1
         tsc(("LPI", 0, 16), ("LPI", 0, 16), 4095, None, A_.bitwise_and)
         copy(("RU", 240, 256), ("LPI", 0, 16))
@@ -457,19 +465,12 @@ def build_ops():
     copy(("RU", 0, 256), ("RI", 0, 256))
     tsc(yr(0, 256), ("RI", 0, 256), -YO, None, A_.add)
     copy(("MU", 0, 256), ("BI", 0, 256))
-    tsc(("YM", 0, 256), ("BI", 0, 256), -YO, None, A_.add)
-    tsc(("TH0", 0, 1), ("TI", 0, 1), float(SC), None, A_.mult)
-    copy(("THR", 0, 1), ("TH0", 0, 1))
-    copy(("EPF", 0, 1), ("EI", 0, 1))
+    tsc(ym(0, 256), ("BI", 0, 256), -YO, None, A_.add)
+    tsc(("THR", 0, 1), ("TI", 0, 1), float(SC), None, A_.mult)
     tsc(("ES", 0, 1), ("EI", 0, 1), 2.0, 1.0, A_.mult, A_.add)
     O({"V": 250}, lambda e, g, T, op: g.vector.reciprocal(T.ES[:], T.ES[:]), [("ES", 0, 1)], [("ES", 0, 1)])
     tsc(("EP", 0, 128), ("IP", 0, 128), ("ES", 0, 1), None, A_.mult)
     tsc(("EN", 0, 128), ("IN", 0, 128), ("ES", 0, 1), None, A_.mult)
-
-    def pieces(t):
-        b = [0] + [x + 2 for x in BNDS[t][1:-1]] + [240]
-        return [("%d%d" % (k, q), x, y) for k in range(NCH) for q, (x, y) in enumerate(cut(b[k], b[k + 1], TBP[t][k]))] + [
-            ("%dL" % (NCH - 1), 240, 256)]
 
     for t in range(RO + 1):
         last = t == RO
@@ -477,11 +478,13 @@ def build_ops():
         pre = "F" if last else ""
         if last:
             cur[0] = "F"
-            plus(("MR", 0, 256), ("YM", 0, 256), YO)
-            tsc(("AC", 0, 1), ("THR", 0, 1), ("TH0", 0, 1), 1.0 / (16 * SC), A_.subtract, A_.mult)
+            tsc(("AC", 0, 1), ("THR", RO, RO + 1), ("THR", 0, 1), 1.0 / (16 * SC), A_.subtract, A_.mult)
             store("ya", ("AC", 0, 1))
+            lin([(("KB0", 0, 256), [("IP", ym(0, 256))])])
+            plus(("MR", 0, 256), ("KB0", 0, 256), YO)
             for x, y in ((0, 240), (240, 256)):
-                plus(("OR", x, y), yr(x, y), YO)
+                lin([(("KB0", 256 + x, 256 + y), [("IP", yr(x, y))])])
+                plus(("OR", x, y), ("KB0", 256 + x, 256 + y), YO)
                 store("yr", ("OR", x, y))
         for k in range(NCH):
             ps = pieces(t)
@@ -490,9 +493,7 @@ def build_ops():
                     continue
                 cur[0] = pre + "R" + i
                 gather(("GR", 16 * ta, 16 * tb), XWIN, ("RU", ta, tb))
-                if j == 0 and not last:
-                    plus(yr(-1, 0), yr(0, 1), 0.0)
-                if not (NA or last):
+                if not last:
                     if tb == 240:
                         continue
                     if tb == 256:
@@ -512,16 +513,18 @@ def build_ops():
             hi = min(16 * b, 4080)
             absdiff(("NW", 16 * a, hi), ("GR", 16 * a, hi), ("GR", 16 * a + 16, hi + 16))
             choose(k, a, b)
-            for q, (x, y) in enumerate(cut(a, b, NSP[t][k])):
+            for q, (x, y) in enumerate(after_choice(t, a, b)):
                 cur[0] = "Q%d%d" % (k, q)
                 necks(x - 16 if x else 0, y - 16, y == 256)
             if b == 256:
                 cur[0] = "O"
                 snd = loops(t)
+            c = 0
             for i, ta, tb in pieces(t + 1)[:-1]:
                 if a < tb + 16 <= b:
                     cur[0] = "S" + i
-                    shift(ta, tb)
+                    shift(k, c, ta, tb)
+                    c += 2 * (tb - ta)
         if not last:
             cur[0] = "I"
             loop_in(t, snd)
@@ -530,228 +533,343 @@ def build_ops():
     return ops
 
 
-def place(ops, before, after, mate, key):
-    LAT, WIN, FILL, HOLD, BOOST = PRM["LAT"], PRM["WIN"], PRM["FILL"], PRM["HOLD"], PRM["BOOST"]
-    n = len(ops)
-    engs = [{op["first"]: op["engs"][op["first"]]} if "first" in op else op["engs"] for op in ops]
-    start, fin, eng, bank = [0.0] * n, [0.0] * n, [None] * n, {}
-    left = [len(x) for x in before]
-    head = {b: a for a, b in mate.items()}
-    key = list(key)
-    free = {e: 0.0 for e in EN}
-    used = [{} for b in BANKS]
-    pool = {b: 0.0 for b in POOL}
-    ready = {i: 0.0 for i in range(n) if left[i] == 0}
+def place(seg, st0, fin, alt, D, key, how):
+    pre, bks, role, mate, LAT = D
+    WIN, FILL, HOLD, BOOST = how
+    st = st0[:]
+    left, after = {}, {i: [] for i in seg}
+    for i in seg:
+        left[i] = 0
+        for p, lag in pre[i]:
+            if p in after:
+                left[i] += 1
+                after[p].append(i)
+    ready = {i: max([fin[p] + lag for p, lag in pre[i]] + [0.0]) for i in seg if left[i] == 0}
+    slot, order, used = {}, [], {}
     while ready:
         found = []
-        opts = [(x, b) for b, x in pool.items() if x is not None]
-        px = min(opts) if opts else None
+        a, b = st[17], st[18]
+        s1 = None if a < 0 and b < 0 else 18 if a < 0 or 0 <= b < a else 17
         for i, t in ready.items():
-            if i in mate:
-                if px is None:
+            if role[i] == 1:
+                if s1 is None:
                     continue
                 j = mate[i]
-                e = min(engs[j])
-                x = free[e] - HOLD - min(engs[i].values()) + (2000.0 if left[j] > 1 else 0.0)
+                e = alt[j][0][0]
+                x = st[e] - HOLD - alt[i][0][1] + (2000.0 if left[j] > 1 else 0.0)
+                kj = key[j] - BOOST
                 for q in ready:
-                    if key[q] < key[j] - BOOST and e in engs[q] and q not in mate:
-                        x += engs[q][e]
-                t = max(t, px[0], x)
+                    if key[q] < kj and alt[q][0][0] == e and role[q] != 1:
+                        x += alt[q][0][1]
+                t = max(t, x, st[s1])
             c = None
-            for e, d in engs[i].items():
-                s = max(free[e], t)
-                for b in ops[i]["bk"]:
-                    for f, x in used[b].items():
-                        if f != e and x > s:
-                            s = x
+            for e, d in alt[i]:
+                s = st[e] if st[e] > t else t
+                for q in bks[i]:
+                    for f in (q, q + 1, q + 2):
+                        if st[f] > s and f != q + e:
+                            s = st[f]
                 if c is None or s + d < c[3]:
                     c = (s, e, i, s + d)
             found.append(c)
         s0, e0 = min(found)[:2]
-        mine = [x for x in found if x[1] == e0 and x[0] <= s0 + (WIN if e0 in "VSP" else 0.0)]
+        mine = [x for x in found if x[1] == e0 and x[0] <= s0 + (WIN if e0 < 3 else 0.0)]
         best = min(mine, key=lambda x: key[x[2]])
-        short = [x for x in mine if x[3] <= best[0] + FILL and x[0] < best[0]]
-        if short:
-            best = min(short, key=lambda x: key[x[2]])
+        if best[0] > s0:
+            short = [x for x in mine if x[3] <= best[0] + FILL and x[0] < best[0]]
+            if short:
+                best = min(short, key=lambda x: key[x[2]])
         s, e, i, f = best
         del ready[i]
-        start[i], fin[i], eng[i] = s, f, e
-        free[e] = s if e == "Y" else f
-        if i in mate:
-            bank[i] = bank[mate[i]] = px[1]
-            pool[px[1]] = None
+        fin[i], used[i] = f, e
+        order.append((s, len(order), i))
+        st[e] = f if e != 4 else s
+        if role[i] == 1:
+            slot[i] = s1
+            st[s1] = -1.0
             key[mate[i]] -= BOOST
-        if i in head:
-            pool[bank[i]] = f + LAT
-        for b in ops[i]["bk"]:
-            used[b][e] = f + LAT
+        elif role[i] == 2:
+            st[slot[mate[i]]] = f + LAT
+        for q in bks[i]:
+            st[q + e] = f + LAT
         for q in after[i]:
             left[q] -= 1
             if left[q] == 0:
-                ready[q] = max(fin[p] + lag for p, lag in before[q])
-    return start, fin, eng
+                ready[q] = max(fin[p] + lag for p, lag in pre[q])
+    return [x[2] for x in sorted(order)], used
 
 
-STEP = 48
-
-
-def run(perm, eng, dur, D, old=None, a=0):
-    pre, bks, role, src, LAT = D
-    n = len(perm)
-    if old is None:
-        fin, why, slot, marks, c = [0.0] * n, [-1] * n, [0] * n, [], 0
-        st, so = [0.0] * 19, [-1] * 19
-    else:
-        c = a // STEP
-        fin, why, slot, marks = old[0][:], old[1][:], old[2][:], old[3][:c]
-        st, so = old[3][c][0][:], old[3][c][1][:]
-    for c in range(c * STEP, n, STEP):
-        marks.append((st[:], so[:]))
-        for i in perm[c:c + STEP]:
-            e = eng[i]
-            t = st[e]
-            w = so[e]
-            for p, lag in pre[i]:
-                x = fin[p] + lag
-                if x > t:
-                    t = x
-                    w = p
-            r = role[i]
-            if r == 1:
+def walk(seg, st, so, fin, eng, dur, D, slot, fixed):
+    pre, bks, role, mate, LAT = D
+    why = {}
+    for i in seg:
+        e = eng[i]
+        t = st[e]
+        w = so[e]
+        for p, lag in pre[i]:
+            x = fin[p] + lag
+            if x > t:
+                t = x
+                w = p
+        r = role[i]
+        if r == 1:
+            if fixed:
+                s = slot[i]
+            else:
                 a, b = st[17], st[18]
                 if a < 0 and b < 0:
                     return None
-                s = 18 if a < 0 or 0 <= b < a else 17
-                if st[s] > t:
-                    t = st[s]
-                    w = so[s]
-                st[s] = -1.0
-                slot[i] = s
-            bk = bks[i]
-            for b in bk:
-                for f in (b, b + 1, b + 2):
-                    if st[f] > t and f != b + e:
-                        t = st[f]
-                        w = so[f]
-            f = t + dur[i]
-            fin[i] = f
-            why[i] = w
-            if e != 4:
-                st[e] = f
-                so[e] = i
-            else:
-                st[e] = t
-            if r == 2:
-                s = slot[i] = slot[src[i]]
-                st[s] = f + LAT
-                so[s] = i
-            for b in bk:
-                st[b + e] = f + LAT
-                so[b + e] = i
-    return fin, why, slot, marks
-
-
-def anneal(ops, D, perm, eng, rng):
-    n = len(ops)
-    moves = PRM["MOVES"]
-    pset = [set(op["preds"]) for op in ops]
-    dur = [ops[i]["engs"][EN[eng[i]]] for i in range(n)]
-    cur = run(perm, eng, dur, D)
-    val = max(cur[0])
-    best = (val, list(perm), list(eng))
-    arcs = None
-    kept = 0
-    for it, (r0, r1, r2, r3) in enumerate(rng.rand(moves, 4).tolist()):
-        temp = PRM["T0"] * (PRM["T1"] / PRM["T0"]) ** (it / moves)
-        if arcs is None:
-            fin, why = cur[0], cur[1]
-            v = fin.index(val)
-            arcs, two = [], []
-            while why[v] >= 0:
-                if len(ops[v]["engs"]) > 1:
-                    two.append(v)
-                if why[v] not in pset[v]:
-                    arcs.append((why[v], v))
-                v = why[v]
-            pos = [0] * n
-            for j, x in enumerate(perm):
-                pos[x] = j
-        if r0 < 0.1 and two:
-            v = two[int(r1 * len(two))]
-            undo = (v, eng[v], dur[v])
-            eng[v] = 1 - eng[v]
-            dur[v] = ops[v]["engs"][EN[eng[v]]]
-            new, a = perm, pos[v]
+                s = slot[i] = 18 if a < 0 or 0 <= b < a else 17
+            if st[s] > t:
+                t = st[s]
+                w = so[s]
+            st[s] = -1.0
+        bk = bks[i]
+        for b in bk:
+            for f in (b, b + 1, b + 2):
+                if st[f] > t and f != b + e:
+                    t = st[f]
+                    w = so[f]
+        f = t + dur[i]
+        fin[i] = f
+        why[i] = w
+        if e != 4:
+            st[e] = f
+            so[e] = i
         else:
-            undo = None
-            u, v = arcs[int(r1 * len(arcs))]
-            a, b = pos[u], pos[v]
-            seg = perm[a:b + 1]
-            if r2 < 0.5:
-                mov, need = {v}, set(pset[v])
-                for y in reversed(seg[:-1]):
-                    if y in need:
-                        mov.add(y)
-                        need |= pset[y]
-                if u in mov:
-                    continue
-                new = perm[:a] + [y for y in seg if y in mov] + [y for y in seg if y not in mov] + perm[b + 1:]
+            st[e] = t
+        if r == 2:
+            s = slot[i] = slot[mate[i]]
+            st[s] = f + LAT
+            so[s] = i
+        for b in bk:
+            st[b + e] = f + LAT
+            so[b + e] = i
+    return why
+
+
+def improve(views, perm, eng, rng, sweeps, lists, moves, hot, cold):
+    ops = views[0][0]
+    pre, bks, role, mate, _ = views[0][1]
+    n, W = len(ops), PRM["WIDTH"]
+    pset = [set(op["preds"]) for op in ops]
+    both = [len(op["engs"]) > 1 for op in ops]
+    succ, durs = [], []
+    for o, D, w in views:
+        succ.append([[] for _ in range(n)])
+        for i in range(n):
+            for p, lag in D[0][i]:
+                succ[-1][p].append((i, lag))
+        durs.append([o[i]["engs"][EN[eng[i]]] for i in range(n)])
+
+    def move(pairs):
+        for i, e in pairs:
+            if eng[i] != e:
+                eng[i] = e
+                for (o, D, w), d in zip(views, durs):
+                    d[i] = o[i]["engs"][EN[e]]
+
+    def whole(p):
+        slot, fins = [0] * n, []
+        for j, (o, D, w) in enumerate(views):
+            fins.append([0.0] * n)
+            if walk(p, [0.0] * 19, [-1] * 19, fins[j], eng, durs[j], D, slot, j > 0) is None:
+                return None
+        return sum(v[2] * max(f) for v, f in zip(views, fins)), fins, slot
+
+    def clear(p, a, b):
+        held = 0
+        for j in range(a, n):
+            held += (role[p[j]] == 1) - (role[p[j]] == 2)
+            if held == 0 and j + 1 >= b:
+                return j + 1
+        return n
+
+    def local(s, ctx, slot):
+        tot, res, swap = 0.0, [], False
+        for j, (st0, so0, fin, D, w, ex, out) in enumerate(ctx):
+            st, so = st0[:], so0[:]
+            why = walk(s, st, so, fin, eng, durs[j], D, slot, j > 0)
+            if why is None:
+                return None
+            if j == 0:
+                swap = st[18] < st[17]
+            if swap:
+                st[17], st[18], so[17], so[18] = st[18], st[17], so[18], so[17]
+            val, end = 0.0, -1
+            for i, x in ex:
+                if fin[i] + x > val:
+                    val, end = fin[i] + x, i
+            for q, x in out:
+                if st[q] + x > val and so[q] in why:
+                    val, end = st[q] + x, so[q]
+            tot += w * val
+            res.append((end, why))
+        return tot, res
+
+    cur = whole(perm)
+    for sw in range(sweeps):
+        a = 0
+        while a < n - 10:
+            b = clear(perm, a, a + (W if a else W - int(rng.rand() * W / 2)))
+            seg, slot, ctx = perm[a:b], cur[2][:], []
+            for j, (o, D, w) in enumerate(views):
+                LAT, dur, fin = D[4], durs[j], cur[1][j][:]
+                st, so = [0.0] * 19, [-1] * 19
+                walk(perm[:a], st, so, fin, eng, dur, D, slot, True)
+                tail, nx, first = [0.0] * n, [0.0] * 19, 17
+                for i in reversed(perm[b:]):
+                    e = eng[i]
+                    x = max([nx[e] if e != 4 else 0.0] + [tail[q] + lag for q, lag in succ[j][i]]
+                            + [nx[f] + LAT for q in bks[i] for f in (q, q + 1, q + 2) if f != q + e]
+                            + ([nx[slot[i]] + LAT] if role[i] == 2 else [])) + dur[i]
+                    tail[i] = nx[e] = x
+                    for q in bks[i]:
+                        nx[q + e] = x
+                    if role[i] == 1:
+                        nx[slot[i]] = x
+                        first = slot[i]
+                out = [(e, nx[e]) for e in range(4)] + [(17, nx[first]), (18, nx[35 - first])]
+                out += [(q + e, max(nx[q + f] for f in range(3) if f != e)) for q in range(5, 17, 3) for e in range(3)]
+                ex = [(i, max([tail[q] + lag for q, lag in succ[j][i] if tail[q] > 0] + [0.0])) for i in seg]
+                ctx.append((st, so, fin, D, w, [x for x in ex if x[1] > 0 or b == n], out))
+            f0, d0 = ctx[0][2], durs[0]
+            val = local(seg, ctx, slot)[0]
+            start = best = (val, seg, [(i, eng[i]) for i in seg])
+            for _ in range(lists):
+                local(seg, ctx, slot)
+                noise = float(rng.choice(PRM["NOISE"][:3]))
+                key = {i: f0[i] - d0[i] + noise * x for i, x in zip(seg, rng.rand(len(seg)).tolist())}
+                alt = {}
+                for i, x in zip(seg, rng.rand(len(seg)).tolist()):
+                    es = [eng[i]] if not both[i] else [eng[i], 1 - eng[i]] if d0[i] < 400 else [eng[i] if x > 0.05 else 1 - eng[i]]
+                    alt[i] = [(e, ops[i]["engs"][EN[e]]) for e in es]
+                new, used = place(seg, ctx[0][0], f0, alt, ctx[0][3], key, [float(rng.choice(PRM[x])) for x in HOW])
+                was = [(i, eng[i]) for i in seg]
+                move(used.items())
+                r = local(new, ctx, slot)
+                if r and r[0] < val + 100.0:
+                    seg, val = new, r[0]
+                    if val < best[0]:
+                        best = (val, seg, list(used.items()))
+                else:
+                    move(was)
+            move(best[2])
+            seg = best[1]
+            loc = local(seg, ctx, slot)
+            val, arcs, kept = loc[0], None, 0
+            for it, (r0, r1, r2, r3) in enumerate(rng.rand(moves, 4).tolist()):
+                if arcs is None:
+                    arcs, two = [], []
+                    for v, why in loc[1]:
+                        while v in why:
+                            if both[v]:
+                                two.append(v)
+                            u = why[v]
+                            if u in why and u not in pset[v]:
+                                arcs.append((u, v))
+                            v = u
+                    if not arcs:
+                        break
+                    pos = {x: j for j, x in enumerate(seg)}
+                undo = None
+                if r0 < 0.1 and two:
+                    undo = two[int(r1 * len(two))]
+                    move([(undo, 1 - eng[undo])])
+                    new = seg
+                else:
+                    u, v = arcs[int(r1 * len(arcs))]
+                    x, y = pos[u], pos[v]
+                    mid = seg[x:y + 1]
+                    if r2 < 0.5:
+                        mov, need = {v}, set(pset[v])
+                        for z in reversed(mid[:-1]):
+                            if z in need:
+                                mov.add(z)
+                                need |= pset[z]
+                        if u in mov:
+                            continue
+                        new = seg[:x] + [z for z in mid if z in mov] + [z for z in mid if z not in mov] + seg[y + 1:]
+                    else:
+                        mov = {u}
+                        for z in mid[1:]:
+                            if pset[z] & mov:
+                                mov.add(z)
+                        if v in mov:
+                            continue
+                        new = seg[:x] + [z for z in mid if z not in mov] + [z for z in mid if z in mov] + seg[y + 1:]
+                r = local(new, ctx, slot)
+                if r and (r[0] <= val or r3 < math.exp((val - r[0]) / (hot * (cold / hot) ** (it / moves)))):
+                    seg, loc, val, arcs = new, r, r[0], None
+                    kept += 1
+                    if kept % 4 == 0:
+                        s2 = sorted(seg, key=lambda i: f0[i] - d0[i])
+                        z = local(s2, ctx, slot)
+                        if z and z[0] <= val:
+                            seg, loc, val = s2, z, z[0]
+                    if val < best[0]:
+                        best = (val, seg, [(i, eng[i]) for i in seg])
+                elif undo is not None:
+                    move([(undo, 1 - eng[undo])])
+            move(best[2])
+            new = perm[:a] + best[1] + perm[b:]
+            r = whole(new)
+            if r and r[0] <= cur[0]:
+                p2 = sorted(new, key=lambda i: r[1][0][i] - d0[i])
+                z = whole(p2)
+                perm, cur = (p2, z) if z and z[0] <= r[0] else (new, r)
             else:
-                mov = {u}
-                for y in seg[1:]:
-                    if pset[y] & mov:
-                        mov.add(y)
-                if v in mov:
-                    continue
-                new = perm[:a] + [y for y in seg if y not in mov] + [y for y in seg if y in mov] + perm[b + 1:]
-        r = run(new, eng, dur, D, cur, a)
-        nv = max(r[0]) if r else None
-        if r and (nv <= val or r3 < math.exp((val - nv) / temp)):
-            perm, cur, val, arcs = new, r, nv, None
-            kept += 1
-            if kept % 8 == 0:
-                p2 = sorted(perm, key=lambda i: r[0][i] - dur[i])
-                z = run(p2, eng, dur, D)
-                if z and max(z[0]) <= val:
-                    perm, cur, val = p2, z, max(z[0])
-            if val < best[0]:
-                best = (val, list(perm), list(eng))
-        elif undo:
-            eng[undo[0]], dur[undo[0]] = undo[1], undo[2]
-    return best
+                move(start[2])
+            a = clear(perm, 0, a + W // 2)
+    return perm, cur
+
+
+def graph(ops, lat, back=False):
+    pre = [[] for _ in ops]
+    for op in ops:
+        for p in op["preds"]:
+            lag = lat + ops[p].get("lag", 0.0)
+            if back:
+                pre[p].append((op["i"], lag))
+            else:
+                pre[op["i"]].append((p, lag))
+    mate = {op["i"]: op["src"]["i"] for op in ops if "src" in op}
+    mate.update({b: a for a, b in mate.items()})
+    role = [(2 if back else 1) if op.get("alloc") else (1 if back else 2) if "src" in op else 0 for op in ops]
+    return pre, [[5 + 3 * b for b in op["bk"]] for op in ops], role, mate, lat
 
 
 def schedule(ops):
     n = len(ops)
-    fw, bw = [[] for _ in range(n)], [[] for _ in range(n)]
-    for op in ops:
-        for p in op["preds"]:
-            lag = PRM["LAT"] + ops[p].get("lag", 0.0)
-            fw[op["i"]].append((p, lag))
-            bw[p].append((op["i"], lag))
-    pair = {op["src"]["i"]: op["i"] for op in ops if "src" in op}
-    back = {b: a for a, b in pair.items()}
-    fa, ba = [[q for q, lag in x] for x in bw], [[q for q, lag in x] for x in fw]
+    D, B = graph(ops, COSTS[0]["LAT"]), graph(ops, COSTS[0]["LAT"], True)
+    alt = [[(EN.index(e), op["engs"][e]) for e in op.get("first", op["engs"])] for op in ops]
     rng = np.random.RandomState(PRM["SEED"])
     best = None
     key = [float(i) for i in range(n)]
     for turn in range(PRM["TRIES"] + 1):
-        for _ in range(2 if turn else PRM["PASSES"]):
-            r = place(ops, fw, fa, pair, [-1.0e9 if op["grp"] == "0" else x for op, x in zip(ops, key)])
-            if best is None or max(r[1]) < max(best[1]):
-                best = r
-            key = [-x for x in place(ops, bw, ba, back, [-x for x in r[1]])[1]]
-        key = [s + PRM["NOISE"] * x for s, x in zip(best[0], rng.rand(n).tolist())]
-    D = (fw, [[5 + 3 * b for b in op["bk"]] for op in ops], [1 if op.get("alloc") else 2 if "src" in op else 0 for op in ops],
-         [op["src"]["i"] if "src" in op else -1 for op in ops], PRM["LAT"])
-    span, order, eng = anneal(ops, D, sorted(range(n), key=lambda i: (best[0][i], i)), [EN.index(e) for e in best[2]], rng)
-    fin, why, slot, marks = run(order, eng, [ops[i]["engs"][EN[eng[i]]] for i in range(n)], D)
+        how = [float(rng.choice(PRM[x])) for x in HOW]
+        for _ in range(2 if turn else 5):
+            fin, rev = [0.0] * n, [0.0] * n
+            order, used = place(range(n), [0.0] * 19, fin, alt, D, [-1.0e9 if op["grp"] == "0" else x for op, x in zip(ops, key)], how)
+            if best is None or max(fin) < max(best[0]):
+                best = (fin, order, used)
+            place(range(n), [0.0] * 19, rev, alt, B, [-x for x in fin], how)
+            key = [-x for x in rev]
+        noise = float(rng.choice(PRM["NOISE"]))
+        key = [best[0][i] - ops[i]["engs"][EN[best[2][i]]] + noise * x for i, x in enumerate(rng.rand(n).tolist())]
+    order, eng = best[1], [best[2][i] for i in range(n)]
+    views = [(ops, D, COSTS[0]["W"])]
+    order, cur = improve(views, order, eng, rng, *PRM["ONE"])
+    for c in COSTS[1:]:
+        o = build_ops(c)
+        views.append((o, graph(o, c["LAT"]), c["W"]))
+    order, cur = improve(views, order, eng, rng, *PRM["ALL"])
     last = {}
     for i in order:
         op = ops[i]
-        op["eng"], op["fin"], op["deps"] = EN[eng[i]], fin[i], list(op["preds"])
+        op["eng"], op["fin"], op["deps"] = EN[eng[i]], cur[1][0][i], list(op["preds"])
         if op.get("alloc"):
-            op["bank"] = POOL[slot[i] - 17]
+            op["bank"] = POOL[cur[2][i] - 17]
             op["deps"] += last.get(op["bank"], [])
         if "src" in op:
             last[op["src"]["bank"]] = [i]
@@ -759,11 +877,11 @@ def schedule(ops):
             d = last.setdefault(b, {})
             op["deps"] += [q for f, q in d.items() if f != eng[i]]
             d[eng[i]] = i
-    return order, span
+    return order, max(cur[1][0])
 
 
 def make_plan():
-    ops = build_ops()
+    ops = build_ops(COSTS[0])
     order, span = schedule(ops)
     know = {e: {} for e in EN}
     cnt = {"V": 0, "S": 0, "P": 0, "G": 0}
@@ -832,10 +950,8 @@ def rank_program(g, core, T, topo):
             t = op["send"]
             dst = T.cores[(rank + 1 + t % (N - 1)) % N]
             rid, pid, _s = topo.addr(dst)
-            mask = 0
-            for x in link(core, dst):
-                mask |= 1 << x
-            g.remote_dma(T["LAND%d" % t][:], T["SEND%d" % t][:], T.sem["arr%d" % t], T.sem["snt%d" % t], pid, rid, mask)
+            g.remote_dma(T["LAND%d" % t][:], T["SEND%d" % t][:], T.sem["arr%d" % t], T.sem["snt%d" % t], pid, rid,
+                         sum(1 << x for x in link(core, dst)))
             continue
         ins = op["fn"](e, g, T, op)
         sem, v = op["tok"]

import math
import numpy as np
from concourse.mybir import AluOpType, AxisListType, ActivationFunctionType

A_ = AluOpType
F_ = ActivationFunctionType
BNDS = [[0, 102, 172, 256], [0, 102, 204, 256], [0, 84, 186, 256], [0, 66, 168, 256], [0, 48, 150, 256]]
NCH = 3
RO = 4
SM = 102
SC = 1024
YO = 2048.0
BIG = 12582912.0
ENGINES = 8
CY = 0.83
PRM = {
    "ONS": ["C10", "C20@3"],
    "ONV": ["FR2L", "R00@0"],
    "END": 24,
    "WIN": [100, 150, 200, 250], "FILL": [100, 150, 200], "HOLD": [700, 1000, 1500], "BOOST": [700, 1000, 2000],
    "TRIES": 50, "NOISE": [500, 1000, 2000, 3000], "SEED": 15, "WIDTH": 70,
    "ONE": (3, 10, 900, 100.0, 12.0), "ALL": (6, 0, 520, 120.0, 15.0),
}
HOW = ("WIN", "FILL", "HOLD", "BOOST")
COSTS = [{"GC": 1.55, "PEC": 0.48, "LAT": 100.0, "FV": 55.0, "FS": 75.0, "SND": 2000.0, "XLD": 6000.0, "W": 0.35},
         {"GC": 1.2, "PEC": 0.5, "LAT": 110.0, "FV": 55.0, "FS": 90.0, "SND": 2300.0, "XLD": 6000.0, "W": 0.12},
         {"GC": 1.8, "PEC": 0.58, "LAT": 70.0, "FV": 55.0, "FS": 70.0, "SND": 1400.0, "XLD": 4200.0, "W": 0.16},
         {"GC": 2.0, "PEC": 0.45, "LAT": 70.0, "FV": 55.0, "FS": 70.0, "SND": 1500.0, "XLD": 4500.0, "W": 0.2},
         {"GC": 1.35, "PEC": 0.44, "LAT": 55.0, "FV": 52.0, "FS": 67.0, "SND": 1300.0, "XLD": 4500.0, "W": 0.22}]
CONST = {"KX": YO + 32.0, "KY": YO, "K1": 2464.0, "K2": 4928.0, "K3": 7392.0}
DIAGS = {"IP": 1.0, "IA": YO + 32.0, "IB": 1152.0, "IW": YO + 1184.0, "IN": -1.0, "IF": 1.0}

SCRATCH = {
    "X": ("sbuf", [128, 4096], "bfloat16"), "RI": ("sbuf", [128, 256], "int32"), "BI": ("sbuf", [128, 256], "int32"),
    "TI": ("sbuf", [128, 1], "int32"), "EI": ("sbuf", [128, 1], "int32"),
    "ES": ("sbuf", [128, 1], "float32"), "THR": ("sbuf", [128, RO + 1], "float32"),
    "AC": ("sbuf", [128, 1], "float32"), "CNT": ("sbuf", [128, 1], "float32"),
    "OR": ("sbuf", [128, 256], "float32"), "OM": ("sbuf", [128, 256], "float32"), "MR": ("sbuf", [128, 256], "float32"),
    "YR": ("sbuf", [128, 520], "float16"), "YM": ("sbuf", [128, 520], "float16"),
    "YP": ("sbuf", [128, 768], "float16"), "LW0": ("sbuf", [128, 272], "float32"), "LW1": ("sbuf", [128, 272], "float32"),
    "RU": ("sbuf", [128, 256], "uint16"), "MU": ("sbuf", [128, 256], "uint16"), "PU": ("sbuf", [128, 256], "uint16"),
    "GR": ("sbuf", [128, 4112], "bfloat16"), "GM": ("sbuf", [128, 4096], "bfloat16"), "GP": ("sbuf", [128, 4096], "bfloat16"),
    "AB": ("sbuf", [128, 3840], "bfloat16"), "NW": ("sbuf", [128, 4096], "bfloat16"),
    "I3": ("sbuf", [128, 4096], "bfloat16"), "NR": ("sbuf", [128, 4096], "bfloat16"),
    "MK": ("sbuf", [128, 768], "bfloat16"), "MA": ("sbuf", [128, 512], "bfloat16"), "M0": ("sbuf", [128, 256], "bfloat16"),
    "MS0": ("sbuf", [128, 512], "bfloat16"), "MS1": ("sbuf", [128, 512], "bfloat16"),
    "ZE": ("sbuf", [128, 256], "bfloat16"), "JK": ("sbuf", [128, 256], "bfloat16"),
    "TG": ("sbuf", [128, 5 * SM], "float16"), "TF": ("sbuf", [128, 5 * SM], "float32"), "CMD": ("sbuf", [128, 256], "float32"),
    "DIAG": ("sbuf", [128, 256], "float32"), "SEG": ("sbuf", [128, 256], "bfloat16"), "IK": ("sbuf", [128, 16], "float32"),
    "PI": ("sbuf", [128, 1], "int32"), "PF": ("sbuf", [128, 1], "float32"), "ZT": ("sbuf", [128, 144], "bfloat16"),
    "ZF": ("sbuf", [128, 128], "float32"), "EP": ("sbuf", [128, 128], "float16"), "EN": ("sbuf", [128, 128], "float16"),
    "OFF": ("sbuf", [128, 16], "uint16"), "LG": ("sbuf", [128, 256], "float32"), "LS": ("sbuf", [128, 256], "float32"),
    "LPI": ("sbuf", [128, 16], "int32"),
    "KB0": ("psum", [128, 512], "float32"), "KB1": ("psum", [128, 512], "float32"), "KB2": ("psum", [128, 512], "float32"),
    "NB": ("psum", [128, 512], "float32"),
    "SB0": ("psum", [128, 1024], "float32"), "SB1": ("psum", [128, 1024], "float32"),
}
for _k in CONST:
    SCRATCH[_k] = ("sbuf", [128, SM + 2], "bfloat16")
for _k in DIAGS:
    SCRATCH[_k] = ("sbuf", [128, 128], "float32" if _k[1] == "F" else "bfloat16")
for _k in range(NCH):
    for _b, _w, _d in (("CI", 4, "int32"), ("CU", 4, "uint16"), ("DS", 64, "bfloat16"), ("DA", 80, "bfloat16"), ("KM", 1, "float32"),
                       ("KI", 1, "int32"), ("MI", 1, "int32"), ("OU", 1, "uint16"), ("EC", 4, "float32")):
        SCRATCH["%s%d" % (_b, _k)] = ("sbuf", [128, _w * SM], _d)
    SCRATCH["PB%d" % _k] = ("sbuf", [128, SM + 2], "int32")
for _k in range(RO):
    SCRATCH["SEND%d" % _k] = ("sbuf", [128, 16], "float32")
    SCRATCH["LAND%d" % _k] = ("sbuf", [128, 16], "float32")
SEMAPHORES = (["qV", "qS", "qP", "qG"] + ["ld" + n for n in ("RI", "BI", "X", "TI", "EI")] + ["st%d" % n for n in range(7)]
              + ["arr%d" % t for t in range(RO)] + ["snt%d" % t for t in range(RO)])
PSUM = [n for n in SCRATCH if SCRATCH[n][0] == "psum"]
WIDE = [n for n in SCRATCH if SCRATCH[n][2] in ("float32", "int32")]
POOL = ["SB0", "SB1"]
BANKS = [b for b in PSUM if b not in POOL]
BW = 1024
EN = "VSPGY"


def after_choice(t, a, b):
    return [(a, b - PRM["END"]), (b - PRM["END"], b)] if t == RO - 1 and b == 256 else [(a, b)]


def pieces(t):
    b = [0] + [x + 2 for x in BNDS[t][1:-1]] + [240]
    return [("%d0" % k, b[k], b[k + 1]) for k in range(NCH)] + [("%dL" % (NCH - 1), 240, 256)]


def sl(T, r):
    return T[r[0]][:, r[1]:r[2]:r[3]] if len(r) > 3 else T[r[0]][:, r[1]:r[2]]


def ln(r):
    return len(range(*r[1:]))


def odd(b, x, y, c=0):
    return (b, c + 2 * x + 1, c + 2 * y, 2)


def even(b, x, y, c=0):
    return (b, c + 2 * x, c + 2 * y - 1, 2)


def third(b, x, y, j):
    return (b, 3 * x + j, 3 * y - 2 + j, 3)


def every(r):
    return (r[0], r[1] - r[3] + 1, r[2])


def build_ops(cost):
    ops = []
    seen = {}
    cur = [""]
    rnd = [0]
    stores = [0]
    PEC, GC, FV, FS, SND = [cost[x] for x in ("PEC", "GC", "FV", "FS", "SND")]

    def on(name):
        return cur[0] in PRM[name] or "%s@%d" % (cur[0], rnd[0]) in PRM[name]

    def O(engs, fn, R, W, **kw):
        op = dict(kw, engs=engs, fn=fn, R=[r[:3] for r in R], W=[r[:3] for r in W], preds={}, i=len(ops), grp=cur[0])
        for rd, lst in ((True, op["R"]), (False, op["W"])):
            for (b, c0, c1) in lst:
                if b == "POOL":
                    continue
                ws, rs = seen.setdefault(b, ([], []))
                for (x0, x1, q) in ws:
                    if x0 < c1 and c0 < x1:
                        op["preds"][q["i"]] = 1
                if not rd:
                    for (x0, x1, q) in rs:
                        if x0 < c1 and c0 < x1:
                            op["preds"][q["i"]] = 1
        for (b, c0, c1) in op["R"]:
            if b != "POOL":
                seen[b][1].append((c0, c1, op))
        for (b, c0, c1) in op["W"]:
            if b != "POOL":
                ws, rs = seen[b]
                ws[:] = [w for w in ws if not (c0 <= w[0] and w[1] <= c1)] + [(c0, c1, op)]
                rs[:] = [w for w in rs if not (c0 <= w[0] and w[1] <= c1) or w[2] is op]
        op["preds"].pop(op["i"], None)
        ops.append(op)
        return op

    def vt(n, c):
        return FV + CY * max(64, n * c)

    def st(n):
        return FS + CY * n

    def tt(o, a, b, alu):
        cost = 1 if (a[0] in PSUM or b[0] in PSUM) else 2
        return O({"V": vt(ln(o), cost)}, lambda e, g, T, op: g.vector.tensor_tensor(sl(T, o), sl(T, a), sl(T, b), alu), [a, b], [o])

    def tsc(o, a, s1, s2, op0, op1=None):
        cost = 1 if (o[0] in WIDE or a[0] in WIDE) else 0.5

        def fn(e, g, T, op):
            v1 = sl(T, s1) if isinstance(s1, tuple) else s1
            v2 = sl(T, s2) if isinstance(s2, tuple) else s2
            if op1 is None:
                return g.vector.tensor_scalar(sl(T, o), sl(T, a), v1, None, op0)
            return g.vector.tensor_scalar(sl(T, o), sl(T, a), v1, v2, op0, op1)
        return O({"V": vt(ln(o), cost)}, fn, [a] + [s for s in (s1, s2) if isinstance(s, tuple)], [o])

    def copy(o, a):
        return O({"V": vt(ln(o), 1)}, lambda e, g, T, op: g.vector.tensor_copy(sl(T, o), sl(T, a)), [a], [o])

    def plus(o, a, add):
        def fn(e, g, T, op):
            if e == "V":
                return g.vector.tensor_scalar(sl(T, o), sl(T, a), add, None, A_.add)
            return g.scalar.activation(sl(T, o), sl(T, a), F_.Copy, bias=add)
        return O({"V": vt(ln(o), 1), "S": st(ln(o))}, fn, [a], [o])

    def over(o, a, limit, scale=1.0, only=None):
        def fn(e, g, T, op):
            if e == "V":
                return g.vector.tensor_scalar(sl(T, o), sl(T, a), limit, None, A_.is_gt)
            return g.scalar.activation(sl(T, o), sl(T, a), F_.Sigmoid, bias=-limit * scale, scale=scale)
        return O(only or {"V": vt(ln(o), 1), "S": st(ln(o))}, fn, [a], [o])

    def memset(o, v):
        return O({"V": vt(ln(o), 0.5)}, lambda e, g, T, op: g.vector.memset(sl(T, o), v), [], [o])

    def gather(o, win, off):
        def fn(e, g, T, op):
            src = sl(T, win).indirect(sl(T, off))
            if e == "V":
                return g.vector.tensor_copy(sl(T, o), src)
            return g.scalar.activation(sl(T, o), src, F_.Copy)
        O({"V": 50 + GC * CY * ln(o), "S": 65 + GC * CY * ln(o)}, fn, [win, off], [o], first="V" if on("ONV") else "S")

    def gather_tt(o, win, off, b, alu):
        O({"V": 50 + GC * CY * ln(o)}, lambda e, g, T, op: g.vector.tensor_tensor(
            sl(T, o), sl(T, win).indirect(sl(T, off)), sl(T, b), alu), [win, off, b], [o])

    def lin(sums):
        def fn(e, g, T, op):
            r = None
            for o, terms in sums:
                for j, (w, x) in enumerate(terms):
                    r = g.tensor.matmul(sl(T, o), T[w][:], sl(T, x), j == 0, j == len(terms) - 1)
            return r
        ns = 30 + sum(PEC * max(64, ln(o)) * (4 if w in WIDE else 1) for o, terms in sums for w, x in terms)
        rd = [x for o, terms in sums for w, x in terms] + [(w, 0, 128) for o, terms in sums for w, x in terms]
        return O({"P": ns}, fn, rd, [o for o, terms in sums])

    def diff(o, a, b, wp, wn, engs, read):
        tot = o[2] - o[1]
        w = -(-tot // ((tot + BW - 1) // BW))
        w = -(-w // 32) * 32
        for c in range(0, tot, w):
            m = min(w, tot - c)
            o1, a1, b1 = [(x[0], x[1] + c, x[1] + c + m) for x in (o, a, b)]

            def sub(e, g, T, op, a1=a1, b1=b1, m=m):
                r = None
                for x in range(0, m, 512):
                    y = min(x + 512, m)
                    d = T[op["bank"]][:, x:y]
                    g.tensor.matmul(d, T[wp][:], T[a1[0]][:, a1[1] + x:a1[1] + y], True, False)
                    r = g.tensor.matmul(d, T[wn][:], T[b1[0]][:, b1[1] + x:b1[1] + y], False, True)
                return r
            q = O({"P": 2 * PEC * max(64, m) + 30}, sub, [a1, b1, (wp, 0, 128), (wn, 0, 128)], [("POOL", 0, m)], alloc=True)
            r = O(engs(m), lambda e, g, T, op, o1=o1, m=m: read(g, sl(T, o1), T[op["src"]["bank"]][:, 0:m]),
                  [("POOL", 0, m)], [o1], src=q)
            r["preds"][q["i"]] = 1

    def absdiff(o, a, b):
        diff(o, a, b, "IP", "IN", lambda m: {"S": st(m)}, lambda g, x, y: g.scalar.activation(x, y, F_.Abs))

    def within(o, a, b):
        diff(o, a, b, "EP", "EN", lambda m: {"V": vt(m, 1)},
             lambda g, x, y: g.vector.tensor_scalar(x, y, BIG, BIG, A_.add, A_.is_equal))

    def stage_sum(o, a, tag=None):
        def fn(e, g, T, op):
            d = sl(T, o)
            r = None
            if tag:
                g.tensor.matmul(d, T.IP[:], sl(T, tag), True, False)
            for p in range(16):
                r = g.tensor.matmul(d, T.ZT[:, 15 - p:143 - p], T[a[0]][:, a[1] + p:a[2]:16], not tag and p == 0, p == 15)
            return r
        O({"P": (17 if tag else 16) * PEC * max(64, ln(o)) + 30}, fn, [a, ("ZT", 0, 144)] + ([tag, ("IP", 0, 128)] if tag else []), [o])

    def pick(o, mask, d, names):
        O({"V": vt(ln(every(o)), 1)}, lambda e, g, T, op: g.vector.tensor_tensor_scan(
            sl(T, every(o)), sl(T, every(mask)), sl(T, every(d)), 0.0, A_.mult, A_.add), [every(mask), every(d)], [every(o)])
        tsc(names, o, YO, None, A_.add)

    def load(dst, src, w, ns):
        O({"Y": ns}, lambda e, g, T, op: g.sync.dma_start(T[dst][:], T[src][:]), [], [(dst, 0, w)], sem="ld" + dst)

    def store(dst, r):
        whole = ln(r) == SCRATCH[r[0]][1][1]
        O({"Y": 1300.0 + 2 * ln(r)}, lambda e, g, T, op: g.sync.dma_start(T[dst][:] if whole else T[dst][:, r[1]:r[2]], sl(T, r)),
          [r], [], sem="st%d" % stores[0])
        stores[0] += 1
    load("RI", "riv", 256, 1500)
    load("X", "flood", 4096, cost.get("XLD", 6000.0))
    load("BI", "bord", 256, 2000)
    load("TI", "th", 1, 2000)
    load("EI", "eps", 1, 2000)

    def sel(o, a, pattern, cmp, fill, base, cm):
        O({"G": 170 + 2 * CY * ln(o)}, lambda e, g, T, op: g.affine_select(sl(T, o), sl(T, a), pattern, cmp, fill, base, cm), [a], [o])

    def iota(r, pattern, base, cm):
        kw = {} if r[0] == "PI" else {"allow_small_or_imprecise_dtypes": True}
        O({"G": 130 + 2 * CY * ln(r)}, lambda e, g, T, op: g.iota(sl(T, r), pattern, base, cm, **kw), [], [r])
    cur[0] = "0"
    iota(("CMD", 0, 256), [[0, 16], [1, 16]], 0, 0)
    over(("SEG", 0, 256), ("CMD", 0, 256), 0.5, 1024.0, {"S": st(256) + 1300})
    cur[0] = ""
    memset(("ZE", 0, 256), 0.0)
    memset(("ZF", 0, 128), 0.0)
    for b in DIAGS:
        sel((b, 0, 128), ("ZF" if b in WIDE else "ZE", 0, 128), [[-1, 128]], A_.not_equal, DIAGS[b], 0, 1)
    for b in CONST:
        iota((b, 0, SM + 2), [[0, SM + 2]], int(CONST[b]), 0)
    zt = ("ZT", 0, 144)
    iota(zt, [[0, 144]], SC, 0)
    sel(zt, zt, [[0, 9], [1, 16]], A_.is_equal, 0.0, -15, 0)
    sel(zt, zt, [[-16, 9], [0, 16]], A_.is_ge, 0.0, 0, 1)
    sel(zt, zt, [[16, 9], [0, 16]], A_.is_ge, 0.0, 15, -1)
    iota(("PI", 0, 1), [[0, 1]], 0, 1)
    iota(("TF", 0, 5 * SM), [[1, 5 * SM]], 0, 0)
    copy(("TG", 0, 5 * SM), ("TF", 0, 5 * SM))
    iota(("IK", 0, 16), [[1, 16]], 256, 0)
    tsc(("PI", 0, 1), ("PI", 0, 1), 15, None, A_.bitwise_and)
    copy(("PF", 0, 1), ("PI", 0, 1))
    tsc(("DIAG", 0, 256), ("CMD", 0, 256), ("PF", 0, 1), None, A_.is_equal)
    for r in (("GR", 4096, 4112), ("NW", 4080, 4096), ("MK", 0, 768), ("M0", 240, 256), ("MS0", 0, 512), ("MA", 0, 512),
              ("MS1", 0, 512)):
        iota(r, [[0, ln(r)]], 0, 0)
    copy(("YR", 512, 520), ("ZE", 0, 8))
    copy(("YM", 512, 520), ("ZE", 0, 8))

    XWIN = ("X", 0, 4096)

    def yr(a, b):
        return odd("YR", a, b)

    def ym(a, b):
        return odd("YM", a, b)

    def yp(a, b):
        return third("YP", a, b, 2)

    def lw(a, b):
        return ("LW%d" % (rnd[0] % 2), a, b)

    def ms(a, b):
        return odd("MS%d" % (rnd[0] % 2), a, b)

    def accretion(ta, tb, last):
        gr, gm, i3 = [(b, 16 * ta, 16 * tb) for b in ("GR", "GM", "I3")]
        within(i3, gr, gm)
        stage_sum(("NB", ta, tb), i3)
        ma, terms = odd("MA", ta, tb), [("IP", yr(ta, tb)), ("IN", ym(ta, tb))]
        over(ma, ("NB", ta, tb), 8.5 * SC)
        if last:
            dm = ("NB", 256 + ta, 256 + tb)
            lin([(dm, terms)])
            tt(dm, dm, ma, A_.mult)
            tt(("OM", ta, tb), dm, ("MR", ta, tb), A_.add)
            store("ym", ("OM", ta, tb))
        else:
            lin([(even("NB", 0, tb - ta, 256), terms), (odd("NB", 0, tb - ta, 256), [("IP", ym(ta, tb))])])
            pick(ym(ta, tb), ma, odd("NB", 0, tb - ta, 256), ("MU", ta, tb))

    def lists(k, t, a, b):
        n = b - a
        ci, kb, pb = "CI%d" % k, "KB%d" % k, "PB%d" % k
        c = [("IP", ("K%d" % t, 0, n))] if t else []
        cur[0] = "L%d0" % k
        z = 0 if a else 1
        lin([((kb, 4 * n + z, 5 * n + 1), [("IP", yr(a - 1 + z, b)), ("IP", ("KX", 0, n + 1 - z))]),
             ((kb, n + z, 2 * n), [("IA", yr(a - 1 + z, b - 1)), ("IB", yr(a + z, b))] + [(w, (x[0], 0, n - z)) for w, x in c]),
             ((kb, 2 * n, 3 * n), [("IW", yr(a, b))] + c), ((kb, 3 * n, 4 * n), [("IW", yr(a, b))] + c)]
            + ([((kb, 4 * n, 4 * n + 1), [("IP", yr(0, 1)), ("IP", ("KX", 0, 1))]),
                ((kb, n, n + 1), [("IW", yr(0, 1))] + [(w, (x[0], 0, 1)) for w, x in c])] if z else []))
        for half in range(2):
            cur[0] = "L%d%d" % (k, half)
            r = (ci, 2 * n * half, 2 * n * half + 2 * n)
            if half == 0:
                tt((pb, 0, n + 1), (kb, 4 * n, 5 * n + 1), yr(a, b + 1), A_.mult)
                for q in range(2):
                    tt((ci, q * n, q * n + n), (kb, n + q * n, 2 * n + q * n), (pb, q, q + n), A_.add)
            else:
                for q in range(2):
                    tt((ci, 2 * n + q * n, 3 * n + q * n), (kb, 4 * n + 1, 5 * n + 1), ym(a + q, b + q), A_.mult)
                tt(r, (kb, 2 * n, 4 * n), r, A_.add)
            tsc(r, r, 5, 4095, A_.arith_shift_right, A_.bitwise_and)
            copy(("CU%d" % k,) + r[1:], r)

    def keys(k, a, b):
        n = b - a
        nxt = ("GR", 16 * a + 16, 16 * b + 16)
        for m in (4, 0, 1, 2, 3):
            cur[0] = "C%d%d" % (k, m)
            da, ds = [("%s%d" % (x, k), 16 * n * m, 16 * n * (m + 1)) for x in ("DA", "DS")]
            off = ("CU%d" % k, m * n, m * n + n)
            if m == 4:
                absdiff(da, ("GM", 16 * a, 16 * b), nxt)
            elif on("ONS"):
                gather(ds, XWIN, off)
                absdiff(da, ds, nxt)
            else:
                gather_tt(ds, XWIN, off, nxt, A_.subtract)
                O({"S": st(16 * n)}, lambda e, g, T, op, da=da, ds=ds: g.scalar.activation(sl(T, da), sl(T, ds), F_.Abs), [ds], [da])
            stage_sum(("KB%d" % k, m * n, m * n + n), da, ("TG", m * n, m * n + n))

    def choose(k, a, b):
        n = b - a
        kb, ec = "KB%d" % k, "EC%d" % k
        key = [(kb, m * n, m * n + n) for m in range(5)]
        cur[0] = "K%d" % k
        km, ki = ("KM%d" % k, 0, n), ("KI%d" % k, 0, n)
        plus(km, key[0], 0.0)
        for m in (1, 4, 2, 3):
            tt(ki if m == 3 else km, key[m], km, A_.min)
        tsc(("MI%d" % k, 0, n), ki, SC - 1, None, A_.bitwise_and)
        tsc(("OU%d" % k, 0, n), ("MI%d" % k, 0, n), 16.0, ("PF", 0, 1), A_.mult, A_.add)
        cur[0] = "D%d" % k
        tt(third("MK", a, b, 1), key[4], ki, A_.is_equal)
        for m in range(4):
            tt(key[m], key[m], ki, A_.is_equal)
        tt((ec, 0, 4 * n), (kb, 0, 4 * n), ("CI%d" % k, 0, 4 * n), A_.mult)
        lin([(third(kb, 0, n, 0), [("IP", ym(a, b)), ("IP", ("KY", 0, n))]), (third(kb, 0, n, 2), [("IP", yr(a, b))]),
             (third(kb, 0, n, 1), [("IN", yr(a, b)), ("IN", ("KY", 0, n))] + [("IF", (ec, m * n, m * n + n)) for m in range(4)])])
        ps = after_choice(rnd[0], a, b)
        for q, (x, y) in enumerate(ps):
            cur[0] = "E%d%d" % (k, q)
            nr = ("NR", 16 * x, 16 * y)
            gather_tt(nr, ("DA%d" % k, 0, 80 * n), ("OU%d" % k, x - a, y - a), ("NW", 16 * x, 16 * y), A_.is_lt)
            stage_sum(("NB", x, y), nr)
            over(third("MK", x, y, 2), ("NB", x, y), 8.5 * SC)
        for q, (x, y) in enumerate(ps):
            cur[0] = "P%d%d" % (k, q)
            pick(yp(x, y), third("MK", x, y, 2), third(kb, x - a, y - a, 2), ("PU", x, y))
            gather(("GP", 16 * x, 16 * y), XWIN, ("PU", x, y))
            lin([((kb, 320 + x - a, 320 + y - a), [("IP", yp(x, y))])])
            plus(lw(x, y), (kb, 320 + x - a, 320 + y - a), YO)

    def necks(na, nb, last):
        ab, thr = ("AB", 16 * na, 16 * nb), ("THR", rnd[0], rnd[0] + 1)
        absdiff(ab, ("GP", 16 * na, 16 * nb), ("GP", 16 * na + 256, 16 * nb + 256))
        stage_sum(("NB", na, nb), ab)

        def under(e, g, T, op):
            if e == "V":
                return g.vector.tensor_scalar(T.M0[:, na:nb], T.NB[:, na:nb], sl(T, thr), None, A_.is_lt)
            return g.scalar.activation(T.M0[:, na:nb], T.NB[:, na:nb], F_.Sign, bias=sl(T, thr), scale=-1.0)
        O({"V": vt(nb - na, 1), "S": st(nb - na)}, under, [("NB", na, nb), thr], [("M0", na, nb)])
        hi = 255 if last else nb
        old, new = ms(na, na + 1), ms(na + 1, hi + 1)
        O({"V": vt(hi - na, 0.5)}, lambda e, g, T, op: g.vector.tensor_tensor_scan(
            sl(T, new), T.M0[:, na:hi], T.ZE[:, na:hi], sl(T, old), A_.max, A_.max), [("M0", na, hi), ("ZE", na, hi), old], [new])

    def shift(k, c, ta, tb):
        kb, n = "KB%d" % k, tb - ta
        lin([(even(kb, 0, n, c), [("IP", yp(ta + 16, tb + 16)), ("IN", yp(ta, tb))]), (odd(kb, 0, n, c), [("IP", yp(ta, tb))])])
        pick(yr(ta, tb), ms(ta, tb), odd(kb, 0, n, c), ("RU", ta, tb))

    def loops(t):
        h, mall = ms(255, 256), ms(0, 256)
        plus(lw(256, 272), lw(240, 256), 8192.0)

        def count(e, g, T, op):
            if e == "V":
                return g.vector.tensor_reduce(T.CNT[:], sl(T, mall), AxisListType.X, A_.add)
            return g.scalar.activation(T.JK[:], sl(T, mall), F_.Copy, accum_out=T.CNT[:])
        O({"V": vt(256, 1), "S": st(256) + 20}, count, [mall], [("CNT", 0, 1), ("JK", 0, 256)])
        tsc(("OFF", 0, 16), ("IK", 0, 16), ("CNT", 0, 1), None, A_.subtract)
        gather_tt(("LG", 0, 256), lw(0, 272), ("OFF", 0, 16), ("DIAG", 0, 256), A_.mult)
        O({"V": vt(256, 1)}, lambda e, g, T, op: g.vector.tensor_tensor_scan(T.LS[:], T.SEG[:], T.LG[:], 0.0, A_.mult, A_.add),
          [("SEG", 0, 256), ("LG", 0, 256)], [("LS", 0, 256)])
        s, own = ("SEND%d" % t, 0, 16), ("LS", 15, 256, 16)
        tsc(s, own, 4096.0, h, A_.add, A_.mult)
        snd = O({"G": SND}, None, [s], [], send=t, lag=SND)

        def more(e, g, T, op):
            if e == "V":
                return g.vector.tensor_scalar(T.THR[:, t + 1:t + 2], sl(T, h), 16.0 * SC, T.THR[:, t:t + 1], A_.mult, A_.add)
            return g.scalar.activation(T.THR[:, t + 1:t + 2], sl(T, h), F_.Identity, bias=T.THR[:, t:t + 1], scale=16.0 * SC)
        O({"V": vt(1, 1), "S": st(1)}, more, [h, ("THR", t, t + 1)], [("THR", t + 1, t + 2)])
        return snd

    def loop_in(t, snd):
        q = O({"V": vt(16, 2)}, lambda e, g, T, op: g.vector.tensor_tensor(T.LPI[:], T["LAND%d" % t][:], T.LS[:, 15:256:16], A_.max),
              [("LS", 0, 256)], [("LPI", 0, 16)], ext="arr%d" % t)
        q["preds"][snd["i"]] = 1
        tsc(("LPI", 0, 16), ("LPI", 0, 16), 4095, None, A_.bitwise_and)
        copy(("RU", 240, 256), ("LPI", 0, 16))
        tsc(yr(240, 256), ("LPI", 0, 16), -YO, None, A_.add)

    copy(("RU", 0, 256), ("RI", 0, 256))
    tsc(yr(0, 256), ("RI", 0, 256), -YO, None, A_.add)
    copy(("MU", 0, 256), ("BI", 0, 256))
    tsc(ym(0, 256), ("BI", 0, 256), -YO, None, A_.add)
    tsc(("THR", 0, 1), ("TI", 0, 1), float(SC), None, A_.mult)
    tsc(("ES", 0, 1), ("EI", 0, 1), 2.0, 1.0, A_.mult, A_.add)
    O({"V": 250}, lambda e, g, T, op: g.vector.reciprocal(T.ES[:], T.ES[:]), [("ES", 0, 1)], [("ES", 0, 1)])
    tsc(("EP", 0, 128), ("IP", 0, 128), ("ES", 0, 1), None, A_.mult)
    tsc(("EN", 0, 128), ("IN", 0, 128), ("ES", 0, 1), None, A_.mult)

    for t in range(RO + 1):
        last = t == RO
        rnd[0] = t
        pre = "F" if last else ""
        if last:
            cur[0] = "F"
            tsc(("AC", 0, 1), ("THR", RO, RO + 1), ("THR", 0, 1), 1.0 / (16 * SC), A_.subtract, A_.mult)
            store("ya", ("AC", 0, 1))
            lin([(("KB0", 0, 256), [("IP", ym(0, 256))])])
            plus(("MR", 0, 256), ("KB0", 0, 256), YO)
            for x, y in ((0, 240), (240, 256)):
                lin([(("KB0", 256 + x, 256 + y), [("IP", yr(x, y))])])
                plus(("OR", x, y), ("KB0", 256 + x, 256 + y), YO)
                store("yr", ("OR", x, y))
        for k in range(NCH):
            ps = pieces(t)
            for j, (i, ta, tb) in enumerate(ps):
                if i[0] != str(k):
                    continue
                cur[0] = pre + "R" + i
                gather(("GR", 16 * ta, 16 * tb), XWIN, ("RU", ta, tb))
                if not last:
                    if tb == 240:
                        continue
                    if tb == 256:
                        ta = ps[j - 1][1]
                if t:
                    cur[0] = pre + "A" + i
                    accretion(ta, tb, last)
                if not last:
                    cur[0] = "M" + i
                    gather(("GM", 16 * ta, 16 * tb), XWIN, ("MU", ta, tb))
            if last:
                continue
            a, b = BNDS[t][k:k + 2]
            lists(k, t, a, b)
            keys(k, a, b)
            cur[0] = "N%d" % k
            hi = min(16 * b, 4080)
            absdiff(("NW", 16 * a, hi), ("GR", 16 * a, hi), ("GR", 16 * a + 16, hi + 16))
            choose(k, a, b)
            for q, (x, y) in enumerate(after_choice(t, a, b)):
                cur[0] = "Q%d%d" % (k, q)
                necks(x - 16 if x else 0, y - 16, y == 256)
            if b == 256:
                cur[0] = "O"
                snd = loops(t)
            c = 0
            for i, ta, tb in pieces(t + 1)[:-1]:
                if a < tb + 16 <= b:
                    cur[0] = "S" + i
                    shift(k, c, ta, tb)
                    c += 2 * (tb - ta)
        if not last:
            cur[0] = "I"
            loop_in(t, snd)
    for op in ops:
        op["bk"] = sorted({BANKS.index(r[0]) for r in op["R"] + op["W"] if r[0] in BANKS})
    return ops


def place(seg, st0, fin, alt, D, key, how):
    pre, bks, role, mate, LAT = D
    WIN, FILL, HOLD, BOOST = how
    st = st0[:]
    left, after = {}, {i: [] for i in seg}
    for i in seg:
        left[i] = 0
        for p, lag in pre[i]:
            if p in after:
                left[i] += 1
                after[p].append(i)
    ready = {i: max([fin[p] + lag for p, lag in pre[i]] + [0.0]) for i in seg if left[i] == 0}
    slot, order, used = {}, [], {}
    while ready:
        found = []
        a, b = st[17], st[18]
        s1 = None if a < 0 and b < 0 else 18 if a < 0 or 0 <= b < a else 17
        for i, t in ready.items():
            if role[i] == 1:
                if s1 is None:
                    continue
                j = mate[i]
                e = alt[j][0][0]
                x = st[e] - HOLD - alt[i][0][1] + (2000.0 if left[j] > 1 else 0.0)
                kj = key[j] - BOOST
                for q in ready:
                    if key[q] < kj and alt[q][0][0] == e and role[q] != 1:
                        x += alt[q][0][1]
                t = max(t, x, st[s1])
            c = None
            for e, d in alt[i]:
                s = st[e] if st[e] > t else t
                for q in bks[i]:
                    for f in (q, q + 1, q + 2):
                        if st[f] > s and f != q + e:
                            s = st[f]
                if c is None or s + d < c[3]:
                    c = (s, e, i, s + d)
            found.append(c)
        s0, e0 = min(found)[:2]
        mine = [x for x in found if x[1] == e0 and x[0] <= s0 + (WIN if e0 < 3 else 0.0)]
        best = min(mine, key=lambda x: key[x[2]])
        if best[0] > s0:
            short = [x for x in mine if x[3] <= best[0] + FILL and x[0] < best[0]]
            if short:
                best = min(short, key=lambda x: key[x[2]])
        s, e, i, f = best
        del ready[i]
        fin[i], used[i] = f, e
        order.append((s, len(order), i))
        st[e] = f if e != 4 else s
        if role[i] == 1:
            slot[i] = s1
            st[s1] = -1.0
            key[mate[i]] -= BOOST
        elif role[i] == 2:
            st[slot[mate[i]]] = f + LAT
        for q in bks[i]:
            st[q + e] = f + LAT
        for q in after[i]:
            left[q] -= 1
            if left[q] == 0:
                ready[q] = max(fin[p] + lag for p, lag in pre[q])
    return [x[2] for x in sorted(order)], used


def walk(seg, st, so, fin, eng, dur, D, slot, fixed):
    pre, bks, role, mate, LAT = D
    why = {}
    for i in seg:
        e = eng[i]
        t = st[e]
        w = so[e]
        for p, lag in pre[i]:
            x = fin[p] + lag
            if x > t:
                t = x
                w = p
        r = role[i]
        if r == 1:
            if fixed:
                s = slot[i]
            else:
                a, b = st[17], st[18]
                if a < 0 and b < 0:
                    return None
                s = slot[i] = 18 if a < 0 or 0 <= b < a else 17
            if st[s] > t:
                t = st[s]
                w = so[s]
            st[s] = -1.0
        bk = bks[i]
        for b in bk:
            for f in (b, b + 1, b + 2):
                if st[f] > t and f != b + e:
                    t = st[f]
                    w = so[f]
        f = t + dur[i]
        fin[i] = f
        why[i] = w
        if e != 4:
            st[e] = f
            so[e] = i
        else:
            st[e] = t
        if r == 2:
            s = slot[i] = slot[mate[i]]
            st[s] = f + LAT
            so[s] = i
        for b in bk:
            st[b + e] = f + LAT
            so[b + e] = i
    return why


def improve(views, perm, eng, rng, sweeps, lists, moves, hot, cold):
    ops = views[0][0]
    pre, bks, role, mate, _ = views[0][1]
    n, W = len(ops), PRM["WIDTH"]
    pset = [set(op["preds"]) for op in ops]
    both = [len(op["engs"]) > 1 for op in ops]
    succ, durs = [], []
    for o, D, w in views:
        succ.append([[] for _ in range(n)])
        for i in range(n):
            for p, lag in D[0][i]:
                succ[-1][p].append((i, lag))
        durs.append([o[i]["engs"][EN[eng[i]]] for i in range(n)])

    def move(pairs):
        for i, e in pairs:
            if eng[i] != e:
                eng[i] = e
                for (o, D, w), d in zip(views, durs):
                    d[i] = o[i]["engs"][EN[e]]

    def whole(p):
        slot, fins = [0] * n, []
        for j, (o, D, w) in enumerate(views):
            fins.append([0.0] * n)
            if walk(p, [0.0] * 19, [-1] * 19, fins[j], eng, durs[j], D, slot, j > 0) is None:
                return None
        return sum(v[2] * max(f) for v, f in zip(views, fins)), fins, slot

    def clear(p, a, b):
        held = 0
        for j in range(a, n):
            held += (role[p[j]] == 1) - (role[p[j]] == 2)
            if held == 0 and j + 1 >= b:
                return j + 1
        return n

    def local(s, ctx, slot):
        tot, res, swap = 0.0, [], False
        for j, (st0, so0, fin, D, w, ex, out) in enumerate(ctx):
            st, so = st0[:], so0[:]
            why = walk(s, st, so, fin, eng, durs[j], D, slot, j > 0)
            if why is None:
                return None
            if j == 0:
                swap = st[18] < st[17]
            if swap:
                st[17], st[18], so[17], so[18] = st[18], st[17], so[18], so[17]
            val, end = 0.0, -1
            for i, x in ex:
                if fin[i] + x > val:
                    val, end = fin[i] + x, i
            for q, x in out:
                if st[q] + x > val and so[q] in why:
                    val, end = st[q] + x, so[q]
            tot += w * val
            res.append((end, why))
        return tot, res

    cur = whole(perm)
    for sw in range(sweeps):
        a = 0
        while a < n - 10:
            b = clear(perm, a, a + (W if a else W - int(rng.rand() * W / 2)))
            seg, slot, ctx = perm[a:b], cur[2][:], []
            for j, (o, D, w) in enumerate(views):
                LAT, dur, fin = D[4], durs[j], cur[1][j][:]
                st, so = [0.0] * 19, [-1] * 19
                walk(perm[:a], st, so, fin, eng, dur, D, slot, True)
                tail, nx, first = [0.0] * n, [0.0] * 19, 17
                for i in reversed(perm[b:]):
                    e = eng[i]
                    x = max([nx[e] if e != 4 else 0.0] + [tail[q] + lag for q, lag in succ[j][i]]
                            + [nx[f] + LAT for q in bks[i] for f in (q, q + 1, q + 2) if f != q + e]
                            + ([nx[slot[i]] + LAT] if role[i] == 2 else [])) + dur[i]
                    tail[i] = nx[e] = x
                    for q in bks[i]:
                        nx[q + e] = x
                    if role[i] == 1:
                        nx[slot[i]] = x
                        first = slot[i]
                out = [(e, nx[e]) for e in range(4)] + [(17, nx[first]), (18, nx[35 - first])]
                out += [(q + e, max(nx[q + f] for f in range(3) if f != e)) for q in range(5, 17, 3) for e in range(3)]
                ex = [(i, max([tail[q] + lag for q, lag in succ[j][i] if tail[q] > 0] + [0.0])) for i in seg]
                ctx.append((st, so, fin, D, w, [x for x in ex if x[1] > 0 or b == n], out))
            f0, d0 = ctx[0][2], durs[0]
            val = local(seg, ctx, slot)[0]
            start = best = (val, seg, [(i, eng[i]) for i in seg])
            for _ in range(lists):
                local(seg, ctx, slot)
                noise = float(rng.choice(PRM["NOISE"][:3]))
                key = {i: f0[i] - d0[i] + noise * x for i, x in zip(seg, rng.rand(len(seg)).tolist())}
                alt = {}
                for i, x in zip(seg, rng.rand(len(seg)).tolist()):
                    es = [eng[i]] if not both[i] else [eng[i], 1 - eng[i]] if d0[i] < 400 else [eng[i] if x > 0.05 else 1 - eng[i]]
                    alt[i] = [(e, ops[i]["engs"][EN[e]]) for e in es]
                new, used = place(seg, ctx[0][0], f0, alt, ctx[0][3], key, [float(rng.choice(PRM[x])) for x in HOW])
                was = [(i, eng[i]) for i in seg]
                move(used.items())
                r = local(new, ctx, slot)
                if r and r[0] < val + 100.0:
                    seg, val = new, r[0]
                    if val < best[0]:
                        best = (val, seg, list(used.items()))
                else:
                    move(was)
            move(best[2])
            seg = best[1]
            loc = local(seg, ctx, slot)
            val, arcs, kept = loc[0], None, 0
            for it, (r0, r1, r2, r3) in enumerate(rng.rand(moves, 4).tolist()):
                if arcs is None:
                    arcs, two = [], []
                    for v, why in loc[1]:
                        while v in why:
                            if both[v]:
                                two.append(v)
                            u = why[v]
                            if u in why and u not in pset[v]:
                                arcs.append((u, v))
                            v = u
                    if not arcs:
                        break
                    pos = {x: j for j, x in enumerate(seg)}
                undo = None
                if r0 < 0.1 and two:
                    undo = two[int(r1 * len(two))]
                    move([(undo, 1 - eng[undo])])
                    new = seg
                else:
                    u, v = arcs[int(r1 * len(arcs))]
                    x, y = pos[u], pos[v]
                    mid = seg[x:y + 1]
                    if r2 < 0.5:
                        mov, need = {v}, set(pset[v])
                        for z in reversed(mid[:-1]):
                            if z in need:
                                mov.add(z)
                                need |= pset[z]
                        if u in mov:
                            continue
                        new = seg[:x] + [z for z in mid if z in mov] + [z for z in mid if z not in mov] + seg[y + 1:]
                    else:
                        mov = {u}
                        for z in mid[1:]:
                            if pset[z] & mov:
                                mov.add(z)
                        if v in mov:
                            continue
                        new = seg[:x] + [z for z in mid if z not in mov] + [z for z in mid if z in mov] + seg[y + 1:]
                r = local(new, ctx, slot)
                if r and (r[0] <= val or r3 < math.exp((val - r[0]) / (hot * (cold / hot) ** (it / moves)))):
                    seg, loc, val, arcs = new, r, r[0], None
                    kept += 1
                    if kept % 4 == 0:
                        s2 = sorted(seg, key=lambda i: f0[i] - d0[i])
                        z = local(s2, ctx, slot)
                        if z and z[0] <= val:
                            seg, loc, val = s2, z, z[0]
                    if val < best[0]:
                        best = (val, seg, [(i, eng[i]) for i in seg])
                elif undo is not None:
                    move([(undo, 1 - eng[undo])])
            move(best[2])
            new = perm[:a] + best[1] + perm[b:]
            r = whole(new)
            if r and r[0] <= cur[0]:
                p2 = sorted(new, key=lambda i: r[1][0][i] - d0[i])
                z = whole(p2)
                perm, cur = (p2, z) if z and z[0] <= r[0] else (new, r)
            else:
                move(start[2])
            a = clear(perm, 0, a + W // 2)
    return perm, cur


def graph(ops, lat, back=False):
    pre = [[] for _ in ops]
    for op in ops:
        for p in op["preds"]:
            lag = lat + ops[p].get("lag", 0.0)
            if back:
                pre[p].append((op["i"], lag))
            else:
                pre[op["i"]].append((p, lag))
    mate = {op["i"]: op["src"]["i"] for op in ops if "src" in op}
    mate.update({b: a for a, b in mate.items()})
    role = [(2 if back else 1) if op.get("alloc") else (1 if back else 2) if "src" in op else 0 for op in ops]
    return pre, [[5 + 3 * b for b in op["bk"]] for op in ops], role, mate, lat


def schedule(ops):
    n = len(ops)
    D, B = graph(ops, COSTS[0]["LAT"]), graph(ops, COSTS[0]["LAT"], True)
    alt = [[(EN.index(e), op["engs"][e]) for e in op.get("first", op["engs"])] for op in ops]
    rng = np.random.RandomState(PRM["SEED"])
    best = None
    key = [float(i) for i in range(n)]
    for turn in range(PRM["TRIES"] + 1):
        how = [float(rng.choice(PRM[x])) for x in HOW]
        for _ in range(2 if turn else 5):
            fin, rev = [0.0] * n, [0.0] * n
            order, used = place(range(n), [0.0] * 19, fin, alt, D, [-1.0e9 if op["grp"] == "0" else x for op, x in zip(ops, key)], how)
            if best is None or max(fin) < max(best[0]):
                best = (fin, order, used)
            place(range(n), [0.0] * 19, rev, alt, B, [-x for x in fin], how)
            key = [-x for x in rev]
        noise = float(rng.choice(PRM["NOISE"]))
        key = [best[0][i] - ops[i]["engs"][EN[best[2][i]]] + noise * x for i, x in enumerate(rng.rand(n).tolist())]
    order, eng = best[1], [best[2][i] for i in range(n)]
    views = [(ops, D, COSTS[0]["W"])]
    order, cur = improve(views, order, eng, rng, *PRM["ONE"])
    for c in COSTS[1:]:
        o = build_ops(c)
        views.append((o, graph(o, c["LAT"]), c["W"]))
    order, cur = improve(views, order, eng, rng, *PRM["ALL"])
    last = {}
    for i in order:
        op = ops[i]
        op["eng"], op["fin"], op["deps"] = EN[eng[i]], cur[1][0][i], list(op["preds"])
        if op.get("alloc"):
            op["bank"] = POOL[cur[2][i] - 17]
            op["deps"] += last.get(op["bank"], [])
        if "src" in op:
            last[op["src"]["bank"]] = [i]
        for b in op["bk"]:
            d = last.setdefault(b, {})
            op["deps"] += [q for f, q in d.items() if f != eng[i]]
            d[eng[i]] = i
    return order, max(cur[1][0])


def make_plan():
    ops = build_ops(COSTS[0])
    order, span = schedule(ops)
    know = {e: {} for e in EN}
    cnt = {"V": 0, "S": 0, "P": 0, "G": 0}
    out = []
    for i in order:
        op = ops[i]
        e = op["eng"]
        need = {}
        srcs = []
        for d in op["deps"]:
            q = ops[d]
            if "send" in q:
                need[op["ext"]] = "ARR"
                continue
            sem, v = q["tok"]
            if know[e].get(sem, 0) < v:
                srcs.append((v, sem, q))
        srcs.sort(key=lambda x: -x[2]["pos"])
        for v, sem, q in srcs:
            if know[e].get(sem, 0) >= v:
                continue
            need[sem] = max(need.get(sem, 0), v)
            know[e][sem] = v
            for s2, v2 in q["clk"].items():
                if know[e].get(s2, 0) < v2:
                    know[e][s2] = v2
        op["waits"] = need
        op["clk"] = dict(know[e])
        op["pos"] = len(out)
        if "sem" in op:
            op["tok"] = (op["sem"], 16)
        elif "send" in op:
            op["tok"] = None
        else:
            cnt[e] += 1
            op["tok"] = ("q" + e, cnt[e])
        out.append(op)
    return out, cnt, span


CACHE = {}


def rank_program(g, core, T, topo):
    rank = T.rank_of(core)
    if rank is None:
        return
    if "plan" not in CACHE:
        CACHE["plan"] = make_plan()
    plan, cnt, span = CACHE["plan"]
    N = len(T.cores)
    hand = {"V": g.vector, "S": g.scalar, "P": g.tensor, "G": g, "Y": g.sync}

    def link(src, dst):
        return topo.engines(src, dst)[:ENGINES]

    for op in plan:
        e = op["eng"]
        h = hand[e]
        for sem, v in op["waits"].items():
            if v == "ARR":
                t = int(sem[3:])
                v = len(link(T.cores[(rank - 1 - t % (N - 1)) % N], core))
            h.wait_ge(T.sem[sem], v)
        if "send" in op:
            t = op["send"]
            dst = T.cores[(rank + 1 + t % (N - 1)) % N]
            rid, pid, _s = topo.addr(dst)
            g.remote_dma(T["LAND%d" % t][:], T["SEND%d" % t][:], T.sem["arr%d" % t], T.sem["snt%d" % t], pid, rid,
                         sum(1 << x for x in link(core, dst)))
            continue
        ins = op["fn"](e, g, T, op)
        sem, v = op["tok"]
        ins.then_inc(T.sem[sem], 16 if "sem" in op else 1)
    for t in range(RO):
        g.wait_ge(T.sem["snt%d" % t], len(link(core, T.cores[(rank + 1 + t % (N - 1)) % N])))
    for e in "VSPG":
        g.wait_ge(T.sem["q" + e], cnt[e])
    for op in plan:
        if "sem" in op:
            g.sync.wait_ge(T.sem[op["sem"]], 16)
